import numpy as np, ml_dtypes
CORES = [40,64,80,88,96,104,120,144]
N = 8
import mx_ref
BF = ml_dtypes.bfloat16
def pick(q, e):
    c = np.concatenate([q[0].reshape(128, -1, 4), np.zeros((128, 1, 4), np.uint8)], axis=1); s = np.concatenate([q[1], np.ones((16, 1), np.uint8)], axis=1)
    return (np.ascontiguousarray(c[:, e].reshape(128, -1)), np.ascontiguousarray(s[:, e]))
def join(*qs):
    return (np.concatenate([q[0] for q in qs], axis=1), np.concatenate([q[1] for q in qs], axis=1))
def put(q, e, v):
    c, s = q[0].reshape(128, -1, 4).copy(), q[1].copy(); c[:, e] = v[0].reshape(128, -1, 4); s[:, e] = v[1]
    return (c.reshape(128, -1), s)
def pk(c, s):
    return (np.ascontiguousarray(c), mx_ref.live(s))
def emit(q):
    return q[0], q[1]
def decode(q):
    o = []
    for b in range(4):
        e = np.zeros((128, 128, 4), np.float32); e[np.arange(128), np.arange(128), b] = 1
        o.append(mx_ref.matmul(mx_ref.quantize(e.reshape(128, 512).astype(BF)), q))
    return np.stack(o, axis=2).reshape(128, -1)
def f(rng, *shape):
    return mx_ref.flush((rng.standard_normal(shape, dtype=np.float32) * np.exp2(rng.integers(-2, 3, shape[:-1] + (1,)))).astype(BF))
def wide(rng, *shape, cols=0):
    v = rng.standard_normal(shape, dtype=np.float32) * np.exp2(rng.integers(-12, 13, shape)).astype(np.float32)
    if cols: v *= np.repeat(np.exp2(rng.integers(-cols, cols + 1, shape[:-2] + (1, shape[-1] // 4))) * (rng.random(shape[:-2] + (1, shape[-1] // 4)) > 0.0625), 4, axis=-1).astype(np.float32)
    return mx_ref.flush(v.astype(BF))
I, B, K, M, R = 24, 256, 6, 6, 3
H = M + M // 2
def least(v):
    v = np.array(v)
    v[np.abs(v.astype(np.float32)) < np.float32(2.0 ** -12)] = 0
    return v
def plain(rng):
    return {"it": least(f(rng, N, 128, 4 * I)), "x": least(f(rng, N, 128, 4 * B)), "w": f(rng, N, 128, 512)}
def lay(m):
    return np.ascontiguousarray(m.reshape(N, 128, 4, -1).transpose(0, 1, 3, 2)).reshape(N, 128, -1).astype(np.float32).astype(BF)
def goods(at):
    m = np.zeros((N, 512, I))
    for q in range(N):
        e = at[I * q:I * q + I]
        m[q, e, np.arange(I)] = 16
        m[q, 256 + e, np.arange(I)] = 2.0 ** -7
    return m
def wishes(at, goal, size, fine):
    m = np.zeros((N, 512, B))
    for r in range(N):
        m[r, at[goal[r]], np.arange(B)] = size[r]
        m[r, 256 + at[goal[r]], np.arange(B)] = fine[r]
    return m
def hot(rng, owners):
    return np.concatenate([I * q + rng.permutation(I)[:H] for q in owners])
def setup_inputs(rng):
    return plain(rng)
def setup_inputs_again(rng):
    at, owners = rng.permutation(256), rng.permutation(N)
    goal = I * owners[rng.integers(0, 2, (N, B))] + rng.integers(0, I, (N, B))
    size = np.full((N, B), 2.0)
    s = np.tile(1 + (np.arange(H) < H // 2), 2)
    e = hot(rng, owners[:2])
    slots = np.concatenate([[0], 1 + rng.permutation(N * K - 1)[:4 * H - 1]])
    number = np.stack([np.concatenate([[0], 1 + rng.permutation(B - 1)[:K - 1]])] + [rng.permutation(B)[:K] for r in range(1, N)])[slots // K, slots % K]
    goal[slots // K, number] = np.concatenate([e, e])
    size[slots // K, number] = 16 * np.concatenate([8 * s, 7 * s])
    return {**plain(rng), "it": lay(goods(at)), "x": lay(wishes(at, goal, size, np.zeros((N, B))))}
def setup_inputs_below(rng):
    d = plain(rng)
    low = np.argsort(rng.random((N, 128, I)), axis=1) < 64
    half = np.argsort(rng.random((N, 128, B)), axis=1) < 64
    e = rng.permutation(np.concatenate([I * q + rng.permutation(I)[:K] for q in range(N)])).reshape(N, K)
    for r in range(N):
        b = rng.permutation(B)[:K]
        half[r][:, b] = low[e[r] // I, :, e[r] % I].T
    d["it"] = ((1 + 0.25 * rng.random((N, 128, 4 * I)) + np.where(np.repeat(low, 4, axis=2), 0.0, 0.75)) * 2.0 ** 29).astype(np.float32).astype(BF)
    d["x"] = (-(1 + rng.random((N, 128, 4 * B))) * 2.0 ** 29 * np.repeat(half, 4, axis=2)).astype(np.float32)
    d["x"][d["x"] == 0] = 0
    d["x"] = d["x"].astype(BF)
    return d
def setup_inputs_near(rng):
    at, o = rng.permutation(256), int(rng.integers(0, N - 1))
    pool = I * o + np.sort(rng.permutation(I)[:2 * K])
    goal, size, fine = rng.integers(0, N * I, (N, B)), np.full((N, B), 16.0), np.zeros((N, B))
    for r in range(1, N):
        b = K + rng.permutation(B - K)[:K]
        goal[r, b] = pool[K:] if r % 2 == (N - 1) % 2 else pool[:K]
        fine[r, b] = r * 2.0 ** -7
    m = wishes(at, goal, size, fine)
    q = I * ((o + 1) % N)
    i = rng.integers(0, I - 1, B)
    j = rng.integers(i + 1, I)
    n = rng.integers(1, 8, B)
    n[:K] = 1
    n[B - K:] = 8
    m[0] = 0
    m[0, at[q + i], np.arange(B)] = 16
    m[0, at[q + j], np.arange(B)] = 16
    m[0, 256 + at[q + j], np.arange(B)] = n * 2.0 ** -7
    return {**plain(rng), "it": lay(goods(at)), "x": lay(m)}
def setup_inputs_ties(rng):
    at, owners, z = rng.permutation(256), rng.permutation(N), int(rng.integers(0, N))
    goal = rng.integers(0, N * I, (N, B))
    e = np.resize(rng.permutation(hot(rng, owners[:2])), (N - 1) * K).reshape(N - 1, K)
    goal[np.arange(N) != z, :K] = rng.permuted(e, axis=1)
    m = wishes(at, goal, np.full((N, B), 16.0), np.zeros((N, B)))
    m[z] = 0
    for q in owners[2:4]:
        e = rng.integers(0, I, B)
        e[:2] = np.min(e[:K])
        m[z, at[I * q + e], np.arange(B)] = 16
    return {**plain(rng), "it": lay(goods(at)), "x": lay(m)}
def setup_inputs_spread(rng):
    return {**plain(rng), "it": least(wide(rng, N, 128, 4 * I, cols=4)), "x": least(wide(rng, N, 128, 4 * B, cols=4))}
def check_inputs(d):
    b = []
    for k, low in (("it", 2.0 ** -12), ("x", 2.0 ** -12), ("w", 2.0 ** -30)):
        v = np.abs(d[k].astype(np.float32))
        if not (np.isfinite(v).all() and ((v == 0) | (v >= low) & (v <= 2.0 ** 30)).all()): b.append("a value of " + k)
    return b
def values(xq, g, price):
    s = np.concatenate([mx_ref.matmul(pick(xq, np.arange(128 * i, 128 * i + 128)), g) for i in range(B // 128)])
    return s + np.float32(0) - price
def reference(it, x, w):
    xq = [mx_ref.quantize(np.ascontiguousarray(x[r])) for r in range(N)]
    g = join(*[mx_ref.quantize(np.ascontiguousarray(it[q])) for q in range(N)])
    price, holder, free = np.zeros(N * I, np.float32), np.full(N * I, -1), np.ones((N, B), bool)
    ho, pr = np.zeros((N, R, I), np.float32), np.zeros((N, R, I), np.float32)
    every = np.arange(B)
    for t in range(R):
        best, who = np.zeros(N * I, np.float32), np.full(N * I, -1)
        for r in range(N):
            v = values(xq[r], g, price)
            goal = np.argmax(v, axis=1)
            large = v[every, goal]
            v[every, goal] = -np.inf
            bid = large - np.max(v, axis=1)
            c = np.flatnonzero(free[r])
            for b in c[np.argsort(-bid[c], kind="stable")[:K]]:
                i = goal[b]
                if who[i] < 0 or bid[b] > best[i]: best[i], who[i] = bid[b], B * r + b
        sold = []
        for q in range(N):
            c = np.arange(I * q, I * q + I)
            c = c[who[c] >= 0]
            sold.extend(c[np.argsort(-best[c], kind="stable")[:M]].tolist())
        n = len(sold)
        buyers = join(*[pick(xq[who[i] // B], np.array([who[i] % B])) for i in sold])
        none = np.full(N * M - n, -1)
        old = decode(pick(g, np.concatenate([np.array(sold), none])))
        new = np.float32(0.5) * (old + decode(pick(buyers, np.concatenate([np.arange(n), none]))))
        g = put(g, np.array(sold), pick(mx_ref.quantize(np.ascontiguousarray(new.astype(BF))), np.arange(n)))
        for i in sold:
            if holder[i] >= 0: free[holder[i] // B, holder[i] % B] = True
            free[who[i] // B, who[i] % B] = False
            holder[i] = who[i]
            price[i] = price[i] + best[i]
        ho[:, t], pr[:, t] = holder.reshape(N, I), price.reshape(N, I)
    y = np.stack([mx_ref.matmul(mx_ref.quantize(np.ascontiguousarray(w[r])), g) for r in range(N)])
    own = [emit(pick(g, np.arange(I * q, I * q + I))) for q in range(N)]
    return {"y": y, "oc": np.stack([a for a, b in own]), "osc": np.stack([b for a, b in own]), "ho": ho, "pr": pr}

@@ -1,0 +1,591 @@
+from concourse.bass import DstId, RemoteDMATransfer
+from concourse.mybir import dt, AluOpType, AxisListType, ActivationFunctionType
+
+N, I, B, K, M, R = 8, 24, 256, 6, 6, 3
+NI = N * I
+NC = N * K
+NW = NI + R * NC
+BIG = 1.0e29
+HELD = 1.0e28
+FAR = 2.0 ** 90
+EPS = 1.0e-30
+TAG = 8192.0
+UNIT = 2.0 ** 22
+GID = 512.0
+C4, U8, F, BF, I32, U16 = "float8_e4m3fn_x4", "uint8", "float32", "bfloat16", "int32", "uint16"
+
+
+def _sb(n, d=F):
+    return ("sbuf", [128, n], d)
+
+
+SCRATCH = {
+    "itt": _sb(512, BF), "iq": _sb(128, C4), "isc": _sb(128, U8),
+    "xt": _sb(1024, BF), "xp": _sb(1024, BF), "wt": _sb(512, BF), "et": _sb(2048, BF), "ident": _sb(128, BF),
+    "xq": _sb(256, C4), "xs": _sb(256, U8), "pq": _sb(256, C4), "ps": _sb(256, U8),
+    "wq": _sb(128, C4), "ws": _sb(128, U8), "eq": _sb(512, C4), "es": _sb(512, U8),
+    "win": _sb(NW, C4), "wins": _sb(NW, U8), "oq": _sb(64, C4), "osc2": _sb(64, U8),
+    "ej": _sb(129), "jr": _sb(1024), "pi": _sb(8, I32), "pc": _sb(24), "neg": _sb(NI), "zero": _sb(32), "m4": _sb(32),
+    "tb1": _sb(128), "tb3": _sb(64), "k1": _sb(32), "kp": _sb(32), "kx": _sb(96), "m01": _sb(32), "dm": _sb(32),
+    "dx": _sb(1024), "dw": _sb(4 * (NI + 2 * NC)), "xg": _sb(32), "ct": _sb(512, BF),
+    "vw0": _sb(NI + 2 * NC), "vw1": _sb(NI + 2 * NC), "cpw": _sb(NI + NC),
+    "yw": _sb(NW), "yf": _sb(NI), "v0": _sb(NI), "v1": _sb(NI),
+    "pm0": _sb(NI + 1), "pm1": _sb(NI + 1), "m20": _sb(NI), "m21": _sb(NI),
+    "junk": _sb(NI), "fb": _sb(64), "goal": _sb(2), "gid": _sb(2),
+    "srow": _sb(NI), "prow": _sb(NI), "bb": _sb(64), "tr": _sb(64), "d1": _sb(128), "a1": _sb(128), "qr": _sb(2),
+    "w1": _sb(128), "w1t": _sb(128), "xx": _sb(72), "sb": _sb(36), "sg": _sb(36), "br": _sb(32),
+    "d2": _sb(32), "a2": _sb(64), "r2": _sb(64), "kt": _sb(96), "ktr": _sb(96), "mm": _sb(64), "bm": _sb(64), "tm": _sb(64),
+    "gi": _sb(2, I32), "g16": _sb(2, U16), "sm": _sb(8), "lk": _sb(64), "w2": _sb(128), "w2t": _sb(128), "u2": _sb(4),
+    "l2": _sb(4, U16), "idg": _sb(32), "eh": _sb(16), "cpc": _sb(10), "cpb": _sb(64), "cpt": _sb(64),
+    "best": _sb(80), "t3": _sb(64), "d3": _sb(64), "a3": _sb(68), "pos": _sb(2), "mw": _sb(32), "wt2": _sb(2),
+    "sd": _sb(4), "tag": _sb(R + 1), "price": _sb(R + 1), "mb": _sb(64), "mbt": _sb(64),
+    "x3": _sb(48 * (R + 1)), "x12": _sb(12), "lst": _sb(12 * R, U16), "hi": _sb(2, I32), "hf": _sb(R),
+    "hb": _sb(8 * R), "hc": _sb(I, C4), "hs": _sb(4 * I, U8),
+    "p_s": ("psum", [128, 1024], F), "p_d": ("psum", [128, 2048], F), "p_y": ("psum", [128, 512], F),
+}
+for _t in range(R):
+    SCRATCH["land%d" % _t] = _sb(64 + 256)
+    SCRATCH["cq%d" % _t] = _sb(128, C4)
+    SCRATCH["cs%d" % _t] = _sb(128, U8)
+    SCRATCH["hc%d" % _t] = _sb(K, C4)
+    SCRATCH["hs%d" % _t] = _sb(4 * K, U8)
+
+STAGES = ["i"] + ["%s%d" % (k, t) for t in range(R) for k in "ab"]
+SEMAPHORES = (["sv", "ss", "st", "sg", "loc"] + ["arr_" + s for s in STAGES] + ["hop_" + s for s in STAGES]
+              + ["dm%d" % k for k in range(32)])
+A = AluOpType
+ACT = ActivationFunctionType
+
+
+def V(name, c0, c1, step=1, p0=0, p1=128):
+    return (name, c0, c1, step, p0, p1)
+
+
+def _deal(engines, parts):
+    n = len(engines) // parts
+    return [sum(1 << e for e in engines[n * k:n * k + n]) for k in range(parts)]
+
+
+def _bits(m):
+    return bin(m).count("1")
+
+
+def _routes(T, topo, r, stage):
+    me = T.cores[r]
+    others = [T.cores[(r + d) % N] for d in range(1, N)]
+    near = [c for c in others if topo.may_write(me, c)]
+    far = [c for c in others if not topo.may_write(me, c)]
+    mates = sorted([c for c in topo.cores_of(me) if c != me], key=lambda c: topo.die(c) != topo.die(me))
+    port = [c for c in mates if all(topo.may_write(c, d) for d in far)]
+    on = topo.engines(me, port[0])
+    off = topo.engines(me, near[0])
+    half = len(far) // 2
+    if stage[0] == "a":
+        out = [(me, near, "b", topo.mask(me, near[0]), False, 0)]
+        hand, pool = [("b", port[0], far[:half]), ("b", port[1], far[half:])], [e for e in on if e not in off]
+    else:
+        out = [(me, near, "c", topo.mask(me, near[0]), False, 1), (me, near, "s", topo.mask(me, near[0]), False, 2)]
+        hand, pool = [("c", port[2], far[:half]), ("c", port[0], far[half:]), ("s", port[3], far[:half]), ("s", port[1], far[half:])], on
+    for (k, h, ds), m in zip(hand, _deal(pool, len(hand))):
+        out.append((me, [h], k, m, True, 0))
+        out.append((h, ds, k, topo.mask(h, ds[0]), False, 0))
+    return out
+
+
+def _places(r, stage, kind):
+    if stage == "i":
+        if kind == "c":
+            return V("iq", 0, I), V("iq", 0, I), V("hc", 0, I), V("hc", 0, I), V("win", I * r, I * r + I)
+        return V("isc", 0, I), V("isc", 0, 4 * I), V("hs", 0, 4 * I), V("hs", 0, I), V("wins", I * r, I * r + I)
+    t = int(stage[1])
+    c = NI + NC * t + K * r
+    if kind == "b":
+        n = 5 if t < R - 1 else 4
+        v = V("land%d" % t, 8 * r, 8 * r + n)
+        return v, v, V("hb", 8 * t, 8 * t + n), V("hb", 8 * t, 8 * t + n), v
+    if kind == "c":
+        return V("cq%d" % t, 0, K), V("cq%d" % t, 0, K), V("hc%d" % t, 0, K), V("hc%d" % t, 0, K), V("win", c, c + K)
+    return V("cs%d" % t, 0, K), V("cs%d" % t, 0, 4 * K), V("hs%d" % t, 0, 4 * K), V("hs%d" % t, 0, K), V("wins", c, c + K)
+
+
+def _ap(T, v):
+    if v[0] == "ind":
+        return _ap(T, v[1]).indirect(_ap(T, v[2]))
+    n, c0, c1, s, p0, p1 = v
+    return T[n][p0:p1, c0:c1] if s == 1 else T[n][p0:p1, c0:c1:s]
+
+
+def _bytes(T, v):
+    a = _ap(T, v)
+    return a.bitcast(dt.uint8) if SCRATCH[v[0]][2] == C4 else a
+
+
+def _fused(g, T, topo, r, stage, writes):
+    trs = []
+    for src, dsts, kind, m, hop, call in writes:
+        home, hand, held, leave, land = _places(r, stage, kind)
+        a, b = (hand, held) if hop else ((home if src == T.cores[r] else leave), land)
+        ids = [DstId(rid=topo.addr(d, src)[0], pnc=topo.addr(d, src)[1]) for d in dsts]
+        trs.append(RemoteDMATransfer(dst_ids=ids, dma_engine_mask=m, remote_sem=T.sem[("hop_" if hop else "arr_") + stage],
+                                     srcs=[_bytes(T, a)], dsts=[_bytes(T, b) for d in dsts]))
+    g.remote_dma_fused(trs, local_sem=T.sem.loc)
+    return sum(_bits(w[3]) for w in writes)
+
+
+def _helper(g, core, T, topo):
+    owners = [r for r in range(N) if core in topo.cores_of(T.cores[r])]
+    if not owners:
+        return
+    r, sent = owners[0], 0
+    for stage in STAGES:
+        rt = _routes(T, topo, r, stage)
+        mine = [w for w in rt if w[0] == core]
+        if mine:
+            g.wait_ge(T.sem["hop_" + stage], sum(_bits(w[3]) for w in rt if core in w[1]))
+            sent += _fused(g, T, topo, r, stage, mine)
+    if sent:
+        g.wait_ge(T.sem.loc, sent)
+
+
+def rank_program(g, core, T, topo):
+    rank = T.rank_of(core)
+    if rank is None:
+        return _helper(g, core, T, topo)
+    Q = {"v": g.vector, "s": g.scalar, "t": g.tensor, "g": g, "y": g.sync}
+    count = {"sv": 0, "ss": 0, "st": 0, "sg": 0, "loc": 0}
+    waited = {q: {} for q in Q}
+    log = {}
+    ndma = [0]
+
+    def flat(vs):
+        out = []
+        for v in vs:
+            if isinstance(v, tuple):
+                out += [v[1], v[2]] if v[0] == "ind" else [v]
+        return [((v[0], v[1] // 512 * 512, v[1] // 512 * 512 + 512, 1, 0, 128) if SCRATCH[v[0]][0] == "psum" else v) for v in out]
+
+    def meet(a, b):
+        if a[2] <= b[1] or b[2] <= a[1] or a[5] <= b[4] or b[5] <= a[4]:
+            return False
+        return not (a[3] == b[3] > 1 and (a[1] - b[1]) % a[3])
+
+    def need(q, tok):
+        if waited[q].get(tok[0], 0) < tok[1]:
+            Q[q].wait_ge(T.sem[tok[0]], tok[1])
+            waited[q][tok[0]] = tok[1]
+
+    def order(q, reads, writes):
+        want = {}
+        for vs, w in ((flat(reads), False), (flat(writes), True)):
+            for v in vs:
+                for u, uw, tok, uq in log.get(v[0], []):
+                    if (w or uw or (SCRATCH[v[0]][0] == "psum" and uq != q)) and meet(u, v):
+                        want[tok[0]] = max(want.get(tok[0], 0), tok[1])
+        for s in want:
+            need(q, (s, want[s]))
+
+    def note(q, reads, writes, tok):
+        for vs, w in ((flat(reads), False), (flat(writes), True)):
+            for v in vs:
+                log.setdefault(v[0], []).append((v, w, tok, q))
+
+    def op(q, call, out, ins, more=()):
+        order(q, ins, [out] + list(more))
+        s = "s" + q
+        count[s] += 1
+        call().then_inc(T.sem[s], 1)
+        note(q, ins, [out] + list(more), (s, count[s]))
+
+    def x(v):
+        return _ap(T, v) if isinstance(v, tuple) else v
+
+    def ts(out, a, s1, o0, s2=None, o1=None):
+        if o1 is None:
+            op("v", lambda: g.vector.tensor_scalar(x(out), x(a), x(s1), None, o0), out, [a, s1])
+        else:
+            op("v", lambda: g.vector.tensor_scalar(x(out), x(a), x(s1), x(s2), o0, o1), out, [a, s1, s2])
+
+    def tt(out, a, b, o):
+        op("v", lambda: g.vector.tensor_tensor(x(out), x(a), x(b), o), out, [a, b])
+
+    def fill(out, c):
+        op("v", lambda: g.vector.memset(x(out), c), out, [])
+
+    def scan(out, a, b, init, o0, o1):
+        op("v", lambda: g.vector.tensor_tensor_scan(x(out), x(a), x(b), x(init), o0, o1), out, [a, b, init])
+
+    def turn(out, a):
+        op("v", lambda: g.vector.transpose(x(out), x(a)), out, [a])
+
+    def quant(q, s, a):
+        op("v", lambda: g.vector.quantize_mx(x(q), x(s), x(a)), q, [a], [s])
+
+    def act(out, a, f, acc=None, **kw):
+        kx = {k: x(kw[k]) for k in kw}
+        if acc is not None:
+            kx["accum_out"] = x(acc)
+        op("s", lambda: g.scalar.activation(x(out), x(a), f, **kx), out, [a] + list(kw.values()), [acc] if acc else [])
+
+    def cp(out, a, side=0):
+        if side:
+            act(out, a, ACT.Copy)
+        else:
+            op("v", lambda: g.vector.tensor_copy(x(out), x(a)), out, [a])
+
+    def red(out, a, o, side=0):
+        if side:
+            act(a, a, ACT.Identity, out)
+        else:
+            op("v", lambda: g.vector.tensor_reduce(x(out), x(a), AxisListType.X, o), out, [a])
+
+    def diff(out, a, col, side):
+        if side:
+            act(out, a, ACT.Identity, scale=-1.0, bias=col)
+        else:
+            ts(out, a, col, A.subtract)
+
+    def mm(out, lq, ls, l0, rq, rs, r0, n):
+        a, b, c, d = V(lq, l0, l0 + 128), V(ls, l0, l0 + 128), V(rq, r0, r0 + n), V(rs, r0, r0 + n)
+        op("t", lambda: g.tensor.matmul_mx(x(out), x(a), x(b), x(c), x(d), True, True), out, [a, b, c, d])
+
+    def iota(out, pat, base, cm, small=True):
+        if small:
+            op("g", lambda: g.iota(x(out), pat, base, cm, allow_small_or_imprecise_dtypes=True), out, [])
+        else:
+            op("g", lambda: g.iota(x(out), pat, base, cm), out, [])
+
+    def dma(q, out, a):
+        ins = [a] if isinstance(a, tuple) else []
+        outs = [out] if isinstance(out, tuple) else []
+        order(q, ins, outs)
+        s = "dm%d" % ndma[0]
+        ndma[0] += 1
+        count[s] = 16
+        Q[q].dma_start(_bytes(T, out) if outs else out, _bytes(T, a) if ins else a).then_inc(T.sem[s], 16)
+        note(q, ins, outs, (s, 16))
+
+    def send(stage):
+        mine = [w for w in _routes(T, topo, rank, stage) if w[0] == core]
+        order("g", [_places(rank, stage, w[2])[1] for w in mine], [])
+        for k in sorted(set(w[5] for w in mine)):
+            count["loc"] += _fused(g, T, topo, rank, stage, [w for w in mine if w[5] == k])
+        come = [(r, w) for r in range(N) for w in _routes(T, topo, r, stage) if core in w[1]]
+        s = "arr_" + stage
+        count[s] = sum(_bits(w[3]) for r, w in come)
+        note("r", [], [_places(r, stage, w[2])[4] for r, w in come], (s, count[s]))
+        for kind in sorted(set(w[2] for w in mine) - {"b"}):
+            p = _places(rank, stage, kind)
+            dma("y", p[4], p[0])
+
+    def ind(w, o):
+        return ("ind", w, o)
+
+    def c(name, j):
+        return V(name, j, j + 1)
+
+    def h32(name, h):
+        return V(name, 32 * h, 32 * h + 32)
+
+    dma("y", V("itt", 0, 4 * I), T.it[:, :])
+    dma("s", V("xt", 0, 1024), T.x[:, :])
+    dma("y", V("wt", 0, 512), T.w[:, :])
+    fill(V("itt", 4 * I, 512), 0.0)
+    iota(c("pi", 0), [[0, 1]], 0, 1, False)
+    iota(V("ej", 0, 128), [[1, 128]], 0, 0)
+    iota(c("ej", 128), [[0, 1]], 0, 1)
+    iota(V("kx", 0, 32), [[0, 2], [1, 4], [0, 4]], 0, 0)
+    iota(V("kx", 32, 64), [[0, 2], [1, 4], [0, 4]], 4, 0)
+    iota(V("kx", 64, 96), [[0, 2], [1, 16]], 0, 0)
+    fill(V("et", 0, 2048), 0.0)
+    quant(V("iq", 0, 128), V("isc", 0, 128), V("itt", 0, 512))
+    send("i")
+
+    iota(V("jr", 0, 1024), [[1, 1024]], 0, 0)
+    for h in range(2):
+        for a in range(4):
+            cp(V("xp", 512 * h + 128 * a, 512 * h + 128 * a + 128), V("xt", 256 * a + 128 * h, 256 * a + 128 * h + 128), h)
+    ts(V("ident", 0, 128), V("ej", 0, 128), c("ej", 128), A.is_equal)
+    quant(V("xq", 0, 256), V("xs", 0, 256), V("xt", 0, 1024))
+    for b in range(4):
+        cp(V("et", 512 * b + b, 512 * b + 512, 4), V("ident", 0, 128))
+    quant(V("pq", 0, 256), V("ps", 0, 256), V("xp", 0, 1024))
+    quant(V("eq", 0, 512), V("es", 0, 512), V("et", 0, 2048))
+    for b in range(4):
+        mm(V("p_d", 512 * b, 512 * b + 256), "eq", "es", 128 * b, "xq", "xs", 0, 256)
+        act(V("dx", b, 1024, 4), V("p_d", 512 * b, 512 * b + 256), ACT.Identity, scale=0.5)
+    quant(V("wq", 0, 128), V("ws", 0, 128), V("wt", 0, 512))
+    LANE, QUAD, L16, L4, L8, ID, ID4, KEY, TMP, KF, THR = 0, 1, 2, 3, 4, 6, 8, 10, 12, 18, 20
+    ts(c("pi", 1), c("pi", 0), 31, A.bitwise_and)
+    ts(c("pi", 2), c("pi", 0), 5, A.logical_shift_right)
+    ts(c("pi", 3), c("pi", 0), 15, A.bitwise_and)
+    ts(c("pi", 4), c("pi", 0), 3, A.bitwise_and)
+    ts(c("pi", 6), c("pi", 0), 8.0, A.add)
+    fill(V("neg", 0, NI), -BIG)
+    fill(V("zero", 0, 32), 0.0)
+    ts(c("pi", 5), c("pi", 6), 15, A.bitwise_and)
+    fill(V("tb1", 32, 64), 0.0)
+    fill(V("tb1", 64, 96), EPS)
+    cp(V("pc", 0, 5), V("pi", 1, 6))
+    for nm in ("pm0", "pm1"):
+        fill(c(nm, 0), -BIG)
+    for o, e in ((V("tb1", 0, 32), -EPS), (V("tb1", 96, 128), EPS), (V("tb3", 0, 32), -EPS), (V("tb3", 32, 64), EPS)):
+        ts(o, V("ej", 0, 32), c("pc", LANE), A.is_lt, e, A.mult)
+    slot0 = K * (rank % 4) + (8 if rank < 4 else 0)
+    ts(c("pc", TMP), c("pc", QUAD), 6.0, A.mult)
+    ts(c("pc", ID), c("pc", QUAD), 64.0, A.mult, c("pc", LANE), A.add)
+    ts(c("pc", TMP + 1), c("pc", QUAD), 48.0, A.mult, c("pc", LANE), A.add)
+    ts(c("pc", TMP + 2), c("pc", LANE), 7.5, A.is_lt, -1000.0, A.mult)
+    ts(c("pc", TMP + 3), c("pc", LANE), 23.5, A.is_gt, -1000.0, A.mult)
+    ts(V("d2", 0, 32), V("ej", 0, 32), c("pc", TMP), A.subtract)
+    ts(c("pc", ID + 1), c("pc", ID), 32.0, A.add)
+    ts(c("pc", TMP + 4), c("pc", TMP + 1), -8.0, A.add, c("pc", TMP + 2), A.add)
+    ts(c("pc", TMP + 5), c("pc", TMP + 1), 24.0, A.add, c("pc", TMP + 3), A.add)
+    ts(V("a2", 0, 32), V("d2", 0, 32), 5.5, A.is_gt, -1000.0, A.mult)
+    fill(V("xx", 8, 72), 0.0)
+    ts(V("pc", KEY, KEY + 2), V("pc", TMP + 4, TMP + 6), 1.0 / 256, A.mult, float(K - 1), A.add)
+    fill(V("a2", 32, 64), 0.0)
+    tt(V("k1", 0, 32), V("d2", 0, 32), V("a2", 0, 32), A.add)
+    ts(V("pc", KF, KF + 2), V("pc", KEY, KEY + 2), -FAR, A.mult)
+    fill(V("kp", 0, 32), -1.0)
+    fill(V("ct", 32, 512), 0.0)
+    cp(V("kp", slot0, slot0 + K), V("ej", 0, K))
+    own_h, own_p = rank % 2, 32 * (rank // 2) + (0 if rank % 2 else 8)
+
+    def later():
+        ts(V("m01", 0, 32), V("kx", 64, 96), c("pc", L8), A.is_equal)
+        ts(c("pc", TMP), c("pc", QUAD), 48.0, A.mult, c("pc", L16), A.add)
+        for t in range(R):
+            fill(V("land%d" % t, 64, 320), -BIG)
+        ts(V("x3", 15, 48, 16), V("ej", 0, 48, 16), c("pc", TMP), A.add, TAG / UNIT, A.mult)
+        ts(V("dm", 0, 16), V("ej", 0, 16), c("pc", L16), A.is_equal, 4.0, A.mult)
+        ts(V("dm", 16, 32), V("ej", 0, 16), c("pc", L16), A.is_equal)
+        ts(V("pc", ID4, ID4 + 2), V("pc", ID, ID + 2), 4.0, A.mult)
+        ts(c("tag", 0), c("pc", TMP + 4 + own_h), TAG / UNIT, A.mult)
+        fill(c("price", 0), 0.0)
+        fill(V("cpw", 0, NI), 0.0)
+        fill(V("m4", 0, 32), -4.0)
+        fill(c("pc", THR), HELD / 10)
+
+    def books(t):
+        h = own_h
+        ts(c("tag", t + 1), c("wt2", h), c("sd", h), A.mult, c("tag", t), A.max)
+        ts(c("sd", 2), c("pos", h), M - 0.5, A.is_lt, c("best", 40 * h + 8), A.mult)
+        ts(c("hi", 0), c("tag", t + 1), UNIT, A.mult)
+        tt(c("price", t + 1), c("price", t), c("sd", 2), A.add)
+        ts(c("hi", 1), c("hi", 0), int(TAG) - 1, A.bitwise_and)
+        dma("s" if t == R - 1 else "y", T.pr[t, :], V("price", t + 1, t + 2, 1, own_p, own_p + I))
+        ts(c("hf", t), c("hi", 1), -1.0, A.add)
+        dma("y", T.ho[t, :], V("hf", t, t + 1, 1, own_p, own_p + I))
+
+    for t in range(R):
+        last = t == R - 1
+        wn = NI + NC * t
+        n, lo = (NI, 0) if t == 0 else (128, wn - 128)
+        new = NI if t == 0 else NC
+        lst = V("lst", 12 * (t - 1), 12 * t)
+        vv = [V("p_s", 512 * h, 512 * h + NI) if t == 0 else V("v%d" % h, 0, NI) for h in range(2)]
+        for h in range(2):
+            if t == 0:
+                mm(vv[h], "pq", "ps", 128 * h, "win", "wins", lo, n)
+            else:
+                cp(vv[h], ind(V("vw%d" % h, 0, wn), lst), h)
+        for b in range(4):
+            mm(V("p_d", 512 * b, 512 * b + n), "eq", "es", 128 * b, "win", "wins", lo, n)
+        mm(V("p_y", 0, n), "wq", "ws", 0, "win", "wins", lo, n)
+        for h in range(2):
+            scan(V("pm%d" % h, 1, NI + 1), vv[h], V("neg", 0, NI), -BIG, A.max, A.max)
+        for h in range(2):
+            scan(V("m2%d" % h, 0, NI), vv[h], V("pm%d" % h, 0, NI), -BIG, A.max, A.min)
+        m1 = [c("pm%d" % h, NI) for h in range(2)]
+        for h in range(2):
+            if t > 0:
+                act(h32("fb", h), V("m4", 0, 32), ACT.Identity, scale=m1[h], bias=c("pc", THR))
+            act(V("junk", 0, NI), V("pm%d" % h, 1, NI + 1), ACT.Sign, c("goal", h), scale=-1.0, bias=m1[h])
+        for h in range(2):
+            act(c("gid", h), c("goal", h), ACT.Identity, scale=GID, bias=c("pc", ID + h))
+
+        def unpack(bs):
+            for b in bs:
+                act(V("dw", 4 * (wn - new) + b, 4 * wn, 4), V("p_d", 512 * b + n - new, 512 * b + n), ACT.Identity, scale=0.5)
+
+        for h in range(2):
+            if t > 0:
+                ts(h32("bb", h), h32("fb", h), m1[h], A.min, c("m2%d" % h, NI - 1), A.subtract)
+            else:
+                ts(h32("bb", h), V("zero", 0, 32), m1[h], A.add, c("m2%d" % h, NI - 1), A.subtract)
+        turn(V("tr", 0, 64), V("bb", 0, 64))
+        for h in range(2):
+            diff(V("d1", 64 * h, 64 * h + 64), V("tr", 0, 64), c("bb", 32 * h), h)
+        for h in range(2):
+            tt(V("a1", 64 * h, 64 * h + 64), V("d1", 64 * h, 64 * h + 64), V("tb1", 64 * h, 64 * h + 64), A.is_lt if h else A.is_gt)
+        for h in range(2):
+            red(c("qr", h), V("a1", 64 * h, 64 * h + 64), A.add, 1 - h)
+        if t > 0:
+            act(V("srow", 0, NI), ind(V("jr", 0, wn), lst), ACT.Copy)
+        else:
+            unpack([0])
+        for h in range(2):
+            ts(h32("w1", h), V("k1", 0, 32), c("qr", h), A.is_equal, c("bb", 32 * h), A.mult)
+        for h in range(2):
+            ts(h32("w1", 2 + h), V("k1", 0, 32), c("qr", h), A.is_equal, c("gid", h), A.mult)
+        for j in range(2):
+            turn(V("w1t", 64 * j, 64 * j + 64), V("w1", 64 * j, 64 * j + 64))
+        for j in range(2):
+            red(c("xx", j), V("w1t", 64 * j, 64 * j + 64), A.add, 1 - j)
+        for d in range(2):
+            cp(V("xx", 2, 4, 1, 64 * d, 64 * d + 64), V("xx", 0, 2, 1, 64 - 64 * d, 128 - 64 * d), d)
+        for d in range(4):
+            cp(V("xx", 4, 8, 1, 32 * d, 32 * d + 32), V("xx", 0, 4, 1, 32 * (d ^ 1), 32 * (d ^ 1) + 32), d % 2)
+        if t == 0:
+            unpack([1])
+        elif not last:
+            act(V("prow", 0, NI), ind(V("cpw", 0, wn), lst), ACT.Copy)
+        scan(V("sb", 0, 36), V("xx", 0, 72, 2), V("neg", 0, 36), 0.0, A.add, A.max)
+        scan(V("sg", 0, 36), V("xx", 1, 72, 2), V("neg", 0, 36), 0.0, A.add, A.max)
+        turn(V("br", 0, 32), V("sb", 4, 36))
+        if t > 0:
+            ts(c("g16", 0), c("sg", 4), 1.0 / GID, A.mult)
+        tt(V("d2", 0, 32), V("br", 0, 32), V("sb", 4, 36), A.subtract)
+        ts(c("gi", 0), c("sg", 4), 1.0 / GID, A.mult)
+        tt(V("a2", 0, 32), V("d2", 0, 32), V("tb3", 0, 32), A.is_gt)
+        ts(c("sm", 1), c("gi", 0), -GID, A.mult, c("sg", 4), A.add)
+        scan(V("r2", 0, 64), V("a2", 0, 64), V("neg", 0, 64), 0.0, A.add, A.max)
+        ts(c("sm", 0), c("gi", 0), 1.0 / 256, A.mult)
+        act(c("sm", 2), c("sm", 1), ACT.Copy, scale=1.0 / UNIT, bias=(float(wn + K * rank) * TAG + B * rank + 1) / UNIT)
+        if 0 < t < R - 1:
+            tt(V("lk", 16, 32), ind(V("prow", 0, NI), c("g16", 0)), V("dm", 16, 32), A.mult)
+        r2 = V("r2", 32, 64)
+        ts(V("kt", 0, 32), r2, float(K - 1), A.max, c("sm", 0), A.add)
+        act(V("kt", 32, 64), r2, ACT.Identity, scale=TAG / UNIT, bias=c("sm", 2))
+        if 0 < t < R - 1:
+            red(c("sm", 5), V("lk", 16, 32), A.add)
+        turn(V("ktr", 0, 32), V("kt", 0, 32))
+        turn(V("ktr", 32, 64), V("kt", 32, 64))
+        ld = "land%d" % t
+        if t == 0:
+            ts(V("kt", 64, 96), V("kp", 0, 32), c("r2", 32), A.is_equal, c("sb", 4), A.mult)
+        elif not last:
+            act(c("sm", 6), c("sm", 5), ACT.Identity, bias=c("sb", 4))
+        ts(h32("mm", 0), V("ktr", 0, 32), c("pc", KEY), A.not_equal, BIG / 10, A.mult)
+        act(h32("mm", 1), V("ktr", 0, 32), ACT.Abs, scale=FAR, bias=c("pc", KF + 1))
+        if 0 < t < R - 1:
+            ts(V("kt", 64, 96), V("kp", 0, 32), c("r2", 32), A.is_equal, c("sm", 6), A.mult)
+        for h in range(2):
+            tt(h32("bm", h), V("br", 0, 32), h32("mm", h), A.subtract)
+            if h == 0 and not last:
+                turn(V("ktr", 64, 96), V("kt", 64, 96))
+                red(c(ld, 8 * rank + 4), V("ktr", 64, 96), A.add, 1)
+            tt(h32("tm", h), V("ktr", 32, 64), h32("mm", h), A.add)
+        act(c("sm", 3), c("sm", 1), ACT.Identity, scale=4.0)
+        unpack([2, 3] if t == 0 else [0, 1, 2, 3])
+        for h in range(2):
+            red(c(ld, 8 * rank + h), h32("bm", h), A.max)
+            red(c(ld, 8 * rank + 2 + h), h32("tm", h), A.min)
+        send("a%d" % t)
+        if t > 0:
+            tt(V("lk", 0, 16), ind(V("srow", 0, NI), c("g16", 0)), V("dm", 0, 16), A.mult)
+        else:
+            ts(c("sm", 4), c("gi", 0), 4.0, A.mult)
+
+        def block(j):
+            ts(h32("w2", j), h32("kx", j % 2), c("r2", 32), A.is_equal, c("sm", 3 + j // 2), A.mult)
+
+        block(0)
+        if t > 0:
+            red(c("sm", 4), V("lk", 0, 16), A.add)
+        block(1)
+        block(2)
+        block(3)
+        turn(V("w2t", 0, 64), V("w2", 0, 64))
+        turn(V("w2t", 64, 128), V("w2", 64, 128))
+        for j in (0, 2, 1, 3):
+            red(c("u2", j), h32("w2t", j), A.add, j in (1, 3))
+        ts(V("l2", 0, 2), V("u2", 0, 2), c("pc", L4), A.add)
+        ts(V("l2", 2, 4), V("u2", 2, 4), c("pc", L4), A.add)
+        cp(V("xg", 0, 32), ind(V("dx", 0, 1024), V("l2", 0, 2)))
+        tt(V("ct", 0, 32), ind(V("dw", 0, 4 * wn), V("l2", 2, 4)), V("xg", 0, 32), A.add)
+        quant(V("cq%d" % t, 0, 128), V("cs%d" % t, 0, 128), V("ct", 0, 512))
+        send("b%d" % t)
+        act(V("yw", wn - new, wn), V("p_y", n - new, n), ACT.Copy)
+        if t == 0:
+            for h in range(2):
+                cp(V("vw%d" % h, 0, NI), vv[h], 1)
+            later()
+        else:
+            books(t - 1)
+        if not last:
+            act(V("idg", 0, 32), ind(V("jr", 0, 1024), V("l2", 0, 2)), ACT.Copy)
+            for h in range(2):
+                ts(V("eh", 8 * h, 8 * h + K), V("idg", 0, 4 * K, 4), c("pc", ID4 + h), A.is_equal, HELD, A.mult)
+        w2 = wn + NC
+        if not last:
+            for h in range(2):
+                mm(V("p_s", 512 * h, 512 * h + 128), "pq", "ps", 128 * h, "win", "wins", w2 - 128, 128)
+        else:
+            mm(V("p_y", 0, 128), "wq", "ws", 0, "win", "wins", w2 - 128, 128)
+        for h in range(2):
+            scan(V("best", 40 * h, 40 * h + 40), V(ld, h, 320, 8), V("neg", 0, 40), -BIG, A.max, A.max)
+        bs = [c("best", 40 * h + 8) for h in range(2)]
+        for h in range(2):
+            turn(h32("t3", h), V("best", 40 * h + 8, 40 * h + 40))
+        for h in range(2):
+            act(V("mw", 8 * h, 8 * h + 8), V(ld, h, 64, 8), ACT.Sign, scale=-1.0, bias=bs[h])
+        for h in range(2):
+            diff(h32("d3", h), h32("t3", h), bs[h], h)
+        act(V("a3", 32, 68, 34), V("best", 8, 80, 40), ACT.Relu, scale=-1.0)
+        tt(V("mw", 16, 24), V("mw", 0, 8), V(ld, 2, 64, 8), A.max)
+        tt(V("a3", 0, 32), h32("d3", 0), h32("tb3", 0), A.is_gt)
+        tt(V("a3", 34, 66), h32("d3", 1), h32("tb3", 1), A.is_lt)
+        tt(V("mw", 24, 32), V("mw", 8, 16), V(ld, 3, 64, 8), A.max)
+        for h in range(2):
+            red(c("pos", h), V("a3", 34 * h, 34 * h + 33), A.add, 1 - h)
+        for h in range(2):
+            red(c("wt2", h), V("mw", 16 + 8 * h, 24 + 8 * h), A.min)
+        act(V("sd", 0, 2), V("pos", 0, 2), ACT.Sign, scale=-1.0, bias=M - 0.5)
+        if not last:
+            for h in range(2):
+                act(V("cpc", 2 + 4 * h, 6 + 4 * h), V(ld, 32 * h + 4, 32 * h + 36, 8), ACT.Identity, c("cpc", h))
+            for h in range(2):
+                act(h32("cpb", h), V("zero", 0, 32), ACT.Identity, bias=c("cpc", h))
+        for h in range(2):
+            ts(h32("mb", h), V("m01", 0, 32), c("wt2", h), A.mult, c("sd", h), A.mult)
+        turn(V("mbt", 0, 64), V("mb", 0, 64))
+        x0 = 48 * (t + 1)
+        for j in range(3):
+            scan(V("x3", x0 + 16 * j, x0 + 16 * j + 16), V("mbt", 8 + 16 * j, 24 + 16 * j), V("neg", 0, 16),
+                 c("x3", x0 - 33 + 16 * j), A.max, A.max)
+        if not last:
+            turn(V("cpt", 0, 64), V("cpb", 0, 64))
+        for a in range(4):
+            cp(V("x12", 3 * a, 3 * a + 3, 1, 0, 32), V("x3", x0 + 15, x0 + 48, 16, 32 * a, 32 * a + 32), a % 2)
+        for d in range(4):
+            ts(V("lst", 12 * t, 12 * t + 12, 1, 32 * d, 32 * d + 32), V("x12", 0, 12, 1, 0, 32), UNIT / TAG, A.mult)
+        if t == 0:
+            cp(V("cpw", wn, w2), V("cpt", 8, 8 + NC), 1)
+        if not last:
+            for h in (1, 0):
+                tt(V("vw%d" % h, wn, w2), V("p_s", 512 * h + 128 - NC, 512 * h + 128), V("cpt", 8, 8 + NC), A.subtract)
+            for h in (1, 0):
+                own = V("vw%d" % h, wn + K * rank, wn + K * rank + K)
+                tt(own, own, V("eh", 8 * h, 8 * h + K), A.add)
+        else:
+            act(V("yw", wn, w2), V("p_y", 128 - NC, 128), ACT.Copy)
+
+    l0 = 12 * (R - 1)
+    c0 = I * rank // 32 * 2
+    c1 = -(-(I * rank + I) // 16)
+    at, n = I * rank - 16 * c0, 16 * (c1 - c0)
+    sub = V("lst", l0 + c0, l0 + c1)
+    op("v", lambda: g.vector.tensor_copy(T.oq[:, 0:n].bitcast(dt.uint32), T.win[:, 0:NW].bitcast(dt.uint32).indirect(x(sub))),
+       V("oq", 0, n), [V("win", 0, NW), sub])
+    for h in range(2):
+        cp(V("yf", 96 * h, 96 * h + 96), ind(V("yw", 0, NW), V("lst", l0 + 6 * h, l0 + 6 * h + 6)), h)
+    dma("y", T.oc[:, :], V("oq", at, at + I))
+    dma("y", T.y[:, :], V("yf", 0, NI))
+    act(V("osc2", 0, n), ind(V("wins", 0, NW), sub), ACT.Copy)
+    for k in range(4):
+        dma("s", T.osc[4 * k:4 * k + 4, :], V("osc2", at, at + I, 1, 32 * k, 32 * k + 4))
+    books(R - 1)
+    for s in count:
+        if max(waited[q].get(s, 0) for q in Q) < count[s]:
+            need("g", (s, count[s]))

@@ -7,11 +7,13 @@ NC = N * K
 NW = NI + R * NC
 BIG = 1.0e29
 HELD = 1.0e28
-FAR = 2.0 ** 90
+FAR = 2.0 ** 84
 EPS = 1.0e-30
+NIL = 2.0 ** -100
 TAG = 8192.0
 UNIT = 2.0 ** 22
 GID = 512.0
+WHOLE = 2.0 ** 23
 C4, U8, F, BF, I32, U16 = "float8_e4m3fn_x4", "uint8", "float32", "bfloat16", "int32", "uint16"
 
 
@@ -32,13 +34,13 @@ SCRATCH = {
     "yw": _sb(NW), "yf": _sb(NI), "v0": _sb(NI), "v1": _sb(NI),
     "pm0": _sb(NI + 1), "pm1": _sb(NI + 1), "m20": _sb(NI), "m21": _sb(NI),
     "junk": _sb(NI), "fb": _sb(64), "goal": _sb(2), "gid": _sb(2),
-    "srow": _sb(NI), "prow": _sb(NI), "bb": _sb(64), "tr": _sb(64), "d1": _sb(128), "a1": _sb(128), "qr": _sb(2),
-    "w1": _sb(128), "w1t": _sb(128), "xx": _sb(72), "sb": _sb(36), "sg": _sb(36), "br": _sb(32),
-    "d2": _sb(32), "a2": _sb(64), "r2": _sb(64), "kt": _sb(96), "ktr": _sb(96), "mm": _sb(64), "bm": _sb(64), "tm": _sb(64),
-    "gi": _sb(2, I32), "g16": _sb(2, U16), "sm": _sb(8), "lk": _sb(64), "w2": _sb(128), "w2t": _sb(128), "u2": _sb(4),
-    "l2": _sb(4, U16), "idg": _sb(32), "eh": _sb(16), "cpc": _sb(10), "cpb": _sb(64), "cpt": _sb(64),
+    "srow": _sb(2 * NI), "bb": _sb(64), "tr": _sb(64), "d1": _sb(128), "a1": _sb(128), "qr": _sb(2),
+    "w1": _sb(128), "w1t": _sb(128), "xx": _sb(72), "sb": _sb(36), "sg": _sb(36), "br": _sb(32), "gf": _sb(32),
+    "d2": _sb(64), "a2": _sb(64), "r2": _sb(64), "kt": _sb(96), "ktr": _sb(96), "mm": _sb(64), "bm": _sb(64), "tm": _sb(64),
+    "gi": _sb(1, I32), "g16": _sb(2, U16), "sm": _sb(8), "lk": _sb(32), "w2": _sb(128), "w2t": _sb(128), "u2": _sb(4),
+    "l2": _sb(4, U16), "idg": _sb(32), "eh": _sb(2 * NC), "cpx": _sb(2 * NC), "cpc": _sb(10), "cpb": _sb(64), "cpt": _sb(64),
     "best": _sb(80), "t3": _sb(64), "d3": _sb(64), "a3": _sb(68), "pos": _sb(2), "mw": _sb(32), "wt2": _sb(2),
-    "sd": _sb(4), "tag": _sb(R + 1), "price": _sb(R + 1), "mb": _sb(64), "mbt": _sb(64),
+    "sd": _sb(3), "tag": _sb(R + 1), "price": _sb(R + 1), "mb": _sb(64), "mbt": _sb(64),
     "x3": _sb(48 * (R + 1)), "x12": _sb(12), "lst": _sb(12 * R, U16), "hi": _sb(2, I32), "hf": _sb(R),
     "hb": _sb(8 * R), "hc": _sb(I, C4), "hs": _sb(4 * I, U8),
     "p_s": ("psum", [128, 1024], F), "p_d": ("psum", [128, 2048], F), "p_y": ("psum", [128, 512], F),
@@ -52,7 +54,7 @@ for _t in range(R):
 
 STAGES = ["i"] + ["%s%d" % (k, t) for t in range(R) for k in "ab"]
 SEMAPHORES = (["sv", "ss", "st", "sg", "loc"] + ["arr_" + s for s in STAGES] + ["hop_" + s for s in STAGES]
-              + ["dm%d" % k for k in range(32)])
+              + ["dm%d" % k for k in range(16)])
 A = AluOpType
 ACT = ActivationFunctionType
 
@@ -78,17 +80,20 @@ def _routes(T, topo, r, stage):
     mates = sorted([c for c in topo.cores_of(me) if c != me], key=lambda c: topo.die(c) != topo.die(me))
     port = [c for c in mates if all(topo.may_write(c, d) for d in far)]
     on = topo.engines(me, port[0])
-    off = topo.engines(me, near[0])
+    off = topo.mask(me, near[0])
+    only = [e for e in on if e not in topo.engines(me, near[0])]
     half = len(far) // 2
     if stage[0] == "a":
-        out = [(me, near, "b", topo.mask(me, near[0]), False, 0)]
-        hand, pool = [("b", port[0], far[:half]), ("b", port[1], far[half:])], [e for e in on if e not in off]
+        out = []
+        hand = [("b", port[0], far[:half]), ("b", port[1], far[half:]), ("b", port[2], near[:half]), ("b", port[3], near[half:])]
     else:
-        out = [(me, near, "c", topo.mask(me, near[0]), False, 1), (me, near, "s", topo.mask(me, near[0]), False, 2)]
-        hand, pool = [("c", port[2], far[:half]), ("c", port[0], far[half:]), ("s", port[3], far[:half]), ("s", port[1], far[half:])], on
-    for (k, h, ds), m in zip(hand, _deal(pool, len(hand))):
+        out = [(me, near, "c", off, False, 1), (me, near, "s", off, False, 2)]
+        hand = [("c", port[2], far[:half]), ("c", port[0], far[half:]), ("s", port[3], far[:half]), ("s", port[1], far[half:])]
+    for (k, h, ds), m in zip(hand, _deal(on, len(hand))):
         out.append((me, [h], k, m, True, 0))
         out.append((h, ds, k, topo.mask(h, ds[0]), False, 0))
+        if h in port[2:] and k != "b":
+            out.append((h, [me], k, _deal(only, 2)[0], False, int(stage == "i")))
     return out
 
 
@@ -120,15 +125,16 @@ def _bytes(T, v):
     return a.bitcast(dt.uint8) if SCRATCH[v[0]][2] == C4 else a
 
 
-def _fused(g, T, topo, r, stage, writes):
-    trs = []
-    for src, dsts, kind, m, hop, call in writes:
-        home, hand, held, leave, land = _places(r, stage, kind)
-        a, b = (hand, held) if hop else ((home if src == T.cores[r] else leave), land)
-        ids = [DstId(rid=topo.addr(d, src)[0], pnc=topo.addr(d, src)[1]) for d in dsts]
-        trs.append(RemoteDMATransfer(dst_ids=ids, dma_engine_mask=m, remote_sem=T.sem[("hop_" if hop else "arr_") + stage],
-                                     srcs=[_bytes(T, a)], dsts=[_bytes(T, b) for d in dsts]))
-    g.remote_dma_fused(trs, local_sem=T.sem.loc)
+def _calls(g, T, topo, r, stage, writes):
+    for k in sorted(set(w[5] for w in writes)):
+        trs = []
+        for src, dsts, kind, m, hop, call in [w for w in writes if w[5] == k]:
+            home, hand, held, leave, land = _places(r, stage, kind)
+            a, b = (hand, held) if hop else ((home if src == T.cores[r] else leave), land)
+            ids = [DstId(rid=topo.addr(d, src)[0], pnc=topo.addr(d, src)[1]) for d in dsts]
+            trs.append(RemoteDMATransfer(dst_ids=ids, dma_engine_mask=m, remote_sem=T.sem[("hop_" if hop else "arr_") + stage],
+                                         srcs=[_bytes(T, a)], dsts=[_bytes(T, b) for d in dsts]))
+        g.remote_dma_fused(trs, local_sem=T.sem.loc)
     return sum(_bits(w[3]) for w in writes)
 
 
@@ -142,7 +148,7 @@ def _helper(g, core, T, topo):
         mine = [w for w in rt if w[0] == core]
         if mine:
             g.wait_ge(T.sem["hop_" + stage], sum(_bits(w[3]) for w in rt if core in w[1]))
-            sent += _fused(g, T, topo, r, stage, mine)
+            sent += _calls(g, T, topo, r, stage, mine)
     if sent:
         g.wait_ge(T.sem.loc, sent)
 
@@ -238,12 +244,6 @@ def rank_program(g, core, T, topo):
         else:
             op("v", lambda: g.vector.tensor_reduce(x(out), x(a), AxisListType.X, o), out, [a])
 
-    def diff(out, a, col, side):
-        if side:
-            act(out, a, ACT.Identity, scale=-1.0, bias=col)
-        else:
-            ts(out, a, col, A.subtract)
-
     def mm(out, lq, ls, l0, rq, rs, r0, n):
         a, b, c, d = V(lq, l0, l0 + 128), V(ls, l0, l0 + 128), V(rq, r0, r0 + n), V(rs, r0, r0 + n)
         op("t", lambda: g.tensor.matmul_mx(x(out), x(a), x(b), x(c), x(d), True, True), out, [a, b, c, d])
@@ -267,15 +267,11 @@ def rank_program(g, core, T, topo):
     def send(stage):
         mine = [w for w in _routes(T, topo, rank, stage) if w[0] == core]
         order("g", [_places(rank, stage, w[2])[1] for w in mine], [])
-        for k in sorted(set(w[5] for w in mine)):
-            count["loc"] += _fused(g, T, topo, rank, stage, [w for w in mine if w[5] == k])
+        count["loc"] += _calls(g, T, topo, rank, stage, mine)
         come = [(r, w) for r in range(N) for w in _routes(T, topo, r, stage) if core in w[1]]
         s = "arr_" + stage
         count[s] = sum(_bits(w[3]) for r, w in come)
         note("r", [], [_places(r, stage, w[2])[4] for r, w in come], (s, count[s]))
-        for kind in sorted(set(w[2] for w in mine) - {"b"}):
-            p = _places(rank, stage, kind)
-            dma("y", p[4], p[0])
 
     def ind(w, o):
         return ("ind", w, o)
@@ -287,8 +283,7 @@ def rank_program(g, core, T, topo):
         return V(name, 32 * h, 32 * h + 32)
 
     dma("y", V("itt", 0, 4 * I), T.it[:, :])
-    dma("s", V("xt", 0, 1024), T.x[:, :])
-    dma("y", V("wt", 0, 512), T.w[:, :])
+    dma("y", V("xt", 0, 1024), T.x[:, :])
     fill(V("itt", 4 * I, 512), 0.0)
     iota(c("pi", 0), [[0, 1]], 0, 1, False)
     iota(V("ej", 0, 128), [[1, 128]], 0, 0)
@@ -301,20 +296,21 @@ def rank_program(g, core, T, topo):
     send("i")
 
     iota(V("jr", 0, 1024), [[1, 1024]], 0, 0)
+    ts(V("ident", 0, 128), V("ej", 0, 128), c("ej", 128), A.is_equal)
+    for b in range(4):
+        cp(V("et", 512 * b + b, 512 * b + 512, 4), V("ident", 0, 128))
+    quant(V("eq", 0, 512), V("es", 0, 512), V("et", 0, 2048))
     for h in range(2):
         for a in range(4):
             cp(V("xp", 512 * h + 128 * a, 512 * h + 128 * a + 128), V("xt", 256 * a + 128 * h, 256 * a + 128 * h + 128), h)
-    ts(V("ident", 0, 128), V("ej", 0, 128), c("ej", 128), A.is_equal)
     quant(V("xq", 0, 256), V("xs", 0, 256), V("xt", 0, 1024))
-    for b in range(4):
-        cp(V("et", 512 * b + b, 512 * b + 512, 4), V("ident", 0, 128))
     quant(V("pq", 0, 256), V("ps", 0, 256), V("xp", 0, 1024))
-    quant(V("eq", 0, 512), V("es", 0, 512), V("et", 0, 2048))
     for b in range(4):
         mm(V("p_d", 512 * b, 512 * b + 256), "eq", "es", 128 * b, "xq", "xs", 0, 256)
         act(V("dx", b, 1024, 4), V("p_d", 512 * b, 512 * b + 256), ACT.Identity, scale=0.5)
-    quant(V("wq", 0, 128), V("ws", 0, 128), V("wt", 0, 512))
-    LANE, QUAD, L16, L4, L8, ID, ID4, KEY, TMP, KF, THR = 0, 1, 2, 3, 4, 6, 8, 10, 12, 18, 20
+    need("y", ("arr_i", count["arr_i"]))
+    dma("y", V("wt", 0, 512), T.w[:, :])
+    LANE, QUAD, L16, L4, L8, ID, ID4, KEY, TMP, KF, THR, TWO = 0, 1, 2, 3, 4, 6, 8, 10, 12, 18, 20, 22
     ts(c("pi", 1), c("pi", 0), 31, A.bitwise_and)
     ts(c("pi", 2), c("pi", 0), 5, A.logical_shift_right)
     ts(c("pi", 3), c("pi", 0), 15, A.bitwise_and)
@@ -328,7 +324,7 @@ def rank_program(g, core, T, topo):
     cp(V("pc", 0, 5), V("pi", 1, 6))
     for nm in ("pm0", "pm1"):
         fill(c(nm, 0), -BIG)
-    for o, e in ((V("tb1", 0, 32), -EPS), (V("tb1", 96, 128), EPS), (V("tb3", 0, 32), -EPS), (V("tb3", 32, 64), EPS)):
+    for o, e in ((V("tb1", 0, 32), -EPS), (V("tb1", 96, 128), EPS), (V("tb3", 32, 64), -0.5 / WHOLE)):
         ts(o, V("ej", 0, 32), c("pc", LANE), A.is_lt, e, A.mult)
     slot0 = K * (rank % 4) + (8 if rank < 4 else 0)
     ts(c("pc", TMP), c("pc", QUAD), 6.0, A.mult)
@@ -342,10 +338,11 @@ def rank_program(g, core, T, topo):
     ts(c("pc", TMP + 5), c("pc", TMP + 1), 24.0, A.add, c("pc", TMP + 3), A.add)
     ts(V("a2", 0, 32), V("d2", 0, 32), 5.5, A.is_gt, -1000.0, A.mult)
     fill(V("xx", 8, 72), 0.0)
-    ts(V("pc", KEY, KEY + 2), V("pc", TMP + 4, TMP + 6), 1.0 / 256, A.mult, float(K - 1), A.add)
+    ts(V("pc", KEY, KEY + 2), V("pc", TMP + 4, TMP + 6), WHOLE, A.add)
     fill(V("a2", 32, 64), 0.0)
     tt(V("k1", 0, 32), V("d2", 0, 32), V("a2", 0, 32), A.add)
     ts(V("pc", KF, KF + 2), V("pc", KEY, KEY + 2), -FAR, A.mult)
+    ts(V("tb3", 0, 32), V("tb3", 32, 64), 1.0, A.add)
     fill(V("kp", 0, 32), -1.0)
     fill(V("ct", 32, 512), 0.0)
     cp(V("kp", slot0, slot0 + K), V("ej", 0, K))
@@ -360,25 +357,32 @@ def rank_program(g, core, T, topo):
         ts(V("dm", 0, 16), V("ej", 0, 16), c("pc", L16), A.is_equal, 4.0, A.mult)
         ts(V("dm", 16, 32), V("ej", 0, 16), c("pc", L16), A.is_equal)
         ts(V("pc", ID4, ID4 + 2), V("pc", ID, ID + 2), 4.0, A.mult)
+        ts(V("pc", TWO, TWO + 2), V("ej", 0, 2), NI * GID, A.mult)
         ts(c("tag", 0), c("pc", TMP + 4 + own_h), TAG / UNIT, A.mult)
         fill(c("price", 0), 0.0)
         fill(V("cpw", 0, NI), 0.0)
         fill(V("m4", 0, 32), -4.0)
+        fill(V("eh", 0, 2 * NC), 0.0)
         fill(c("pc", THR), HELD / 10)
 
-    def books(t):
+    def books(t, part):
         h = own_h
-        ts(c("tag", t + 1), c("wt2", h), c("sd", h), A.mult, c("tag", t), A.max)
-        ts(c("sd", 2), c("pos", h), M - 0.5, A.is_lt, c("best", 40 * h + 8), A.mult)
-        ts(c("hi", 0), c("tag", t + 1), UNIT, A.mult)
-        tt(c("price", t + 1), c("price", t), c("sd", 2), A.add)
-        ts(c("hi", 1), c("hi", 0), int(TAG) - 1, A.bitwise_and)
-        dma("s" if t == R - 1 else "y", T.pr[t, :], V("price", t + 1, t + 2, 1, own_p, own_p + I))
-        ts(c("hf", t), c("hi", 1), -1.0, A.add)
-        dma("y", T.ho[t, :], V("hf", t, t + 1, 1, own_p, own_p + I))
+        if part == 0:
+            ts(c("tag", t + 1), c("wt2", h), c("sd", h), A.mult, c("tag", t), A.max)
+            ts(c("sd", 2), c("best", 40 * h + 8), 2 * NIL, A.is_gt, c("sd", h), A.mult)
+        elif part == 1:
+            ts(c("hi", 0), c("tag", t + 1), UNIT, A.mult)
+            ts(c("price", t + 1), c("best", 40 * h + 8), c("sd", 2), A.mult, c("price", t), A.add)
+            dma("y", T.pr[t, :], V("price", t + 1, t + 2, 1, own_p, own_p + I))
+        elif part == 2:
+            ts(c("hi", 1), c("hi", 0), int(TAG) - 1, A.bitwise_and)
+        else:
+            ts(c("hf", t), c("hi", 1), -1.0, A.add)
+            dma("y", T.ho[t, :], V("hf", t, t + 1, 1, own_p, own_p + I))
 
     for t in range(R):
         last = t == R - 1
+        mid = 0 < t < R - 1
         wn = NI + NC * t
         n, lo = (NI, 0) if t == 0 else (128, wn - 128)
         new = NI if t == 0 else NC
@@ -389,9 +393,10 @@ def rank_program(g, core, T, topo):
                 mm(vv[h], "pq", "ps", 128 * h, "win", "wins", lo, n)
             else:
                 cp(vv[h], ind(V("vw%d" % h, 0, wn), lst), h)
+        if mid:
+            act(V("srow", NI, 2 * NI), ind(V("cpw", 0, wn), lst), ACT.Copy)
         for b in range(4):
             mm(V("p_d", 512 * b, 512 * b + n), "eq", "es", 128 * b, "win", "wins", lo, n)
-        mm(V("p_y", 0, n), "wq", "ws", 0, "win", "wins", lo, n)
         for h in range(2):
             scan(V("pm%d" % h, 1, NI + 1), vv[h], V("neg", 0, NI), -BIG, A.max, A.max)
         for h in range(2):
@@ -414,8 +419,8 @@ def rank_program(g, core, T, topo):
             else:
                 ts(h32("bb", h), V("zero", 0, 32), m1[h], A.add, c("m2%d" % h, NI - 1), A.subtract)
         turn(V("tr", 0, 64), V("bb", 0, 64))
-        for h in range(2):
-            diff(V("d1", 64 * h, 64 * h + 64), V("tr", 0, 64), c("bb", 32 * h), h)
+        ts(V("d1", 0, 64), V("tr", 0, 64), c("bb", 0), A.subtract)
+        act(V("d1", 64, 128), V("tr", 0, 64), ACT.Identity, scale=-1.0, bias=c("bb", 32))
         for h in range(2):
             tt(V("a1", 64 * h, 64 * h + 64), V("d1", 64 * h, 64 * h + 64), V("tb1", 64 * h, 64 * h + 64), A.is_lt if h else A.is_gt)
         for h in range(2):
@@ -436,87 +441,88 @@ def rank_program(g, core, T, topo):
             cp(V("xx", 2, 4, 1, 64 * d, 64 * d + 64), V("xx", 0, 2, 1, 64 - 64 * d, 128 - 64 * d), d)
         for d in range(4):
             cp(V("xx", 4, 8, 1, 32 * d, 32 * d + 32), V("xx", 0, 4, 1, 32 * (d ^ 1), 32 * (d ^ 1) + 32), d % 2)
-        if t == 0:
-            unpack([1])
-        elif not last:
-            act(V("prow", 0, NI), ind(V("cpw", 0, wn), lst), ACT.Copy)
-        scan(V("sb", 0, 36), V("xx", 0, 72, 2), V("neg", 0, 36), 0.0, A.add, A.max)
+        scan(V("sb", 0, 36), V("xx", 0, 72, 2), V("neg", 0, 36), NIL, A.add, A.max)
         scan(V("sg", 0, 36), V("xx", 1, 72, 2), V("neg", 0, 36), 0.0, A.add, A.max)
         turn(V("br", 0, 32), V("sb", 4, 36))
+        act(V("d2", 0, 32), V("tb3", 0, 32), ACT.Identity, scale=c("sb", 4))
+        act(V("gf", 0, 32), V("sg", 4, 36), ACT.Copy, scale=1.0 / GID, bias=WHOLE)
+        act(c("sm", 0), c("sg", 4), ACT.Copy, scale=1.0 / UNIT, bias=(float(wn + K * rank) * TAG + B * rank + 1) / UNIT)
+        nl = 2 if mid else 1
         if t > 0:
-            ts(c("g16", 0), c("sg", 4), 1.0 / GID, A.mult)
-        tt(V("d2", 0, 32), V("br", 0, 32), V("sb", 4, 36), A.subtract)
+            ts(V("g16", 0, nl), V("pc", TWO, TWO + nl), c("sg", 4), A.add, 1.0 / GID, A.mult)
         ts(c("gi", 0), c("sg", 4), 1.0 / GID, A.mult)
-        tt(V("a2", 0, 32), V("d2", 0, 32), V("tb3", 0, 32), A.is_gt)
-        ts(c("sm", 1), c("gi", 0), -GID, A.mult, c("sg", 4), A.add)
+        tt(V("a2", 0, 32), V("br", 0, 32), V("d2", 0, 32), A.is_gt)
+        turn(V("ktr", 0, 32), V("gf", 0, 32))
+        if t > 0:
+            tt(V("lk", 0, 16 * nl), ind(V("srow", 0, NI * nl), V("g16", 0, nl)), V("dm", 0, 16 * nl), A.mult)
         scan(V("r2", 0, 64), V("a2", 0, 64), V("neg", 0, 64), 0.0, A.add, A.max)
-        ts(c("sm", 0), c("gi", 0), 1.0 / 256, A.mult)
-        act(c("sm", 2), c("sm", 1), ACT.Copy, scale=1.0 / UNIT, bias=(float(wn + K * rank) * TAG + B * rank + 1) / UNIT)
-        if 0 < t < R - 1:
-            tt(V("lk", 16, 32), ind(V("prow", 0, NI), c("g16", 0)), V("dm", 16, 32), A.mult)
+        act(h32("mm", 1), V("ktr", 0, 32), ACT.Abs, scale=FAR, bias=c("pc", KF + 1))
+        if mid:
+            red(c("sm", 5), V("lk", 16, 32), A.add, 1)
+        ts(c("sm", 2), c("gi", 0), -GID / UNIT, A.mult, c("sm", 0), A.add)
+        ts(h32("mm", 0), V("ktr", 0, 32), c("pc", KEY), A.not_equal, BIG / 10, A.mult)
         r2 = V("r2", 32, 64)
-        ts(V("kt", 0, 32), r2, float(K - 1), A.max, c("sm", 0), A.add)
+        ts(V("kt", 0, 32), r2, K - 0.5, A.is_gt, BIG / 10, A.mult)
         act(V("kt", 32, 64), r2, ACT.Identity, scale=TAG / UNIT, bias=c("sm", 2))
-        if 0 < t < R - 1:
-            red(c("sm", 5), V("lk", 16, 32), A.add)
-        turn(V("ktr", 0, 32), V("kt", 0, 32))
+        if not last:
+            ts(c("sm", 7), c("sb", 4), 2 * NIL, A.is_gt, c("sb", 4), A.mult)
+        tt(h32("d1", 0), V("br", 0, 32), h32("mm", 0), A.subtract)
+        turn(V("d2", 32, 64), V("kt", 0, 32))
+        if mid:
+            act(c("sm", 6), c("sm", 5), ACT.Identity, bias=c("sm", 7))
+        if t > 0:
+            red(c("sm", 4), V("lk", 0, 16), A.add, 1)
+        tt(h32("d1", 1), V("br", 0, 32), h32("mm", 1), A.subtract)
         turn(V("ktr", 32, 64), V("kt", 32, 64))
         ld = "land%d" % t
-        if t == 0:
-            ts(V("kt", 64, 96), V("kp", 0, 32), c("r2", 32), A.is_equal, c("sb", 4), A.mult)
-        elif not last:
-            act(c("sm", 6), c("sm", 5), ACT.Identity, bias=c("sb", 4))
-        ts(h32("mm", 0), V("ktr", 0, 32), c("pc", KEY), A.not_equal, BIG / 10, A.mult)
-        act(h32("mm", 1), V("ktr", 0, 32), ACT.Abs, scale=FAR, bias=c("pc", KF + 1))
-        if 0 < t < R - 1:
-            ts(V("kt", 64, 96), V("kp", 0, 32), c("r2", 32), A.is_equal, c("sm", 6), A.mult)
+        if not last:
+            ts(V("kt", 64, 96), V("kp", 0, 32), c("r2", 32), A.is_equal, c("sm", 6 if t else 7), A.mult)
         for h in range(2):
-            tt(h32("bm", h), V("br", 0, 32), h32("mm", h), A.subtract)
+            tt(h32("bm", h), h32("d1", h), V("d2", 32, 64), A.subtract)
             if h == 0 and not last:
                 turn(V("ktr", 64, 96), V("kt", 64, 96))
                 red(c(ld, 8 * rank + 4), V("ktr", 64, 96), A.add, 1)
             tt(h32("tm", h), V("ktr", 32, 64), h32("mm", h), A.add)
-        act(c("sm", 3), c("sm", 1), ACT.Identity, scale=4.0)
-        unpack([2, 3] if t == 0 else [0, 1, 2, 3])
+        act(c("sm", 1), c("sg", 4), ACT.Identity, scale=4.0)
+        unpack([1, 2, 3] if t == 0 else [0, 1, 2, 3])
         for h in range(2):
             red(c(ld, 8 * rank + h), h32("bm", h), A.max)
+        ts(c("sm", 3), c("gi", 0), -4 * GID, A.mult, c("sm", 1), A.add)
+        for h in range(2):
             red(c(ld, 8 * rank + 2 + h), h32("tm", h), A.min)
         send("a%d" % t)
-        if t > 0:
-            tt(V("lk", 0, 16), ind(V("srow", 0, NI), c("g16", 0)), V("dm", 0, 16), A.mult)
-        else:
+        if t == 0:
             ts(c("sm", 4), c("gi", 0), 4.0, A.mult)
-
-        def block(j):
+        for j in range(4):
             ts(h32("w2", j), h32("kx", j % 2), c("r2", 32), A.is_equal, c("sm", 3 + j // 2), A.mult)
-
-        block(0)
-        if t > 0:
-            red(c("sm", 4), V("lk", 0, 16), A.add)
-        block(1)
-        block(2)
-        block(3)
-        turn(V("w2t", 0, 64), V("w2", 0, 64))
+            if j == 2:
+                turn(V("w2t", 0, 64), V("w2", 0, 64))
+        for j in (0, 1):
+            red(c("u2", j), h32("w2t", j), A.add, j)
         turn(V("w2t", 64, 128), V("w2", 64, 128))
-        for j in (0, 2, 1, 3):
-            red(c("u2", j), h32("w2t", j), A.add, j in (1, 3))
         ts(V("l2", 0, 2), V("u2", 0, 2), c("pc", L4), A.add)
-        ts(V("l2", 2, 4), V("u2", 2, 4), c("pc", L4), A.add)
+        for j in (2, 3):
+            red(c("u2", j), h32("w2t", j), A.add, j == 3)
         cp(V("xg", 0, 32), ind(V("dx", 0, 1024), V("l2", 0, 2)))
+        ts(V("l2", 2, 4), V("u2", 2, 4), c("pc", L4), A.add)
         tt(V("ct", 0, 32), ind(V("dw", 0, 4 * wn), V("l2", 2, 4)), V("xg", 0, 32), A.add)
         quant(V("cq%d" % t, 0, 128), V("cs%d" % t, 0, 128), V("ct", 0, 512))
         send("b%d" % t)
+        if t == 0:
+            quant(V("wq", 0, 128), V("ws", 0, 128), V("wt", 0, 512))
+        mm(V("p_y", 0, n), "wq", "ws", 0, "win", "wins", lo, n)
         act(V("yw", wn - new, wn), V("p_y", n - new, n), ACT.Copy)
         if t == 0:
             for h in range(2):
                 cp(V("vw%d" % h, 0, NI), vv[h], 1)
             later()
         else:
-            books(t - 1)
+            for part in range(4):
+                books(t - 1, part)
         if not last:
             act(V("idg", 0, 32), ind(V("jr", 0, 1024), V("l2", 0, 2)), ACT.Copy)
             for h in range(2):
-                ts(V("eh", 8 * h, 8 * h + K), V("idg", 0, 4 * K, 4), c("pc", ID4 + h), A.is_equal, HELD, A.mult)
+                ts(V("eh", NC * h + K * rank, NC * h + K * rank + K), V("idg", 0, 4 * K, 4), c("pc", ID4 + h), A.is_equal, HELD, A.mult)
         w2 = wn + NC
         if not last:
             for h in range(2):
@@ -528,47 +534,54 @@ def rank_program(g, core, T, topo):
         bs = [c("best", 40 * h + 8) for h in range(2)]
         for h in range(2):
             turn(h32("t3", h), V("best", 40 * h + 8, 40 * h + 40))
+        act(h32("d3", 0), V("tb3", 0, 32), ACT.Identity, scale=bs[0])
+        ts(h32("d3", 1), V("tb3", 0, 32), bs[1], A.mult)
+        act(V("a3", 32, 68, 34), V("best", 8, 80, 40), ACT.Relu, scale=-1.0)
         for h in range(2):
             act(V("mw", 8 * h, 8 * h + 8), V(ld, h, 64, 8), ACT.Sign, scale=-1.0, bias=bs[h])
         for h in range(2):
-            diff(h32("d3", h), h32("t3", h), bs[h], h)
-        act(V("a3", 32, 68, 34), V("best", 8, 80, 40), ACT.Relu, scale=-1.0)
+            tt(V("a3", 34 * h, 34 * h + 32), h32("t3", h), h32("d3", h), A.is_gt)
         tt(V("mw", 16, 24), V("mw", 0, 8), V(ld, 2, 64, 8), A.max)
-        tt(V("a3", 0, 32), h32("d3", 0), h32("tb3", 0), A.is_gt)
-        tt(V("a3", 34, 66), h32("d3", 1), h32("tb3", 1), A.is_lt)
+        for h in range(2):
+            red(c("pos", h), V("a3", 34 * h, 34 * h + 33), A.add)
         tt(V("mw", 24, 32), V("mw", 8, 16), V(ld, 3, 64, 8), A.max)
-        for h in range(2):
-            red(c("pos", h), V("a3", 34 * h, 34 * h + 33), A.add, 1 - h)
-        for h in range(2):
-            red(c("wt2", h), V("mw", 16 + 8 * h, 24 + 8 * h), A.min)
-        act(V("sd", 0, 2), V("pos", 0, 2), ACT.Sign, scale=-1.0, bias=M - 0.5)
         if not last:
             for h in range(2):
                 act(V("cpc", 2 + 4 * h, 6 + 4 * h), V(ld, 32 * h + 4, 32 * h + 36, 8), ACT.Identity, c("cpc", h))
             for h in range(2):
                 act(h32("cpb", h), V("zero", 0, 32), ACT.Identity, bias=c("cpc", h))
+        red(c("wt2", 0), V("mw", 16, 24), A.min)
+        ts(V("sd", 0, 2), V("pos", 0, 2), M - 0.5, A.is_lt)
+        red(c("wt2", 1), V("mw", 24, 32), A.min)
+        if not last:
+            turn(V("cpt", 0, 64), V("cpb", 0, 64))
         for h in range(2):
             ts(h32("mb", h), V("m01", 0, 32), c("wt2", h), A.mult, c("sd", h), A.mult)
+        if not last:
+            tt(V("cpx", NC, 2 * NC), V("cpt", 8, 8 + NC), V("eh", NC, 2 * NC), A.subtract)
         turn(V("mbt", 0, 64), V("mb", 0, 64))
+        if not last:
+            tt(V("cpx", 0, NC), V("cpt", 8, 8 + NC), V("eh", 0, NC), A.subtract)
+        else:
+            books(t, 0)
         x0 = 48 * (t + 1)
         for j in range(3):
             scan(V("x3", x0 + 16 * j, x0 + 16 * j + 16), V("mbt", 8 + 16 * j, 24 + 16 * j), V("neg", 0, 16),
                  c("x3", x0 - 33 + 16 * j), A.max, A.max)
-        if not last:
-            turn(V("cpt", 0, 64), V("cpb", 0, 64))
+        if last:
+            books(t, 1)
         for a in range(4):
             cp(V("x12", 3 * a, 3 * a + 3, 1, 0, 32), V("x3", x0 + 15, x0 + 48, 16, 32 * a, 32 * a + 32), a % 2)
+        if not last:
+            for h in (1, 0):
+                tt(V("vw%d" % h, wn, w2), V("p_s", 512 * h + 128 - NC, 512 * h + 128), V("cpx", NC * h, NC * h + NC), A.subtract)
+        else:
+            books(t, 2)
         for d in range(4):
             ts(V("lst", 12 * t, 12 * t + 12, 1, 32 * d, 32 * d + 32), V("x12", 0, 12, 1, 0, 32), UNIT / TAG, A.mult)
         if t == 0:
             cp(V("cpw", wn, w2), V("cpt", 8, 8 + NC), 1)
-        if not last:
-            for h in (1, 0):
-                tt(V("vw%d" % h, wn, w2), V("p_s", 512 * h + 128 - NC, 512 * h + 128), V("cpt", 8, 8 + NC), A.subtract)
-            for h in (1, 0):
-                own = V("vw%d" % h, wn + K * rank, wn + K * rank + K)
-                tt(own, own, V("eh", 8 * h, 8 * h + K), A.add)
-        else:
+        if last:
             act(V("yw", wn, w2), V("p_y", 128 - NC, 128), ACT.Copy)
 
     l0 = 12 * (R - 1)
@@ -576,16 +589,18 @@ def rank_program(g, core, T, topo):
     c1 = -(-(I * rank + I) // 16)
     at, n = I * rank - 16 * c0, 16 * (c1 - c0)
     sub = V("lst", l0 + c0, l0 + c1)
+    books(R - 1, 3)
+    act(V("osc2", 0, n), ind(V("wins", 0, NW), sub), ACT.Copy)
     op("v", lambda: g.vector.tensor_copy(T.oq[:, 0:n].bitcast(dt.uint32), T.win[:, 0:NW].bitcast(dt.uint32).indirect(x(sub))),
        V("oq", 0, n), [V("win", 0, NW), sub])
     for h in range(2):
         cp(V("yf", 96 * h, 96 * h + 96), ind(V("yw", 0, NW), V("lst", l0 + 6 * h, l0 + 6 * h + 6)), h)
-    dma("y", T.oc[:, :], V("oq", at, at + I))
+    for k in range(2):
+        dma("y", T.osc[4 * k:4 * k + 4, :], V("osc2", at, at + I, 1, 32 * k, 32 * k + 4))
+    dma("s", T.oc[:, :], V("oq", at, at + I))
     dma("y", T.y[:, :], V("yf", 0, NI))
-    act(V("osc2", 0, n), ind(V("wins", 0, NW), sub), ACT.Copy)
-    for k in range(4):
+    for k in range(2, 4):
         dma("s", T.osc[4 * k:4 * k + 4, :], V("osc2", at, at + I, 1, 32 * k, 32 * k + 4))
-    books(R - 1)
     for s in count:
         if max(waited[q].get(s, 0) for q in Q) < count[s]:
             need("g", (s, count[s]))

@@ -7,13 +7,14 @@ NC = N * K
 NW = NI + R * NC
 BIG = 1.0e29
 HELD = 1.0e28
+CAP = 2.0 ** 89
 FAR = 2.0 ** 84
-EPS = 1.0e-30
 NIL = 2.0 ** -100
 TAG = 8192.0
-UNIT = 2.0 ** 22
+UNIT = 1024.0
 GID = 512.0
 WHOLE = 2.0 ** 23
+OFF = 64.0
 C4, U8, F, BF, I32, U16 = "float8_e4m3fn_x4", "uint8", "float32", "bfloat16", "int32", "uint16"
 
 
@@ -27,21 +28,21 @@ SCRATCH = {
     "xq": _sb(256, C4), "xs": _sb(256, U8), "pq": _sb(256, C4), "ps": _sb(256, U8),
     "wq": _sb(128, C4), "ws": _sb(128, U8), "eq": _sb(512, C4), "es": _sb(512, U8),
     "win": _sb(NW, C4), "wins": _sb(NW, U8), "oq": _sb(64, C4), "osc2": _sb(64, U8),
-    "ej": _sb(129), "jr": _sb(1024), "pi": _sb(8, I32), "pc": _sb(24), "neg": _sb(NI), "zero": _sb(32), "m4": _sb(32),
-    "tb1": _sb(128), "tb3": _sb(64), "k1": _sb(32), "kp": _sb(32), "kx": _sb(96), "m01": _sb(32), "dm": _sb(32),
+    "ej": _sb(129), "jr": _sb(1024), "pi": _sb(8, I32), "pc": _sb(28), "neg": _sb(NI), "zero": _sb(32), "minus": _sb(32),
+    "tb1": _sb(128), "k1": _sb(32), "kp": _sb(32), "kx": _sb(96), "mk": _sb(33), "dm": _sb(32), "rk": _sb(97), "keep": _sb(48),
     "dx": _sb(1024), "dw": _sb(4 * (NI + 2 * NC)), "xg": _sb(32), "ct": _sb(512, BF),
     "vw0": _sb(NI + 2 * NC), "vw1": _sb(NI + 2 * NC), "cpw": _sb(NI + NC),
     "yw": _sb(NW), "yf": _sb(NI), "v0": _sb(NI), "v1": _sb(NI),
-    "pm0": _sb(NI + 1), "pm1": _sb(NI + 1), "m20": _sb(NI), "m21": _sb(NI),
-    "junk": _sb(NI), "fb": _sb(64), "goal": _sb(2), "gid": _sb(2),
-    "srow": _sb(2 * NI), "bb": _sb(64), "tr": _sb(64), "d1": _sb(128), "a1": _sb(128), "qr": _sb(2),
-    "w1": _sb(128), "w1t": _sb(128), "xx": _sb(72), "sb": _sb(36), "sg": _sb(36), "br": _sb(32), "gf": _sb(32),
-    "d2": _sb(64), "a2": _sb(64), "r2": _sb(64), "kt": _sb(96), "ktr": _sb(96), "mm": _sb(64), "bm": _sb(64), "tm": _sb(64),
-    "gi": _sb(1, I32), "g16": _sb(2, U16), "sm": _sb(8), "lk": _sb(32), "w2": _sb(128), "w2t": _sb(128), "u2": _sb(4),
+    "pm": _sb(2 * NI + 2), "m2": _sb(2 * NI), "mr": _sb(64), "pen": _sb(4),
+    "junk": _sb(2 * NI), "goal": _sb(2), "gid": _sb(2),
+    "srow": _sb(2 * NI), "bb": _sb(64), "tr": _sb(64), "th": _sb(128), "a1": _sb(128), "qr": _sb(2),
+    "w1": _sb(128), "w1t": _sb(128), "xx": _sb(72), "sb": _sb(36), "sg": _sb(36), "br": _sb(32), "gf": _sb(32), "gr": _sb(32),
+    "cap": _sb(64), "d2": _sb(32), "a2": _sb(98 * R), "r2": _sb(97), "kt": _sb(64), "pk": _sb(64), "mm": _sb(64), "bm": _sb(64), "tm": _sb(64),
+    "g16": _sb(2, U16), "sm": _sb(8), "lk": _sb(32), "w2": _sb(128), "w2t": _sb(128), "u2": _sb(4),
     "l2": _sb(4, U16), "idg": _sb(32), "eh": _sb(2 * NC), "cpx": _sb(2 * NC), "cpc": _sb(10), "cpb": _sb(64), "cpt": _sb(64),
-    "best": _sb(80), "t3": _sb(64), "d3": _sb(64), "a3": _sb(68), "pos": _sb(2), "mw": _sb(32), "wt2": _sb(2),
-    "sd": _sb(3), "tag": _sb(R + 1), "price": _sb(R + 1), "mb": _sb(64), "mbt": _sb(64),
-    "x3": _sb(48 * (R + 1)), "x12": _sb(12), "lst": _sb(12 * R, U16), "hi": _sb(2, I32), "hf": _sb(R),
+    "best": _sb(80), "t3": _sb(64), "d3": _sb(64), "a3": _sb(132), "od": _sb(132), "cn": _sb(132), "mw": _sb(16), "wn": _sb(16),
+    "tag": _sb(2 * R + 2), "price": _sb(R + 1), "bk": _sb(8 * R), "mb": _sb(64), "mbt": _sb(64),
+    "x3": _sb(192), "lst": _sb(12 * R, U16),
     "hb": _sb(8 * R), "hc": _sb(I, C4), "hs": _sb(4 * I, U8),
     "p_s": ("psum", [128, 1024], F), "p_d": ("psum", [128, 2048], F), "p_y": ("psum", [128, 512], F),
 }
@@ -57,6 +58,26 @@ SEMAPHORES = (["sv", "ss", "st", "sg", "loc"] + ["arr_" + s for s in STAGES] + [
               + ["dm%d" % k for k in range(16)])
 A = AluOpType
 ACT = ActivationFunctionType
+CYCLE, COPY, SEND, SLOW, WAY = 0.00095, 1.8, 0.5, 0.015, {"i": 6.0, "a": 4.7, "b": 4.9}
+ORDER = """
+0 2 3 1 4 45 44 40 41 5 42 43 6 48 52 46 7 51 49 8 53 50 55 56 57 61 62 65 54 66 10 25 21 68 26 11 22 27 23 28 24 80 30 14 12 9
+15 58 16 17 18 19 59 20 72 60 29 73 63 31 64 74 76 33 70 32 35 79 37 67 34 75 69 81 36 71 85 38 82 95 88 89 83 91 98 94 197 84
+198 99 97 90 47 93 92 77 13 86 39 100 101 110 104 111 112 113 106 116 119 120 114 121 117 123' 122 118 128' 115 124 129 125' 105
+130' 107 126 127 131 132 102 108 103 133 134 135 136' 196 137' 140 138' 139' 141 142' 144 143 195 147 148 149 145 152 146 151
+150 153 158 154 160 155 156 162 161 109 157 163 164 166 169 170 159 165 168 171 172 167 174 173 176 175 78 178 190 177 179' 96
+181' 180 182 183 184' 185 186 187 192 188 193 87 189 199' 201 200 194' 191 202 216 203 220 204 217 222' 218 221 219 225 226 229
+224 227 223 258 230 231 205' 228 232 206 207 254 208 213 235 209 237 239 236 238 211 241 243 244 256 240 242 210 212 252' 233
+264 253 262 265 270 274 260 271 266 214 275 267 276 277 255 268 279' 272 278 248 284' 273 280 261 285 281' 259 269' 286' 263 282
+249 283 287 288 289 291 234 290 292' 245 293' 351' 294 257' 250 296' 295 297 298' 246' 215 300 299 305 303 304 302 301 307 314
+308 306 309 316' 319 310 312 311 320 317 315 313 318 321 324 329 325 322 328 331 326 327 330 333 251 323 334 352 338 332 349 335
+337' 336 340 341 339' 343 353 342 344 345 346 347 350 354 360 369 373 370 372 375 376 377 371' 374 379 358 378 382 383 380 384
+361 381 359 385 362 348 356 355 388 363 357 411 397 407 392 389 390 391 365 408 396 394 395 393 364 247 366 406 405' 386 416 417
+422 426 418 423 419 409 428 427 401 429 420 436 424 413 421 431' 430 402' 432 437 433' 425 438' 435 434 439 440 415 441 410 443
+367 444' 442 446 445' 449' 448' 368 398 387 447 450 403 451 452 412' 404 454 456 453 457 455 458 460 465 468 459 461 463 469 462
+467 399 464 470 471 474 497 466 475 472 498 473 476 477 414 479 481 400 478 480 482 483' 484 486' 487 485 488 489' 490 495 491
+492 493 496 501 505 502 504 506 507' 511 503 510 514 508 509 494 515 512 499 528 516 513 517 518 532 533 519 529 521 530 534 531
+500 535 523 520 522 526 525 527 524 536' 537 538 539 543' 540 545' 541 544 542
+"""
 
 
 def V(name, c0, c1, step=1, p0=0, p1=128):
@@ -79,21 +100,25 @@ def _routes(T, topo, r, stage):
     far = [c for c in others if not topo.may_write(me, c)]
     mates = sorted([c for c in topo.cores_of(me) if c != me], key=lambda c: topo.die(c) != topo.die(me))
     port = [c for c in mates if all(topo.may_write(c, d) for d in far)]
+    spare = [c for c in mates if c not in port][0]
     on = topo.engines(me, port[0])
     off = topo.mask(me, near[0])
     only = [e for e in on if e not in topo.engines(me, near[0])]
     half = len(far) // 2
     if stage[0] == "a":
+        hand = [("b", [(spare, near), (port[0], far[:half]), (port[1], far[half:])])]
         out = []
-        hand = [("b", port[0], far[:half]), ("b", port[1], far[half:]), ("b", port[2], near[:half]), ("b", port[3], near[half:])]
     else:
-        out = [(me, near, "c", off, False, 1), (me, near, "s", off, False, 2)]
-        hand = [("c", port[2], far[:half]), ("c", port[0], far[half:]), ("s", port[3], far[:half]), ("s", port[1], far[half:])]
-    for (k, h, ds), m in zip(hand, _deal(on, len(hand))):
-        out.append((me, [h], k, m, True, 0))
-        out.append((h, ds, k, topo.mask(h, ds[0]), False, 0))
-        if h in port[2:] and k != "b":
-            out.append((h, [me], k, _deal(only, 2)[0], False, int(stage == "i")))
+        hand = [("c", [(port[2], far[:half] + near[:1]), (port[0], far[half:])]),
+                ("s", [(port[3], far[:half] + near[:1]), (port[1], far[half:])])]
+        out = [(me, near[1:], "c", off, False, 1), (me, [spare], "s", _deal(only, 1)[0], True, 1),
+               (spare, near[1:2], "s", off, False, 0), (me, near[2:], "s", off, False, 2)]
+    for (k, hs), m in zip(hand, _deal(on, len(hand))):
+        out.append((me, [h for h, ds in hs], k, m, True, 0))
+        for h, ds in hs:
+            out.append((h, ds, k, topo.mask(h, ds[0]), False, 0))
+        if k != "b":
+            out.append((hs[0][0], [me], k, _deal(only, 2)[0], False, int(stage == "i")))
     return out
 
 
@@ -106,7 +131,7 @@ def _places(r, stage, kind):
     c = NI + NC * t + K * r
     if kind == "b":
         n = 5 if t < R - 1 else 4
-        v = V("land%d" % t, 8 * r, 8 * r + n)
+        v = V("land%d" % t, 8 * (N - 1 - r), 8 * (N - 1 - r) + n)
         return v, v, V("hb", 8 * t, 8 * t + n), V("hb", 8 * t, 8 * t + n), v
     if kind == "c":
         return V("cq%d" % t, 0, K), V("cq%d" % t, 0, K), V("hc%d" % t, 0, K), V("hc%d" % t, 0, K), V("win", c, c + K)
@@ -153,15 +178,21 @@ def _helper(g, core, T, topo):
         g.wait_ge(T.sem.loc, sent)
 
 
+def _place(calls):
+    plan = [None] * len(calls)
+    for at, word in enumerate(ORDER.split()):
+        k = int(word.strip("'"))
+        plan[k] = (at, calls[k]["ways"][int(word[-1] == "'")])
+    assert all(plan[d][0] < plan[k][0] for k in range(len(calls)) for d in calls[k]["deps"])
+    return plan
+
+
 def rank_program(g, core, T, topo):
     rank = T.rank_of(core)
     if rank is None:
         return _helper(g, core, T, topo)
     Q = {"v": g.vector, "s": g.scalar, "t": g.tensor, "g": g, "y": g.sync}
-    count = {"sv": 0, "ss": 0, "st": 0, "sg": 0, "loc": 0}
-    waited = {q: {} for q in Q}
-    log = {}
-    ndma = [0]
+    calls, log = [], {}
 
     def flat(vs):
         out = []
@@ -171,107 +202,125 @@ def rank_program(g, core, T, topo):
         return [((v[0], v[1] // 512 * 512, v[1] // 512 * 512 + 512, 1, 0, 128) if SCRATCH[v[0]][0] == "psum" else v) for v in out]
 
     def meet(a, b):
-        if a[2] <= b[1] or b[2] <= a[1] or a[5] <= b[4] or b[5] <= a[4]:
+        if a[5] <= b[4] or b[5] <= a[4] or a[2] <= b[1] or b[2] <= a[1]:
             return False
-        return not (a[3] == b[3] > 1 and (a[1] - b[1]) % a[3])
+        return (a[3] == 1 and b[3] == 1) or bool(set(range(a[1], a[2], a[3])) & set(range(b[1], b[2], b[3])))
 
-    def need(q, tok):
-        if waited[q].get(tok[0], 0) < tok[1]:
-            Q[q].wait_ge(T.sem[tok[0]], tok[1])
-            waited[q][tok[0]] = tok[1]
-
-    def order(q, reads, writes):
-        want = {}
+    def put(ways, reads, writes, late=0.0, after=(), sem=None):
+        deps, k = set(after), len(calls)
+        mine = ways[0][0] if len(ways) == 1 else None
         for vs, w in ((flat(reads), False), (flat(writes), True)):
             for v in vs:
-                for u, uw, tok, uq in log.get(v[0], []):
-                    if (w or uw or (SCRATCH[v[0]][0] == "psum" and uq != q)) and meet(u, v):
-                        want[tok[0]] = max(want.get(tok[0], 0), tok[1])
-        for s in want:
-            need(q, (s, want[s]))
-
-    def note(q, reads, writes, tok):
+                for u, uw, j, uq in log.get(v[0], []):
+                    if (w or uw or (SCRATCH[v[0]][0] == "psum" and (uq != mine or mine is None))) and meet(u, v):
+                        deps.add(j)
         for vs, w in ((flat(reads), False), (flat(writes), True)):
             for v in vs:
-                log.setdefault(v[0], []).append((v, w, tok, q))
+                log.setdefault(v[0], []).append((v, w, k, mine))
+        calls.append({"ways": ways, "deps": sorted(deps), "late": late, "sem": sem})
+        return k
 
-    def op(q, call, out, ins, more=()):
-        order(q, ins, [out] + list(more))
-        s = "s" + q
-        count[s] += 1
-        call().then_inc(T.sem[s], 1)
-        note(q, ins, [out] + list(more), (s, count[s]))
+    def width(v):
+        return 16 * (v[2][2] - v[2][1]) if v[0] == "ind" else len(range(v[1], v[2], v[3]))
+
+    def time(a, per=1.0):
+        return 0.07 + 1.56 * width(a) * CYCLE if a[0] == "ind" else max(64, per * width(a)) * CYCLE
+
+    def op(q, call, out, ins, held, more=()):
+        return put([(q, held, call)], ins, [out] + list(more))
 
     def x(v):
         return _ap(T, v) if isinstance(v, tuple) else v
 
-    def ts(out, a, s1, o0, s2=None, o1=None):
+    def ts_(out, a, s1, o0, s2=None, o1=None):
         if o1 is None:
-            op("v", lambda: g.vector.tensor_scalar(x(out), x(a), x(s1), None, o0), out, [a, s1])
-        else:
-            op("v", lambda: g.vector.tensor_scalar(x(out), x(a), x(s1), x(s2), o0, o1), out, [a, s1, s2])
+            return ("v", time(a), lambda: g.vector.tensor_scalar(x(out), x(a), x(s1), None, o0))
+        return ("v", time(a), lambda: g.vector.tensor_scalar(x(out), x(a), x(s1), x(s2), o0, o1))
+
+    def act_(out, a, f, acc=None, **kw):
+        def call():
+            kx = {k: x(kw[k]) for k in kw}
+            if acc is not None:
+                kx["accum_out"] = x(acc)
+            return g.scalar.activation(x(out), x(a), f, **kx)
+        return ("s", time(a) + SLOW + (0.02 if acc else 0.0), call)
+
+    def ts(out, a, s1, o0, s2=None, o1=None):
+        put([ts_(out, a, s1, o0, s2, o1)], [a, s1, s2], [out])
 
     def tt(out, a, b, o):
-        op("v", lambda: g.vector.tensor_tensor(x(out), x(a), x(b), o), out, [a, b])
+        per = 1.0 if a[0] != "ind" and SCRATCH[a[0]][0] == "psum" else 2.0
+        op("v", lambda: g.vector.tensor_tensor(x(out), x(a), x(b), o), out, [a, b], time(a, per))
 
     def fill(out, c):
-        op("v", lambda: g.vector.memset(x(out), c), out, [])
+        op("v", lambda: g.vector.memset(x(out), c), out, [], time(out, 0.5 if SCRATCH[out[0]][2] == BF else 1.0))
 
     def scan(out, a, b, init, o0, o1):
-        op("v", lambda: g.vector.tensor_tensor_scan(x(out), x(a), x(b), x(init), o0, o1), out, [a, b, init])
+        op("v", lambda: g.vector.tensor_tensor_scan(x(out), x(a), x(b), x(init), o0, o1), out, [a, b, init], time(a))
 
     def turn(out, a):
-        op("v", lambda: g.vector.transpose(x(out), x(a)), out, [a])
+        op("v", lambda: g.vector.transpose(x(out), x(a)), out, [a], time(a))
 
     def quant(q, s, a):
-        op("v", lambda: g.vector.quantize_mx(x(q), x(s), x(a)), q, [a], [s])
+        op("v", lambda: g.vector.quantize_mx(x(q), x(s), x(a)), q, [a], 0.015 + 0.000275 * width(a), [s])
 
     def act(out, a, f, acc=None, **kw):
-        kx = {k: x(kw[k]) for k in kw}
-        if acc is not None:
-            kx["accum_out"] = x(acc)
-        op("s", lambda: g.scalar.activation(x(out), x(a), f, **kx), out, [a] + list(kw.values()), [acc] if acc else [])
+        put([act_(out, a, f, acc, **kw)], [a] + list(kw.values()), [out] + ([acc] if acc else []))
 
-    def cp(out, a, side=0):
-        if side:
-            act(out, a, ACT.Copy)
-        else:
-            op("v", lambda: g.vector.tensor_copy(x(out), x(a)), out, [a])
+    def cp(out, a, side=None):
+        ways = [act_(out, a, ACT.Copy), ("v", time(a), lambda: g.vector.tensor_copy(x(out), x(a)))]
+        put(ways if side is None else [ways[1 - side]], [a], [out])
 
-    def red(out, a, o, side=0):
-        if side:
-            act(a, a, ACT.Identity, out)
+    def lin(out, a, scale=None, bias=None):
+        f = ACT.Identity if isinstance(bias, tuple) or isinstance(scale, tuple) else ACT.Copy
+        if bias is None:
+            ways = [act_(out, a, f, scale=scale), ts_(out, a, scale, A.mult)]
+        elif scale is None:
+            ways = [act_(out, a, f, bias=bias), ts_(out, a, bias, A.add)]
         else:
-            op("v", lambda: g.vector.tensor_reduce(x(out), x(a), AxisListType.X, o), out, [a])
+            ways = [act_(out, a, f, scale=scale, bias=bias), ts_(out, a, scale, A.mult, bias, A.add)]
+        put(ways, [a, scale, bias], [out])
+
+    def red(out, a, o):
+        way = ("v", time(a), lambda: g.vector.tensor_reduce(x(out), x(a), AxisListType.X, o))
+        if o == A.add:
+            put([act_(a, a, ACT.Identity, out), way], [a], [out, a])
+        else:
+            put([way], [a], [out])
 
     def mm(out, lq, ls, l0, rq, rs, r0, n):
         a, b, c, d = V(lq, l0, l0 + 128), V(ls, l0, l0 + 128), V(rq, r0, r0 + n), V(rs, r0, r0 + n)
-        op("t", lambda: g.tensor.matmul_mx(x(out), x(a), x(b), x(c), x(d), True, True), out, [a, b, c, d])
+        op("t", lambda: g.tensor.matmul_mx(x(out), x(a), x(b), x(c), x(d), True, True), out, [a, b, c, d], (n + 16) * 0.6 * CYCLE)
 
     def iota(out, pat, base, cm, small=True):
+        held = 0.13 + 2 * width(out) * CYCLE
         if small:
-            op("g", lambda: g.iota(x(out), pat, base, cm, allow_small_or_imprecise_dtypes=True), out, [])
+            op("g", lambda: g.iota(x(out), pat, base, cm, allow_small_or_imprecise_dtypes=True), out, [], held)
         else:
-            op("g", lambda: g.iota(x(out), pat, base, cm), out, [])
+            op("g", lambda: g.iota(x(out), pat, base, cm), out, [], held)
 
-    def dma(q, out, a):
+    ndma, sent, went = [0], [0], []
+
+    def dma(q, out, a, after=()):
         ins = [a] if isinstance(a, tuple) else []
         outs = [out] if isinstance(out, tuple) else []
-        order(q, ins, outs)
         s = "dm%d" % ndma[0]
         ndma[0] += 1
-        count[s] = 16
-        Q[q].dma_start(_bytes(T, out) if outs else out, _bytes(T, a) if ins else a).then_inc(T.sem[s], 16)
-        note(q, ins, outs, (s, 16))
+        ways = [(z, 0.06, lambda z=z: Q[z].dma_start(_bytes(T, out) if outs else out, _bytes(T, a) if ins else a)) for z in q]
+        return put(ways, ins, outs, COPY, after, (s, 16))
 
     def send(stage):
         mine = [w for w in _routes(T, topo, rank, stage) if w[0] == core]
-        order("g", [_places(rank, stage, w[2])[1] for w in mine], [])
-        count["loc"] += _calls(g, T, topo, rank, stage, mine)
+        sent[0] += sum(_bits(w[3]) for w in mine)
+        went.append(put([("g", SEND, lambda: _calls(g, T, topo, rank, stage, mine))], [_places(rank, stage, w[2])[1] for w in mine], [],
+                        after=went, sem=("loc", None)))
+        return went[-1]
+
+    def arrive(stage, k):
         come = [(r, w) for r in range(N) for w in _routes(T, topo, r, stage) if core in w[1]]
-        s = "arr_" + stage
-        count[s] = sum(_bits(w[3]) for r, w in come)
-        note("r", [], [_places(r, stage, w[2])[4] for r, w in come], (s, count[s]))
+        way = put([("r" + stage, 0.001, None)], [], [], WAY[stage[0]] - SEND, [k], ("loc", 0))
+        return put([("r" + stage, 0.001, None)], [], [_places(r, stage, w[2])[4] for r, w in come], 0.0, [way, went[-1]],
+                   ("arr_" + stage, sum(_bits(w[3]) for r, w in come)))
 
     def ind(w, o):
         return ("ind", w, o)
@@ -288,17 +337,17 @@ def rank_program(g, core, T, topo):
     iota(c("pi", 0), [[0, 1]], 0, 1, False)
     iota(V("ej", 0, 128), [[1, 128]], 0, 0)
     iota(c("ej", 128), [[0, 1]], 0, 1)
-    iota(V("kx", 0, 32), [[0, 2], [1, 4], [0, 4]], 0, 0)
-    iota(V("kx", 32, 64), [[0, 2], [1, 4], [0, 4]], 4, 0)
+    iota(V("kx", 0, 32), [[0, 2], [-1, 4], [0, 4]], K - 1, 0)
+    iota(V("kx", 32, 64), [[0, 2], [-1, 4], [0, 4]], K - 5, 0)
     iota(V("kx", 64, 96), [[0, 2], [1, 16]], 0, 0)
     fill(V("et", 0, 2048), 0.0)
     quant(V("iq", 0, 128), V("isc", 0, 128), V("itt", 0, 512))
-    send("i")
+    items = arrive("i", send("i"))
 
     iota(V("jr", 0, 1024), [[1, 1024]], 0, 0)
     ts(V("ident", 0, 128), V("ej", 0, 128), c("ej", 128), A.is_equal)
     for b in range(4):
-        cp(V("et", 512 * b + b, 512 * b + 512, 4), V("ident", 0, 128))
+        cp(V("et", 512 * b + b, 512 * b + 512, 4), V("ident", 0, 128), 0)
     quant(V("eq", 0, 512), V("es", 0, 512), V("et", 0, 2048))
     for h in range(2):
         for a in range(4):
@@ -308,9 +357,8 @@ def rank_program(g, core, T, topo):
     for b in range(4):
         mm(V("p_d", 512 * b, 512 * b + 256), "eq", "es", 128 * b, "xq", "xs", 0, 256)
         act(V("dx", b, 1024, 4), V("p_d", 512 * b, 512 * b + 256), ACT.Identity, scale=0.5)
-    need("y", ("arr_i", count["arr_i"]))
-    dma("y", V("wt", 0, 512), T.w[:, :])
-    LANE, QUAD, L16, L4, L8, ID, ID4, KEY, TMP, KF, THR, TWO = 0, 1, 2, 3, 4, 6, 8, 10, 12, 18, 20, 22
+    dma("y", V("wt", 0, 512), T.w[:, :], [items])
+    LANE, QUAD, L16, L4, L8, ID, ID4, KEY, TMP, THR, TWO, LESS = 0, 1, 2, 3, 4, 6, 8, 10, 12, 20, 22, 24
     ts(c("pi", 1), c("pi", 0), 31, A.bitwise_and)
     ts(c("pi", 2), c("pi", 0), 5, A.logical_shift_right)
     ts(c("pi", 3), c("pi", 0), 15, A.bitwise_and)
@@ -318,68 +366,62 @@ def rank_program(g, core, T, topo):
     ts(c("pi", 6), c("pi", 0), 8.0, A.add)
     fill(V("neg", 0, NI), -BIG)
     fill(V("zero", 0, 32), 0.0)
+    fill(V("minus", 0, 32), -1.0)
     ts(c("pi", 5), c("pi", 6), 15, A.bitwise_and)
-    fill(V("tb1", 32, 64), 0.0)
-    fill(V("tb1", 64, 96), EPS)
-    cp(V("pc", 0, 5), V("pi", 1, 6))
-    for nm in ("pm0", "pm1"):
-        fill(c(nm, 0), -BIG)
-    for o, e in ((V("tb1", 0, 32), -EPS), (V("tb1", 96, 128), EPS), (V("tb3", 32, 64), -0.5 / WHOLE)):
-        ts(o, V("ej", 0, 32), c("pc", LANE), A.is_lt, e, A.mult)
+    fill(V("tb1", 32, 64), 1.0)
+    fill(V("tb1", 64, 96), 1.0 - 0.5 / WHOLE)
+    cp(V("pc", 0, 5), V("pi", 1, 6), 0)
+    fill(V("pm", 0, 2 * NI + 2, NI + 1), -BIG)
+    ts(V("d2", 0, 32), V("ej", 0, 32), c("pc", LANE), A.is_lt, -0.5 / WHOLE, A.mult)
+    for o in (V("tb1", 0, 32), V("tb1", 96, 128)):
+        ts(o, V("d2", 0, 32), 1.0, A.add)
+    tb3 = V("tb1", 0, 32)
     slot0 = K * (rank % 4) + (8 if rank < 4 else 0)
     ts(c("pc", TMP), c("pc", QUAD), 6.0, A.mult)
     ts(c("pc", ID), c("pc", QUAD), 64.0, A.mult, c("pc", LANE), A.add)
     ts(c("pc", TMP + 1), c("pc", QUAD), 48.0, A.mult, c("pc", LANE), A.add)
     ts(c("pc", TMP + 2), c("pc", LANE), 7.5, A.is_lt, -1000.0, A.mult)
     ts(c("pc", TMP + 3), c("pc", LANE), 23.5, A.is_gt, -1000.0, A.mult)
-    ts(V("d2", 0, 32), V("ej", 0, 32), c("pc", TMP), A.subtract)
+    ts(V("br", 0, 32), V("ej", 0, 32), c("pc", TMP), A.subtract)
     ts(c("pc", ID + 1), c("pc", ID), 32.0, A.add)
     ts(c("pc", TMP + 4), c("pc", TMP + 1), -8.0, A.add, c("pc", TMP + 2), A.add)
     ts(c("pc", TMP + 5), c("pc", TMP + 1), 24.0, A.add, c("pc", TMP + 3), A.add)
-    ts(V("a2", 0, 32), V("d2", 0, 32), 5.5, A.is_gt, -1000.0, A.mult)
+    ts(V("gr", 0, 32), V("br", 0, 32), 5.5, A.is_gt, -1000.0, A.mult)
     fill(V("xx", 8, 72), 0.0)
-    ts(V("pc", KEY, KEY + 2), V("pc", TMP + 4, TMP + 6), WHOLE, A.add)
-    fill(V("a2", 32, 64), 0.0)
-    tt(V("k1", 0, 32), V("d2", 0, 32), V("a2", 0, 32), A.add)
-    ts(V("pc", KF, KF + 2), V("pc", KEY, KEY + 2), -FAR, A.mult)
-    ts(V("tb3", 0, 32), V("tb3", 32, 64), 1.0, A.add)
+    ts(V("pc", KEY, KEY + 2), V("pc", TMP + 4, TMP + 6), WHOLE, A.add, -FAR, A.mult)
+    tt(V("k1", 0, 32), V("br", 0, 32), V("gr", 0, 32), A.add)
     fill(V("kp", 0, 32), -1.0)
     fill(V("ct", 32, 512), 0.0)
-    cp(V("kp", slot0, slot0 + K), V("ej", 0, K))
+    ts(V("kp", slot0, slot0 + K), V("ej", 0, K), -1.0, A.mult, K - 1.0, A.add)
+    fill(V("a2", 0, 98 * R), 0.0)
+    fill(V("rk", 0, 97), 1.0)
+    fill(c("rk", 33), 1.0 / UNIT)
+    fill(c("pc", LESS), -NIL)
+    for t in range(R):
+        fill(c("a2", 98 * t + 65), (NI + NC * t + K * rank - 0.5) / UNIT)
+    fill(c("rk", 65), -CAP)
+    ts(V("pc", TWO, TWO + 2), V("ej", 0, 2), NI * GID, A.mult)
+    ts(V("mk", 1, 33), V("kx", 64, 96), c("pc", L8), A.not_equal, OFF, A.mult)
+    fill(c("mk", 0), 0.0)
+    fill(V("od", 0, 132), BIG)
+    fill(V("keep", 0, 48), 1.0)
+    for t in range(R):
+        fill(V("land%d" % t, 64, 320), -BIG)
+    for h in range(2):
+        tt(V("a3", 66 * h + 33, 66 * h + 65), V("mk", 1, 33), V("mk", 0, 32), A.subtract)
+    fill(V("keep", 0, 48, 16), 0.0)
+    ts(V("mk", 1, 33), V("mk", 1, 33), BIG / OFF, A.mult)
+    ts(V("dm", 0, 16), V("ej", 0, 16), c("pc", L16), A.is_equal, 4.0, A.mult)
+    ts(V("dm", 16, 32), V("ej", 0, 16), c("pc", L16), A.is_equal)
+    ts(V("pc", ID4, ID4 + 2), V("pc", ID, ID + 2), 4.0, A.mult)
+    ts(V("tag", 0, 2), V("pc", TMP + 4, TMP + 6), -1.0 / TAG, A.add, -1.0 / UNIT, A.mult)
+    fill(c("price", 0), 0.0)
+    fill(V("cpw", 0, NI), 0.0)
+    fill(V("eh", 0, 2 * NC), 0.0)
+    fill(c("pc", THR), -HELD / 10)
     own_h, own_p = rank % 2, 32 * (rank // 2) + (0 if rank % 2 else 8)
 
-    def later():
-        ts(V("m01", 0, 32), V("kx", 64, 96), c("pc", L8), A.is_equal)
-        ts(c("pc", TMP), c("pc", QUAD), 48.0, A.mult, c("pc", L16), A.add)
-        for t in range(R):
-            fill(V("land%d" % t, 64, 320), -BIG)
-        ts(V("x3", 15, 48, 16), V("ej", 0, 48, 16), c("pc", TMP), A.add, TAG / UNIT, A.mult)
-        ts(V("dm", 0, 16), V("ej", 0, 16), c("pc", L16), A.is_equal, 4.0, A.mult)
-        ts(V("dm", 16, 32), V("ej", 0, 16), c("pc", L16), A.is_equal)
-        ts(V("pc", ID4, ID4 + 2), V("pc", ID, ID + 2), 4.0, A.mult)
-        ts(V("pc", TWO, TWO + 2), V("ej", 0, 2), NI * GID, A.mult)
-        ts(c("tag", 0), c("pc", TMP + 4 + own_h), TAG / UNIT, A.mult)
-        fill(c("price", 0), 0.0)
-        fill(V("cpw", 0, NI), 0.0)
-        fill(V("m4", 0, 32), -4.0)
-        fill(V("eh", 0, 2 * NC), 0.0)
-        fill(c("pc", THR), HELD / 10)
-
-    def books(t, part):
-        h = own_h
-        if part == 0:
-            ts(c("tag", t + 1), c("wt2", h), c("sd", h), A.mult, c("tag", t), A.max)
-            ts(c("sd", 2), c("best", 40 * h + 8), 2 * NIL, A.is_gt, c("sd", h), A.mult)
-        elif part == 1:
-            ts(c("hi", 0), c("tag", t + 1), UNIT, A.mult)
-            ts(c("price", t + 1), c("best", 40 * h + 8), c("sd", 2), A.mult, c("price", t), A.add)
-            dma("y", T.pr[t, :], V("price", t + 1, t + 2, 1, own_p, own_p + I))
-        elif part == 2:
-            ts(c("hi", 1), c("hi", 0), int(TAG) - 1, A.bitwise_and)
-        else:
-            ts(c("hf", t), c("hi", 1), -1.0, A.add)
-            dma("y", T.ho[t, :], V("hf", t, t + 1, 1, own_p, own_p + I))
-
+    P1 = NI + 1
     for t in range(R):
         last = t == R - 1
         mid = 0 < t < R - 1
@@ -388,219 +430,206 @@ def rank_program(g, core, T, topo):
         new = NI if t == 0 else NC
         lst = V("lst", 12 * (t - 1), 12 * t)
         vv = [V("p_s", 512 * h, 512 * h + NI) if t == 0 else V("v%d" % h, 0, NI) for h in range(2)]
+        base = wn + K * rank + K - 1
         for h in range(2):
             if t == 0:
                 mm(vv[h], "pq", "ps", 128 * h, "win", "wins", lo, n)
             else:
-                cp(vv[h], ind(V("vw%d" % h, 0, wn), lst), h)
-        if mid:
-            act(V("srow", NI, 2 * NI), ind(V("cpw", 0, wn), lst), ACT.Copy)
+                cp(vv[h], ind(V("vw%d" % h, 0, wn), lst))
         for b in range(4):
             mm(V("p_d", 512 * b, 512 * b + n), "eq", "es", 128 * b, "win", "wins", lo, n)
-        for h in range(2):
-            scan(V("pm%d" % h, 1, NI + 1), vv[h], V("neg", 0, NI), -BIG, A.max, A.max)
-        for h in range(2):
-            scan(V("m2%d" % h, 0, NI), vv[h], V("pm%d" % h, 0, NI), -BIG, A.max, A.min)
-        m1 = [c("pm%d" % h, NI) for h in range(2)]
-        for h in range(2):
-            if t > 0:
-                act(h32("fb", h), V("m4", 0, 32), ACT.Identity, scale=m1[h], bias=c("pc", THR))
-            act(V("junk", 0, NI), V("pm%d" % h, 1, NI + 1), ACT.Sign, c("goal", h), scale=-1.0, bias=m1[h])
-        for h in range(2):
-            act(c("gid", h), c("goal", h), ACT.Identity, scale=GID, bias=c("pc", ID + h))
-
-        def unpack(bs):
-            for b in bs:
-                act(V("dw", 4 * (wn - new) + b, 4 * wn, 4), V("p_d", 512 * b + n - new, 512 * b + n), ACT.Identity, scale=0.5)
-
-        for h in range(2):
-            if t > 0:
-                ts(h32("bb", h), h32("fb", h), m1[h], A.min, c("m2%d" % h, NI - 1), A.subtract)
-            else:
-                ts(h32("bb", h), V("zero", 0, 32), m1[h], A.add, c("m2%d" % h, NI - 1), A.subtract)
-        turn(V("tr", 0, 64), V("bb", 0, 64))
-        ts(V("d1", 0, 64), V("tr", 0, 64), c("bb", 0), A.subtract)
-        act(V("d1", 64, 128), V("tr", 0, 64), ACT.Identity, scale=-1.0, bias=c("bb", 32))
-        for h in range(2):
-            tt(V("a1", 64 * h, 64 * h + 64), V("d1", 64 * h, 64 * h + 64), V("tb1", 64 * h, 64 * h + 64), A.is_lt if h else A.is_gt)
-        for h in range(2):
-            red(c("qr", h), V("a1", 64 * h, 64 * h + 64), A.add, 1 - h)
+            lin(V("dw", 4 * (wn - new) + b, 4 * wn, 4), V("p_d", 512 * b + n - new, 512 * b + n), 0.5)
         if t > 0:
-            act(V("srow", 0, NI), ind(V("jr", 0, wn), lst), ACT.Copy)
-        else:
-            unpack([0])
+            cp(V("srow", 0, NI), ind(V("jr", 0, wn), lst))
+        if mid:
+            cp(V("srow", NI, 2 * NI), ind(V("cpw", 0, wn), lst))
         for h in range(2):
+            scan(V("pm", P1 * h + 1, P1 * h + P1), vv[h], V("neg", 0, NI), -BIG, A.max, A.max)
+        for h in range(2):
+            scan(V("m2", NI * h, NI * h + NI), vv[h], V("pm", P1 * h, P1 * h + NI), -BIG, A.max, A.min)
+        m1 = [c("pm", P1 * h + NI) for h in range(2)]
+        for h in range(2):
+            act(V("junk", NI * h, NI * h + NI), V("pm", P1 * h + 1, P1 * h + P1), ACT.Sign, c("goal", h), scale=-1.0, bias=m1[h])
+            lin(c("gid", h), c("goal", h), GID, c("pc", ID + h))
+            if t > 0:
+                act(c("pen", h), m1[h], ACT.Relu, scale=4.0, bias=c("pc", THR))
+                lin(h32("mr", h), V("minus", 0, 32), c("pen", h), m1[h])
+            else:
+                lin(h32("mr", h), V("zero", 0, 32), None, m1[h])
+        for h in range(2):
+            ts(h32("bb", h), h32("mr", h), c("m2", NI * h + NI - 1), A.subtract, NIL, A.add)
+        turn(V("tr", 0, 64), V("bb", 0, 64))
+        for h in range(2):
+            lin(V("th", 64 * h, 64 * h + 64), V("tb1", 64 * h, 64 * h + 64), c("bb", 32 * h))
+            tt(V("a1", 64 * h, 64 * h + 64), V("tr", 0, 64), V("th", 64 * h, 64 * h + 64), A.is_gt)
+            red(c("qr", h), V("a1", 64 * h, 64 * h + 64), A.add)
             ts(h32("w1", h), V("k1", 0, 32), c("qr", h), A.is_equal, c("bb", 32 * h), A.mult)
-        for h in range(2):
             ts(h32("w1", 2 + h), V("k1", 0, 32), c("qr", h), A.is_equal, c("gid", h), A.mult)
         for j in range(2):
             turn(V("w1t", 64 * j, 64 * j + 64), V("w1", 64 * j, 64 * j + 64))
-        for j in range(2):
-            red(c("xx", j), V("w1t", 64 * j, 64 * j + 64), A.add, 1 - j)
+            red(c("xx", j), V("w1t", 64 * j, 64 * j + 64), A.add)
         for d in range(2):
-            cp(V("xx", 2, 4, 1, 64 * d, 64 * d + 64), V("xx", 0, 2, 1, 64 - 64 * d, 128 - 64 * d), d)
+            cp(V("xx", 2, 4, 1, 64 * d, 64 * d + 64), V("xx", 0, 2, 1, 64 - 64 * d, 128 - 64 * d))
         for d in range(4):
-            cp(V("xx", 4, 8, 1, 32 * d, 32 * d + 32), V("xx", 0, 4, 1, 32 * (d ^ 1), 32 * (d ^ 1) + 32), d % 2)
-        scan(V("sb", 0, 36), V("xx", 0, 72, 2), V("neg", 0, 36), NIL, A.add, A.max)
+            cp(V("xx", 4, 8, 1, 32 * d, 32 * d + 32), V("xx", 0, 4, 1, 32 * (d ^ 1), 32 * (d ^ 1) + 32))
+        scan(V("sb", 0, 36), V("xx", 0, 72, 2), V("neg", 0, 36), 0.0, A.add, A.max)
         scan(V("sg", 0, 36), V("xx", 1, 72, 2), V("neg", 0, 36), 0.0, A.add, A.max)
         turn(V("br", 0, 32), V("sb", 4, 36))
-        act(V("d2", 0, 32), V("tb3", 0, 32), ACT.Identity, scale=c("sb", 4))
-        act(V("gf", 0, 32), V("sg", 4, 36), ACT.Copy, scale=1.0 / GID, bias=WHOLE)
-        act(c("sm", 0), c("sg", 4), ACT.Copy, scale=1.0 / UNIT, bias=(float(wn + K * rank) * TAG + B * rank + 1) / UNIT)
+        lin(V("d2", 0, 32), tb3, c("sb", 4))
+        turn(V("gf", 0, 32), V("sg", 4, 36))
+        lin(c("sm", 0), c("sg", 4), -1.0 / TAG, -(base + B * rank / TAG))
         nl = 2 if mid else 1
-        if t > 0:
-            ts(V("g16", 0, nl), V("pc", TWO, TWO + nl), c("sg", 4), A.add, 1.0 / GID, A.mult)
-        ts(c("gi", 0), c("sg", 4), 1.0 / GID, A.mult)
-        tt(V("a2", 0, 32), V("br", 0, 32), V("d2", 0, 32), A.is_gt)
-        turn(V("ktr", 0, 32), V("gf", 0, 32))
+        a0 = 98 * t
+        ts(V("g16", 0, nl), V("pc", TWO, TWO + nl), c("sg", 4), A.add, 1.0 / GID, A.mult)
+        tt(V("a2", a0, a0 + 32), V("br", 0, 32), V("d2", 0, 32), A.is_gt)
+        lin(V("gr", 0, 32), V("gf", 0, 32), 1.0 / GID, WHOLE)
+        ts(c("a2", a0 + 33), c("g16", 0), GID / TAG, A.mult, c("sm", 0), A.add)
+        if not last:
+            act(c("sm", 7), c("sb", 4), ACT.Relu, bias=c("pc", LESS))
+        for h in range(2):
+            act(h32("mm", h), V("gr", 0, 32), ACT.Abs, scale=FAR, bias=c("pc", KEY + h))
+            tt(h32("cap", h), V("br", 0, 32), h32("mm", h), A.subtract)
         if t > 0:
             tt(V("lk", 0, 16 * nl), ind(V("srow", 0, NI * nl), V("g16", 0, nl)), V("dm", 0, 16 * nl), A.mult)
-        scan(V("r2", 0, 64), V("a2", 0, 64), V("neg", 0, 64), 0.0, A.add, A.max)
-        act(h32("mm", 1), V("ktr", 0, 32), ACT.Abs, scale=FAR, bias=c("pc", KF + 1))
+            red(c("sm", 4), V("lk", 0, 16), A.add)
+        else:
+            ts(c("sm", 4), c("g16", 0), 4.0, A.mult)
         if mid:
-            red(c("sm", 5), V("lk", 16, 32), A.add, 1)
-        ts(c("sm", 2), c("gi", 0), -GID / UNIT, A.mult, c("sm", 0), A.add)
-        ts(h32("mm", 0), V("ktr", 0, 32), c("pc", KEY), A.not_equal, BIG / 10, A.mult)
-        r2 = V("r2", 32, 64)
-        ts(V("kt", 0, 32), r2, K - 0.5, A.is_gt, BIG / 10, A.mult)
-        act(V("kt", 32, 64), r2, ACT.Identity, scale=TAG / UNIT, bias=c("sm", 2))
+            red(c("sm", 5), V("lk", 16, 32), A.add)
+            lin(c("sm", 6), c("sm", 5), None, c("sm", 7))
+        lin(c("sm", 3), c("a2", a0 + 33), -4 * TAG, -4 * (base * TAG + B * rank))
+        scan(V("r2", 0, 97), V("a2", a0, a0 + 97), V("rk", 0, 97), 0.0, A.add, A.mult)
+        r2 = c("r2", 32)
+        turn(V("kt", 0, 64), V("r2", 33, 97))
+        ld, l0 = "land%d" % t, 8 * (N - 1 - rank)
         if not last:
-            ts(c("sm", 7), c("sb", 4), 2 * NIL, A.is_gt, c("sb", 4), A.mult)
-        tt(h32("d1", 0), V("br", 0, 32), h32("mm", 0), A.subtract)
-        turn(V("d2", 32, 64), V("kt", 0, 32))
-        if mid:
-            act(c("sm", 6), c("sm", 5), ACT.Identity, bias=c("sm", 7))
-        if t > 0:
-            red(c("sm", 4), V("lk", 0, 16), A.add, 1)
-        tt(h32("d1", 1), V("br", 0, 32), h32("mm", 1), A.subtract)
-        turn(V("ktr", 32, 64), V("kt", 32, 64))
-        ld = "land%d" % t
-        if not last:
-            ts(V("kt", 64, 96), V("kp", 0, 32), c("r2", 32), A.is_equal, c("sm", 6 if t else 7), A.mult)
+            ts(h32("pk", 0), V("kp", 0, 32), r2, A.is_equal, c("sm", 6 if t else 7), A.mult)
+            turn(h32("pk", 1), h32("pk", 0))
+            red(c(ld, l0 + 4), h32("pk", 1), A.add)
         for h in range(2):
-            tt(h32("bm", h), h32("d1", h), V("d2", 32, 64), A.subtract)
-            if h == 0 and not last:
-                turn(V("ktr", 64, 96), V("kt", 64, 96))
-                red(c(ld, 8 * rank + 4), V("ktr", 64, 96), A.add, 1)
-            tt(h32("tm", h), V("ktr", 32, 64), h32("mm", h), A.add)
-        act(c("sm", 1), c("sg", 4), ACT.Identity, scale=4.0)
-        unpack([1, 2, 3] if t == 0 else [0, 1, 2, 3])
-        for h in range(2):
-            red(c(ld, 8 * rank + h), h32("bm", h), A.max)
-        ts(c("sm", 3), c("gi", 0), -4 * GID, A.mult, c("sm", 1), A.add)
-        for h in range(2):
-            red(c(ld, 8 * rank + 2 + h), h32("tm", h), A.min)
-        send("a%d" % t)
-        if t == 0:
-            ts(c("sm", 4), c("gi", 0), 4.0, A.mult)
+            tt(h32("tm", h), V("kt", 0, 32), h32("mm", h), A.add)
+            tt(h32("bm", h), h32("cap", h), h32("kt", 1), A.min)
+            red(c(ld, l0 + 2 + h), h32("tm", h), A.min)
+            red(c(ld, l0 + h), h32("bm", h), A.max)
+        bids = send("a%d" % t)
+        for j in range(2):
+            ts(V("w2", 64 * j, 64 * j + 64), V("kx", 0, 64), r2, A.is_equal, c("sm", 3 + j), A.mult)
+            turn(V("w2t", 64 * j, 64 * j + 64), V("w2", 64 * j, 64 * j + 64))
         for j in range(4):
-            ts(h32("w2", j), h32("kx", j % 2), c("r2", 32), A.is_equal, c("sm", 3 + j // 2), A.mult)
-            if j == 2:
-                turn(V("w2t", 0, 64), V("w2", 0, 64))
-        for j in (0, 1):
-            red(c("u2", j), h32("w2t", j), A.add, j)
-        turn(V("w2t", 64, 128), V("w2", 64, 128))
-        ts(V("l2", 0, 2), V("u2", 0, 2), c("pc", L4), A.add)
-        for j in (2, 3):
-            red(c("u2", j), h32("w2t", j), A.add, j == 3)
+            red(c("u2", j), h32("w2t", j), A.add)
+        for j in range(2):
+            ts(V("l2", 2 * j, 2 * j + 2), V("u2", 2 * j, 2 * j + 2), c("pc", L4), A.add)
         cp(V("xg", 0, 32), ind(V("dx", 0, 1024), V("l2", 0, 2)))
-        ts(V("l2", 2, 4), V("u2", 2, 4), c("pc", L4), A.add)
         tt(V("ct", 0, 32), ind(V("dw", 0, 4 * wn), V("l2", 2, 4)), V("xg", 0, 32), A.add)
         quant(V("cq%d" % t, 0, 128), V("cs%d" % t, 0, 128), V("ct", 0, 512))
-        send("b%d" % t)
+        arrive("b%d" % t, send("b%d" % t))
+        arrive("a%d" % t, bids)
         if t == 0:
             quant(V("wq", 0, 128), V("ws", 0, 128), V("wt", 0, 512))
-        mm(V("p_y", 0, n), "wq", "ws", 0, "win", "wins", lo, n)
-        act(V("yw", wn - new, wn), V("p_y", n - new, n), ACT.Copy)
-        if t == 0:
+            mm(V("p_y", 0, n), "wq", "ws", 0, "win", "wins", lo, n)
+            cp(V("yw", 0, NI), V("p_y", 0, NI))
             for h in range(2):
-                cp(V("vw%d" % h, 0, NI), vv[h], 1)
-            later()
-        else:
-            for part in range(4):
-                books(t - 1, part)
+                cp(V("vw%d" % h, 0, NI), vv[h])
+        for h in range(2):
+            lin(V("od", 66 * h + 33, 66 * h + 65), V("mk", 1, 33), None, c("tag", 2 * t + h))
         if not last:
-            act(V("idg", 0, 32), ind(V("jr", 0, 1024), V("l2", 0, 2)), ACT.Copy)
+            cp(V("idg", 0, 32), ind(V("jr", 0, 1024), V("l2", 0, 2)))
             for h in range(2):
                 ts(V("eh", NC * h + K * rank, NC * h + K * rank + K), V("idg", 0, 4 * K, 4), c("pc", ID4 + h), A.is_equal, HELD, A.mult)
         w2 = wn + NC
         if not last:
             for h in range(2):
                 mm(V("p_s", 512 * h, 512 * h + 128), "pq", "ps", 128 * h, "win", "wins", w2 - 128, 128)
-        else:
-            mm(V("p_y", 0, 128), "wq", "ws", 0, "win", "wins", w2 - 128, 128)
-        for h in range(2):
-            scan(V("best", 40 * h, 40 * h + 40), V(ld, h, 320, 8), V("neg", 0, 40), -BIG, A.max, A.max)
+            for h in range(2):
+                act(V("cpc", 2 + 4 * h, 6 + 4 * h), V(ld, 36 - 32 * h, 68 - 32 * h, 8), ACT.Identity, c("cpc", h))
+                lin(h32("cpb", h), V("zero", 0, 32), None, c("cpc", h))
+            turn(V("cpt", 0, 64), V("cpb", 0, 64))
+            for h in range(2):
+                tt(V("cpx", NC * h, NC * h + NC), V("cpt", 8, 8 + NC), V("eh", NC * h, NC * h + NC), A.subtract)
+                tt(V("vw%d" % h, wn, w2), V("p_s", 512 * h + 128 - NC, 512 * h + 128), V("cpx", NC * h, NC * h + NC), A.subtract)
+            if t == 0:
+                cp(V("cpw", wn, w2), V("cpt", 8, 8 + NC))
+        mm(V("p_y", 0, 128), "wq", "ws", 0, "win", "wins", w2 - 128, 128)
+        cp(V("yw", wn, w2), V("p_y", 128 - NC, 128))
         bs = [c("best", 40 * h + 8) for h in range(2)]
         for h in range(2):
+            scan(V("best", 40 * h, 40 * h + 40), V(ld, h, 320, 8), V("neg", 0, 40), -1.0, A.max, A.max)
             turn(h32("t3", h), V("best", 40 * h + 8, 40 * h + 40))
-        act(h32("d3", 0), V("tb3", 0, 32), ACT.Identity, scale=bs[0])
-        ts(h32("d3", 1), V("tb3", 0, 32), bs[1], A.mult)
-        act(V("a3", 32, 68, 34), V("best", 8, 80, 40), ACT.Relu, scale=-1.0)
-        for h in range(2):
+            lin(h32("d3", h), tb3, bs[h])
             act(V("mw", 8 * h, 8 * h + 8), V(ld, h, 64, 8), ACT.Sign, scale=-1.0, bias=bs[h])
+        act(V("a3", 32, 132, 66), V("best", 8, 80, 40), ACT.Relu, scale=-OFF)
         for h in range(2):
-            tt(V("a3", 34 * h, 34 * h + 32), h32("t3", h), h32("d3", h), A.is_gt)
-        tt(V("mw", 16, 24), V("mw", 0, 8), V(ld, 2, 64, 8), A.max)
-        for h in range(2):
-            red(c("pos", h), V("a3", 34 * h, 34 * h + 33), A.add)
-        tt(V("mw", 24, 32), V("mw", 8, 16), V(ld, 3, 64, 8), A.max)
-        if not last:
-            for h in range(2):
-                act(V("cpc", 2 + 4 * h, 6 + 4 * h), V(ld, 32 * h + 4, 32 * h + 36, 8), ACT.Identity, c("cpc", h))
-            for h in range(2):
-                act(h32("cpb", h), V("zero", 0, 32), ACT.Identity, bias=c("cpc", h))
-        red(c("wt2", 0), V("mw", 16, 24), A.min)
-        ts(V("sd", 0, 2), V("pos", 0, 2), M - 0.5, A.is_lt)
-        red(c("wt2", 1), V("mw", 24, 32), A.min)
-        if not last:
-            turn(V("cpt", 0, 64), V("cpb", 0, 64))
-        for h in range(2):
-            ts(h32("mb", h), V("m01", 0, 32), c("wt2", h), A.mult, c("sd", h), A.mult)
-        if not last:
-            tt(V("cpx", NC, 2 * NC), V("cpt", 8, 8 + NC), V("eh", NC, 2 * NC), A.subtract)
+            tt(V("a3", 66 * h, 66 * h + 32), h32("t3", h), h32("d3", h), A.is_gt)
+            scan(V("wn", 8 * h, 8 * h + 8), V("mw", 8 * h, 8 * h + 8), V(ld, 2 + h, 64, 8), c("tag", 2 * t + h), A.mult, A.min)
+            scan(V("cn", 66 * h, 66 * h + 65), V("a3", 66 * h, 66 * h + 65), V("od", 66 * h, 66 * h + 65), 0.5 - M, A.add, A.min)
+            ts(h32("mb", h), V("cn", 66 * h + 33, 66 * h + 65), c("wn", 8 * h + 7), A.max, 0.0, A.min)
+        for h in (own_h, 1 - own_h)[:1 if last else 2]:
+            ts(c("tag", 2 * t + 2 + h), c("cn", 66 * h + 32), c("tag", 2 * t + h), A.min, c("wn", 8 * h + 7), A.max)
         turn(V("mbt", 0, 64), V("mb", 0, 64))
-        if not last:
-            tt(V("cpx", 0, NC), V("cpt", 8, 8 + NC), V("eh", 0, NC), A.subtract)
-        else:
-            books(t, 0)
-        x0 = 48 * (t + 1)
-        for j in range(3):
-            scan(V("x3", x0 + 16 * j, x0 + 16 * j + 16), V("mbt", 8 + 16 * j, 24 + 16 * j), V("neg", 0, 16),
-                 c("x3", x0 - 33 + 16 * j), A.max, A.max)
-        if last:
-            books(t, 1)
         for a in range(4):
-            cp(V("x12", 3 * a, 3 * a + 3, 1, 0, 32), V("x3", x0 + 15, x0 + 48, 16, 32 * a, 32 * a + 32), a % 2)
-        if not last:
-            for h in (1, 0):
-                tt(V("vw%d" % h, wn, w2), V("p_s", 512 * h + 128 - NC, 512 * h + 128), V("cpx", NC * h, NC * h + NC), A.subtract)
-        else:
-            books(t, 2)
+            scan(V("x3", 48 * a, 48 * a + 48, 1, 0, 32), V("keep", 0, 48, 1, 32 * a, 32 * a + 32),
+                 V("mbt", 8, 56, 1, 32 * a, 32 * a + 32), 0.0, A.mult, A.min)
         for d in range(4):
-            ts(V("lst", 12 * t, 12 * t + 12, 1, 32 * d, 32 * d + 32), V("x12", 0, 12, 1, 0, 32), UNIT / TAG, A.mult)
-        if t == 0:
-            cp(V("cpw", wn, w2), V("cpt", 8, 8 + NC), 1)
-        if last:
-            act(V("yw", wn, w2), V("p_y", 128 - NC, 128), ACT.Copy)
+            ts(V("lst", 12 * t, 12 * t + 12, 1, 32 * d, 32 * d + 32), V("x3", 15, 192, 16, 0, 32), -UNIT, A.mult)
+        h, k = own_h, 8 * t
+        act(c("bk", k), bs[h], ACT.Relu, bias=c("pc", LESS))
+        ts(c("bk", k + 1), c("cn", 66 * h + 32), 0.0, A.is_lt, c("bk", k), A.mult)
+        lin(c("price", t + 1), c("bk", k + 1), None, c("price", t))
+        dma("y", T.pr[t, :], V("price", t + 1, t + 2, 1, own_p, own_p + I))
+        lin(c("bk", k + 2), c("tag", 2 * t + 2 + h), -UNIT, WHOLE)
+        lin(c("bk", k + 3), c("bk", k + 2), -TAG, TAG * WHOLE)
+        lin(c("bk", k + 4), c("tag", 2 * t + 2 + h), -TAG * UNIT, c("bk", k + 3))
+        dma("y", T.ho[t, :], V("bk", k + 4, k + 5, 1, own_p, own_p + I))
 
     l0 = 12 * (R - 1)
     c0 = I * rank // 32 * 2
     c1 = -(-(I * rank + I) // 16)
     at, n = I * rank - 16 * c0, 16 * (c1 - c0)
     sub = V("lst", l0 + c0, l0 + c1)
-    books(R - 1, 3)
-    act(V("osc2", 0, n), ind(V("wins", 0, NW), sub), ACT.Copy)
-    op("v", lambda: g.vector.tensor_copy(T.oq[:, 0:n].bitcast(dt.uint32), T.win[:, 0:NW].bitcast(dt.uint32).indirect(x(sub))),
-       V("oq", 0, n), [V("win", 0, NW), sub])
     for h in range(2):
-        cp(V("yf", 96 * h, 96 * h + 96), ind(V("yw", 0, NW), V("lst", l0 + 6 * h, l0 + 6 * h + 6)), h)
-    for k in range(2):
-        dma("y", T.osc[4 * k:4 * k + 4, :], V("osc2", at, at + I, 1, 32 * k, 32 * k + 4))
-    dma("s", T.oc[:, :], V("oq", at, at + I))
-    dma("y", T.y[:, :], V("yf", 0, NI))
-    for k in range(2, 4):
-        dma("s", T.osc[4 * k:4 * k + 4, :], V("osc2", at, at + I, 1, 32 * k, 32 * k + 4))
+        cp(V("yf", 96 * h, 96 * h + 96), ind(V("yw", 0, NW), V("lst", l0 + 6 * h, l0 + 6 * h + 6)))
+    k = dma("y", T.y[:, :], V("yf", 0, NI))
+    calls[k]["late"] += 0.3
+    cp(V("osc2", 0, n), ind(V("wins", 0, NW), sub))
+    op("v", lambda: g.vector.tensor_copy(T.oq[:, 0:n].bitcast(dt.uint32), T.win[:, 0:NW].bitcast(dt.uint32).indirect(x(sub))),
+       V("oq", 0, n), [V("win", 0, NW), sub], time(ind(None, sub)))
+    dma("ys", T.oc[:, :], V("oq", at, at + I))
+    for k in range(4):
+        dma("ys", T.osc[4 * k:4 * k + 4, :], V("osc2", at, at + I, 1, 32 * k, 32 * k + 4))
+
+    plan = _place(calls)
+    count = {"sv": 0, "ss": 0, "st": 0, "sg": 0, "loc": sent[0]}
+    waited = {q: {} for q in Q}
+    token = {}
+
+    def need(q, s, n):
+        if waited[q].get(s, 0) < n:
+            Q[q].wait_ge(T.sem[s], n)
+            waited[q][s] = n
+
+    for k in sorted(range(len(calls)), key=lambda j: (plan[j][0], j)):
+        q, held, call = plan[k][1]
+        sem = calls[k]["sem"]
+        if call is None:
+            token[k] = sem
+            count[sem[0]] = max(count.get(sem[0], 0), sem[1])
+            continue
+        want = {}
+        for d in calls[k]["deps"]:
+            if d in token:
+                want[token[d][0]] = max(want.get(token[d][0], 0), token[d][1])
+        for s in want:
+            need(q, s, want[s])
+        if sem is None:
+            count["s" + q] += 1
+            call().then_inc(T.sem["s" + q], 1)
+            token[k] = ("s" + q, count["s" + q])
+        elif sem[1] is None:
+            call()
+        else:
+            call().then_inc(T.sem[sem[0]], sem[1])
+            token[k] = sem
+            count[sem[0]] = sem[1]
     for s in count:
         if max(waited[q].get(s, 0) for q in Q) < count[s]:
-            need("g", (s, count[s]))
+            need("g", s, count[s])

@@ -7,14 +7,20 @@ NC = N * K
 NW = NI + R * NC
 BIG = 1.0e29
 HELD = 1.0e28
-CAP = 2.0 ** 89
-FAR = 2.0 ** 84
 NIL = 2.0 ** -100
-TAG = 8192.0
-UNIT = 1024.0
+H = 2.0 ** 80
+OUT = 1024.0
+TAG = 4096.0
+LIFT = 512.0
 GID = 512.0
+U = H / 2.0 ** 18
 WHOLE = 2.0 ** 23
-OFF = 64.0
+STEP = 0.5 / WHOLE
+DIM = 2.0 ** -20
+RISE, FALL = 8 * H, 8192 * H
+W2 = NI + 99
+GAP = 140
+CUTS = (((0, 12),), ((0, 12),))
 C4, U8, F, BF, I32, U16 = "float8_e4m3fn_x4", "uint8", "float32", "bfloat16", "int32", "uint16"
 
 
@@ -28,20 +34,22 @@ SCRATCH = {
     "xq": _sb(256, C4), "xs": _sb(256, U8), "pq": _sb(256, C4), "ps": _sb(256, U8),
     "wq": _sb(128, C4), "ws": _sb(128, U8), "eq": _sb(512, C4), "es": _sb(512, U8),
     "win": _sb(NW, C4), "wins": _sb(NW, U8), "oq": _sb(64, C4), "osc2": _sb(64, U8),
-    "ej": _sb(129), "jr": _sb(1024), "pi": _sb(8, I32), "pc": _sb(28), "neg": _sb(NI), "zero": _sb(32), "minus": _sb(32),
-    "tb1": _sb(128), "k1": _sb(32), "kp": _sb(32), "kx": _sb(96), "mk": _sb(33), "dm": _sb(32), "rk": _sb(97), "keep": _sb(48),
+    "ej": _sb(129), "jr": _sb(1024), "pi": _sb(8, I32), "pc": _sb(28), "neg": _sb(NI), "zero": _sb(32),
+    "cf": _sb(128), "cg": _sb(128), "kp": _sb(32), "kx": _sb(96), "kl": _sb(65), "kw": _sb(64), "mk": _sb(34), "mi": _sb(34),
+    "dm": _sb(32), "keep": _sb(48), "rnd": _sb(6), "irow": _sb(48), "tmp": _sb(120),
     "dx": _sb(1024), "dw": _sb(4 * (NI + 2 * NC)), "xg": _sb(32), "ct": _sb(512, BF),
     "vw0": _sb(NI + 2 * NC), "vw1": _sb(NI + 2 * NC), "cpw": _sb(NI + NC),
     "yw": _sb(NW), "yf": _sb(NI), "v0": _sb(NI), "v1": _sb(NI),
-    "pm": _sb(2 * NI + 2), "m2": _sb(2 * NI), "mr": _sb(64), "pen": _sb(4),
+    "pm": _sb(2 * NI + 2), "m2": _sb(2 * W2),
     "junk": _sb(2 * NI), "goal": _sb(2), "gid": _sb(2),
-    "srow": _sb(2 * NI), "bb": _sb(64), "tr": _sb(64), "th": _sb(128), "a1": _sb(128), "qr": _sb(2),
-    "w1": _sb(128), "w1t": _sb(128), "xx": _sb(72), "sb": _sb(36), "sg": _sb(36), "br": _sb(32), "gf": _sb(32), "gr": _sb(32),
-    "cap": _sb(64), "d2": _sb(32), "a2": _sb(98 * R), "r2": _sb(97), "kt": _sb(64), "pk": _sb(64), "mm": _sb(64), "bm": _sb(64), "tm": _sb(64),
-    "g16": _sb(2, U16), "sm": _sb(8), "lk": _sb(32), "w2": _sb(128), "w2t": _sb(128), "u2": _sb(4),
+    "srow": _sb(2 * NI), "bb0": _sb(99), "bb1": _sb(91), "tr": _sb(128), "a1": _sb(240),
+    "eb": _sb(240), "w1": _sb(240), "w1t": _sb(128), "xx": _sb(154), "sb": _sb(77), "sg": _sb(6), "br": _sb(32),
+    "a2a": _sb(169), "a2b": _sb(137), "nb": _sb(56), "rb": _sb(81), "rt": _sb(81), "rx": _sb(120), "kt": _sb(128),
+    "pk": _sb(56), "pkt": _sb(32),
+    "g16": _sb(2, U16), "sm": _sb(8), "lk": _sb(33), "w2": _sb(64), "w2t": _sb(128), "u2": _sb(4),
     "l2": _sb(4, U16), "idg": _sb(32), "eh": _sb(2 * NC), "cpx": _sb(2 * NC), "cpc": _sb(10), "cpb": _sb(64), "cpt": _sb(64),
-    "best": _sb(80), "t3": _sb(64), "d3": _sb(64), "a3": _sb(132), "od": _sb(132), "cn": _sb(132), "mw": _sb(16), "wn": _sb(16),
-    "tag": _sb(2 * R + 2), "price": _sb(R + 1), "bk": _sb(8 * R), "mb": _sb(64), "mbt": _sb(64),
+    "best": _sb(80), "t3": _sb(64), "a3": _sb(8 * GAP), "od": _sb(134), "cn": _sb(134 * R), "mw": _sb(16),
+    "price": _sb(R + 1), "bk": _sb(8 * R), "mbt": _sb(64),
     "x3": _sb(192), "lst": _sb(12 * R, U16),
     "hb": _sb(8 * R), "hc": _sb(I, C4), "hs": _sb(4 * I, U8),
     "p_s": ("psum", [128, 1024], F), "p_d": ("psum", [128, 2048], F), "p_y": ("psum", [128, 512], F),
@@ -60,23 +68,22 @@ A = AluOpType
 ACT = ActivationFunctionType
 CYCLE, COPY, SEND, SLOW, WAY = 0.00095, 1.8, 0.5, 0.015, {"i": 6.0, "a": 4.7, "b": 4.9}
 ORDER = """
-0 2 3 1 4 45 44 40 41 5 42 43 6 48 52 46 7 51 49 8 53 50 55 56 57 61 62 65 54 66 10 25 21 68 26 11 22 27 23 28 24 80 30 14 12 9
-15 58 16 17 18 19 59 20 72 60 29 73 63 31 64 74 76 33 70 32 35 79 37 67 34 75 69 81 36 71 85 38 82 95 88 89 83 91 98 94 197 84
-198 99 97 90 47 93 92 77 13 86 39 100 101 110 104 111 112 113 106 116 119 120 114 121 117 123' 122 118 128' 115 124 129 125' 105
-130' 107 126 127 131 132 102 108 103 133 134 135 136' 196 137' 140 138' 139' 141 142' 144 143 195 147 148 149 145 152 146 151
-150 153 158 154 160 155 156 162 161 109 157 163 164 166 169 170 159 165 168 171 172 167 174 173 176 175 78 178 190 177 179' 96
-181' 180 182 183 184' 185 186 187 192 188 193 87 189 199' 201 200 194' 191 202 216 203 220 204 217 222' 218 221 219 225 226 229
-224 227 223 258 230 231 205' 228 232 206 207 254 208 213 235 209 237 239 236 238 211 241 243 244 256 240 242 210 212 252' 233
-264 253 262 265 270 274 260 271 266 214 275 267 276 277 255 268 279' 272 278 248 284' 273 280 261 285 281' 259 269' 286' 263 282
-249 283 287 288 289 291 234 290 292' 245 293' 351' 294 257' 250 296' 295 297 298' 246' 215 300 299 305 303 304 302 301 307 314
-308 306 309 316' 319 310 312 311 320 317 315 313 318 321 324 329 325 322 328 331 326 327 330 333 251 323 334 352 338 332 349 335
-337' 336 340 341 339' 343 353 342 344 345 346 347 350 354 360 369 373 370 372 375 376 377 371' 374 379 358 378 382 383 380 384
-361 381 359 385 362 348 356 355 388 363 357 411 397 407 392 389 390 391 365 408 396 394 395 393 364 247 366 406 405' 386 416 417
-422 426 418 423 419 409 428 427 401 429 420 436 424 413 421 431' 430 402' 432 437 433' 425 438' 435 434 439 440 415 441 410 443
-367 444' 442 446 445' 449' 448' 368 398 387 447 450 403 451 452 412' 404 454 456 453 457 455 458 460 465 468 459 461 463 469 462
-467 399 464 470 471 474 497 466 475 472 498 473 476 477 414 479 481 400 478 480 482 483' 484 486' 487 485 488 489' 490 495 491
-492 493 496 501 505 502 504 506 507' 511 503 510 514 508 509 494 515 512 499 528 516 513 517 518 532 533 519 529 521 530 534 531
-500 535 523 520 522 526 525 527 524 536' 537 538 539 543' 540 545' 541 544 542
+47 3 7 5 0 6 65 44 92 97 4 45 98 73 41 2 87 40 101 42 43 10 1 24 46 50 15 9 67 29 69 21 99 68 74 18 17 70 83 11 12 13 71 16 72
+19 93 22 76 20 37 27 31 77 106 49 95 23 66 61 82 78 96 53 25 28 91 100 54 26 62 102 51 55 75 84 30 86 94 79 88 63 81 33 89 85
+133 143 64 134 144 145 146 151 38 32 152 153 154 35 155 157 90 147 159 57 149 148 156 160 150 80 158 161 162 163 164 165 166
+168' 171' 36 103 34 167 172 169' 170 173 174 178 177 183 180 179 175 176' 181 182 196 184 185 186 189 190 187 191 192 188 193
+194 198 197 139 141 142 201 140 137 135 138 136 199 203 202 200 204 205 206 207 208 218 8 113 117 217' 107 128 60 52 112 111
+104 130 48 59 110 118 123 116 56 132 119 120 131 122 109 14 129 219 114' 58 220 121 115' 125 124 108 221 39 195 209 210 212 213
+105 211 222 223 226 237 236 238 240 244 239 224 241 243 242 246 245 227 225 228 233 248 231 250 252 251 249 229 255 256 254 253
+230 261 262 263 232 265' 257 258 266 277 271 269 278 259 282 281 284 279 280 287 288 283 285 273 292 294 289 290 291 286 293
+295 296 297 298 276 299 300 301 275 267 302 304' 303 308 306 307' 305' 309 310 312 311 315 313 314 320 321 316 318 323 335 322
+324 328 319 325 329 330 326 331 332 333 270 272 317 336 337 338 327 339 340 342' 343 341 274 268 344 345' 346 347 260 264 334
+348 349 350 353 351 247' 354 126 352 358 356 355 369 372 370 360 373 371 375 374 376 377 378 357 359 361 404 379 362 381 365
+383 384 382 394 390 385 363 387 405 386 389 388 364 366 399 400 406 402 403 395 401 398' 391 409 413 414 410 416 411 412 417
+415 419 392 424 420 426 418 396 407 421 422 423 425 427 428 429 430 431 432 433 434 436' 435 437' 438' 440 439 441 408 442 443
+446 444' 447 450 451 448 445 453 452 454 462 455 456 464 457 459 460 458 449 463 467 466 465 469 470 472 468' 471 473 474 393
+397 461 475 478 479 127 214 215 216' 234 235 367 368' 476 477 480 380 482 483 484 485 488 487 486 490 489 491 502 492 493 497
+494 495 506 507 496 503 499 501 504 481 508 509 500 505 498 510' 511 512 513' 516' 517' 519 514 515 518'
 """
 
 
@@ -142,6 +149,8 @@ def _ap(T, v):
     if v[0] == "ind":
         return _ap(T, v[1]).indirect(_ap(T, v[2]))
     n, c0, c1, s, p0, p1 = v
+    if s < 0:
+        return T[n][p0:p1, c1 - 1:c0 - 1:s] if c0 else T[n][p0:p1, c1 - 1::s]
     return T[n][p0:p1, c0:c1] if s == 1 else T[n][p0:p1, c0:c1:s]
 
 
@@ -204,7 +213,7 @@ def rank_program(g, core, T, topo):
     def meet(a, b):
         if a[5] <= b[4] or b[5] <= a[4] or a[2] <= b[1] or b[2] <= a[1]:
             return False
-        return (a[3] == 1 and b[3] == 1) or bool(set(range(a[1], a[2], a[3])) & set(range(b[1], b[2], b[3])))
+        return (abs(a[3]) == 1 and abs(b[3]) == 1) or bool(set(range(a[1], a[2], abs(a[3]))) & set(range(b[1], b[2], abs(b[3]))))
 
     def put(ways, reads, writes, late=0.0, after=(), sem=None):
         deps, k = set(after), len(calls)
@@ -217,11 +226,11 @@ def rank_program(g, core, T, topo):
         for vs, w in ((flat(reads), False), (flat(writes), True)):
             for v in vs:
                 log.setdefault(v[0], []).append((v, w, k, mine))
-        calls.append({"ways": ways, "deps": sorted(deps), "late": late, "sem": sem})
+        calls.append({"ways": ways, "deps": sorted(deps), "late": late, "sem": sem, "name": (flat(writes) + flat(reads) + [("-", 0)])[0][:2]})
         return k
 
     def width(v):
-        return 16 * (v[2][2] - v[2][1]) if v[0] == "ind" else len(range(v[1], v[2], v[3]))
+        return 16 * (v[2][2] - v[2][1]) if v[0] == "ind" else len(range(v[1], v[2], abs(v[3])))
 
     def time(a, per=1.0):
         return 0.07 + 1.56 * width(a) * CYCLE if a[0] == "ind" else max(64, per * width(a)) * CYCLE
@@ -281,8 +290,8 @@ def rank_program(g, core, T, topo):
             ways = [act_(out, a, f, scale=scale, bias=bias), ts_(out, a, scale, A.mult, bias, A.add)]
         put(ways, [a, scale, bias], [out])
 
-    def red(out, a, o):
-        way = ("v", time(a), lambda: g.vector.tensor_reduce(x(out), x(a), AxisListType.X, o))
+    def red(out, a, o, **kw):
+        way = ("v", time(a), lambda: g.vector.tensor_reduce(x(out), x(a), AxisListType.X, o, **kw))
         if o == A.add:
             put([act_(a, a, ACT.Identity, out), way], [a], [out, a])
         else:
@@ -299,7 +308,7 @@ def rank_program(g, core, T, topo):
         else:
             op("g", lambda: g.iota(x(out), pat, base, cm), out, [], held)
 
-    ndma, sent, went = [0], [0], []
+    ndma, sent, went, stored = [0], [0], [], []
 
     def dma(q, out, a, after=()):
         ins = [a] if isinstance(a, tuple) else []
@@ -313,7 +322,7 @@ def rank_program(g, core, T, topo):
         mine = [w for w in _routes(T, topo, rank, stage) if w[0] == core]
         sent[0] += sum(_bits(w[3]) for w in mine)
         went.append(put([("g", SEND, lambda: _calls(g, T, topo, rank, stage, mine))], [_places(rank, stage, w[2])[1] for w in mine], [],
-                        after=went, sem=("loc", None)))
+                        after=went + stored, sem=("loc", None)))
         return went[-1]
 
     def arrive(stage, k):
@@ -357,68 +366,102 @@ def rank_program(g, core, T, topo):
     for b in range(4):
         mm(V("p_d", 512 * b, 512 * b + 256), "eq", "es", 128 * b, "xq", "xs", 0, 256)
         act(V("dx", b, 1024, 4), V("p_d", 512 * b, 512 * b + 256), ACT.Identity, scale=0.5)
-    dma("y", V("wt", 0, 512), T.w[:, :], [items])
-    LANE, QUAD, L16, L4, L8, ID, ID4, KEY, TMP, THR, TWO, LESS = 0, 1, 2, 3, 4, 6, 8, 10, 12, 20, 22, 24
+    stored.append(dma("y", V("wt", 0, 512), T.w[:, :], [items]))
+    LANE, QUAD, L16, L4, L8, ID, ID4, IDU, TMP, THR, TWO, LESS = 0, 1, 2, 3, 4, 6, 8, 10, 12, 20, 22, 24
     ts(c("pi", 1), c("pi", 0), 31, A.bitwise_and)
     ts(c("pi", 2), c("pi", 0), 5, A.logical_shift_right)
     ts(c("pi", 3), c("pi", 0), 15, A.bitwise_and)
     ts(c("pi", 4), c("pi", 0), 3, A.bitwise_and)
     ts(c("pi", 6), c("pi", 0), 8.0, A.add)
+    ts(c("pi", 5), c("pi", 6), 15, A.bitwise_and)
+    cp(V("pc", 0, 5), V("pi", 1, 6), 0)
     fill(V("neg", 0, NI), -BIG)
     fill(V("zero", 0, 32), 0.0)
-    fill(V("minus", 0, 32), -1.0)
-    ts(c("pi", 5), c("pi", 6), 15, A.bitwise_and)
-    fill(V("tb1", 32, 64), 1.0)
-    fill(V("tb1", 64, 96), 1.0 - 0.5 / WHOLE)
-    cp(V("pc", 0, 5), V("pi", 1, 6), 0)
     fill(V("pm", 0, 2 * NI + 2, NI + 1), -BIG)
-    ts(V("d2", 0, 32), V("ej", 0, 32), c("pc", LANE), A.is_lt, -0.5 / WHOLE, A.mult)
-    for o in (V("tb1", 0, 32), V("tb1", 96, 128)):
-        ts(o, V("d2", 0, 32), 1.0, A.add)
-    tb3 = V("tb1", 0, 32)
     slot0 = K * (rank % 4) + (8 if rank < 4 else 0)
-    ts(c("pc", TMP), c("pc", QUAD), 6.0, A.mult)
-    ts(c("pc", ID), c("pc", QUAD), 64.0, A.mult, c("pc", LANE), A.add)
-    ts(c("pc", TMP + 1), c("pc", QUAD), 48.0, A.mult, c("pc", LANE), A.add)
-    ts(c("pc", TMP + 2), c("pc", LANE), 7.5, A.is_lt, -1000.0, A.mult)
-    ts(c("pc", TMP + 3), c("pc", LANE), 23.5, A.is_gt, -1000.0, A.mult)
-    ts(V("br", 0, 32), V("ej", 0, 32), c("pc", TMP), A.subtract)
-    ts(c("pc", ID + 1), c("pc", ID), 32.0, A.add)
-    ts(c("pc", TMP + 4), c("pc", TMP + 1), -8.0, A.add, c("pc", TMP + 2), A.add)
-    ts(c("pc", TMP + 5), c("pc", TMP + 1), 24.0, A.add, c("pc", TMP + 3), A.add)
-    ts(V("gr", 0, 32), V("br", 0, 32), 5.5, A.is_gt, -1000.0, A.mult)
-    fill(V("xx", 8, 72), 0.0)
-    ts(V("pc", KEY, KEY + 2), V("pc", TMP + 4, TMP + 6), WHOLE, A.add, -FAR, A.mult)
-    tt(V("k1", 0, 32), V("br", 0, 32), V("gr", 0, 32), A.add)
-    fill(V("kp", 0, 32), -1.0)
-    fill(V("ct", 32, 512), 0.0)
-    ts(V("kp", slot0, slot0 + K), V("ej", 0, K), -1.0, A.mult, K - 1.0, A.add)
-    fill(V("a2", 0, 98 * R), 0.0)
-    fill(V("rk", 0, 97), 1.0)
-    fill(c("rk", 33), 1.0 / UNIT)
+    lin(c("pc", TMP), c("pc", QUAD), 6.0)
+    lin(c("pc", ID), c("pc", QUAD), 64.0, c("pc", LANE))
+    lin(c("pc", TMP + 1), c("pc", QUAD), 48.0, c("pc", LANE))
+    lin(c("pc", TMP + 2), c("pc", QUAD), 48.0)
+    lin(c("pc", TMP + 3), c("pc", LANE), -1.0, 32.0)
+    lin(c("pc", ID + 1), c("pc", ID), None, 32.0)
+    lin(V("pc", ID4, ID4 + 2), V("pc", ID, ID + 2), 4.0)
+    lin(V("pc", IDU, IDU + 2), V("pc", ID, ID + 2), U)
+    lin(V("pc", TWO, TWO + 2), V("ej", 0, 2), NI * GID * U)
     fill(c("pc", LESS), -NIL)
-    for t in range(R):
-        fill(c("a2", 98 * t + 65), (NI + NC * t + K * rank - 0.5) / UNIT)
-    fill(c("rk", 65), -CAP)
-    ts(V("pc", TWO, TWO + 2), V("ej", 0, 2), NI * GID, A.mult)
-    ts(V("mk", 1, 33), V("kx", 64, 96), c("pc", L8), A.not_equal, OFF, A.mult)
-    fill(c("mk", 0), 0.0)
-    fill(V("od", 0, 132), BIG)
-    fill(V("keep", 0, 48), 1.0)
-    for t in range(R):
-        fill(V("land%d" % t, 64, 320), -BIG)
+    fill(c("pc", THR), -HELD / 10)
+    fill(V("cg", 0, 128), 1.0)
+    ts(V("tmp", 0, 33), V("ej", 0, 33), c("pc", TMP + 3), A.is_equal, -STEP, A.mult)
+    lin(V("cg", 64, 97), V("tmp", 0, 33), None, 1.0)
+    lin(V("cf", 0, 128), V("cg", 0, 128), -1.0)
+    fill(V("m2", 0, 2 * W2), 0.0)
+    fill(V("m2", NI + 1, 2 * W2, W2), -NIL)
+    ts(V("tmp", 33, 57), V("ej", 0, 24), c("pc", TMP), A.subtract)
+    ts(V("tmp", 57, 81), V("tmp", 33, 57), -1.5, A.is_gt, H, A.mult)
+    ts(V("tmp", 81, 105), V("tmp", 33, 57), 4.5, A.is_gt, -H, A.mult)
+    tt(V("tmp", 57, 81), V("tmp", 57, 81), V("tmp", 81, 105), A.add)
+    ts(V("tmp", 81, 105), V("tmp", 33, 57), 5.0, A.is_equal, -6 * H, A.mult)
+    tt(V("a1", 64, 88, -1), V("tmp", 57, 81), V("tmp", 81, 105), A.add)
+    fill(V("a1", 89, 96), 0.0)
+    ts(c("tmp", 105), c("pc", QUAD), 0.5, A.is_lt, H, A.mult)
+    lin(c("a1", 88), c("tmp", 105), None, -OUT * H)
+    ts(V("tmp", 81, 105), V("tmp", 33, 57), 5.0, A.is_equal, (OUT - 5.5) * H, A.mult)
+    tt(V("tmp", 57, 81), V("tmp", 57, 81), V("tmp", 81, 105), A.add)
+    ts(V("tmp", 81, 105), V("tmp", 33, 57), -1.0, A.is_equal, -(OUT + 1) * H, A.mult)
+    tt(V("a1", 96, 120, -1), V("tmp", 57, 81), V("tmp", 81, 105), A.add)
+    cp(V("a1", 184, 240), V("a1", 64, 120))
     for h in range(2):
-        tt(V("a3", 66 * h + 33, 66 * h + 65), V("mk", 1, 33), V("mk", 0, 32), A.subtract)
+        fill(V("eb", 120 * h, 120 * h + 96), BIG)
+    fill(V("xx", 8, 154), 0.0)
+    fill(V("xx", 9, 13, 2), BIG)
+    fill(V("rnd", 0, 4), 0.0)
+    fill(c("rnd", 4), WHOLE * GID * U)
+    fill(c("rnd", 5), -WHOLE * GID * U)
+    lin(c("pc", TMP + 4), c("pc", TMP + 2), None, -0.5)
+    ts(V("irow", 0, NC), V("ej", 0, NC), c("pc", TMP + 4), A.add, -FALL, A.mult)
+    lin(c("pc", TMP + 5), c("pc", TMP + 2), RISE, OUT * H - RISE)
+    fill(V("rb", 73, 81), -BIG)
+    fill(V("rt", 73, 81), -BIG)
+    fill(V("a2a", 64, 96), 0.0)
+    fill(V("a2a", 96 - K - slot0, 95 - slot0), -H)
+    fill(c("a2a", 95 - slot0), -26.5 * H)
+    back = slot0 + K < 32
+    fill(c("a2a", 95 - K - slot0) if back else c("tmp", 119), 32 * H)
+    fill(c("kl", 0), 0.0)
+    ts(V("kl", 1, 65), V("kx", 0, 64), 0.0, A.max, 1.0, A.add)
+    tt(V("kw", 0, 64), V("kl", 1, 65), V("kl", 0, 64), A.subtract)
+    lin(V("a2a", 0, 63, -1), V("kw", 1, 64), H)
+    fill(c("a2a", 63), (K + 31.5 - (32 if back else 0)) * H)
+    lin(V("a2b", 0, 64, -1), V("kw", 0, 64), H)
+    lin(V("kw", 0, 64), V("kx", 0, 64), -H, (5.5 - OUT) * H)
+    fill(V("kp", 0, 32), BIG)
+    lin(V("kp", slot0, slot0 + K), V("ej", 0, K), H, (0.5 - OUT) * H)
+    fill(V("ct", 32, 512), 0.0)
+    fill(V("od", 0, 118), 0.0)
+    for h in range(2):
+        fill(V("od", 59 * h, 59 * h + I), 0.5 ** (M + 1))
+    fill(V("od", 24, 118, 59), -0.5 ** M)
+    fill(V("od", 25, 118, 59), -BIG)
+    fill(V("a3", 24, 118, 59), -1.0)
+    fill(V("a3", 25, 118, 59), -2.0 ** M)
+    lin(c("od", 26), c("pc", TMP + 1), H, (LIFT - 8 - 1 / TAG) * H)
+    lin(c("od", 85), c("pc", TMP + 1), H, (LIFT + 24 - 1 / TAG) * H)
+    fill(V("best", 32, 40), -1.0)
+    fill(V("mi", 0, 34, 33), 1.0)
+    ts(V("mk", 1, 33), V("kx", 64, 96), c("pc", L8), A.is_equal, DIM, A.max)
+    ts(V("tmp", 0, 32), V("kx", 64, 96), c("pc", L8), A.not_equal, 1 / DIM, A.mult)
+    ts(V("mi", 1, 33), V("tmp", 0, 32), 1.0, A.max)
+    tt(V("a3", 27, 59), V("mk", 1, 33), V("mi", 0, 32), A.mult)
+    tt(V("a3", 86, 118), V("mk", 1, 33, -1), V("mi", 2, 34, -1), A.mult)
+    fill(V("keep", 0, 48), 1.0)
     fill(V("keep", 0, 48, 16), 0.0)
-    ts(V("mk", 1, 33), V("mk", 1, 33), BIG / OFF, A.mult)
+    for t in range(R):
+        fill(V("land%d" % t, 64, 256), -BIG)
     ts(V("dm", 0, 16), V("ej", 0, 16), c("pc", L16), A.is_equal, 4.0, A.mult)
     ts(V("dm", 16, 32), V("ej", 0, 16), c("pc", L16), A.is_equal)
-    ts(V("pc", ID4, ID4 + 2), V("pc", ID, ID + 2), 4.0, A.mult)
-    ts(V("tag", 0, 2), V("pc", TMP + 4, TMP + 6), -1.0 / TAG, A.add, -1.0 / UNIT, A.mult)
     fill(c("price", 0), 0.0)
     fill(V("cpw", 0, NI), 0.0)
     fill(V("eh", 0, 2 * NC), 0.0)
-    fill(c("pc", THR), -HELD / 10)
     own_h, own_p = rank % 2, 32 * (rank // 2) + (0 if rank % 2 else 8)
 
     P1 = NI + 1
@@ -430,12 +473,12 @@ def rank_program(g, core, T, topo):
         new = NI if t == 0 else NC
         lst = V("lst", 12 * (t - 1), 12 * t)
         vv = [V("p_s", 512 * h, 512 * h + NI) if t == 0 else V("v%d" % h, 0, NI) for h in range(2)]
-        base = wn + K * rank + K - 1
         for h in range(2):
             if t == 0:
                 mm(vv[h], "pq", "ps", 128 * h, "win", "wins", lo, n)
             else:
-                cp(vv[h], ind(V("vw%d" % h, 0, wn), lst))
+                for j0, j1 in CUTS[h]:
+                    cp(V("v%d" % h, 16 * j0, 16 * j1), ind(V("vw%d" % h, 0, wn), V("lst", 12 * (t - 1) + j0, 12 * (t - 1) + j1)))
         for b in range(4):
             mm(V("p_d", 512 * b, 512 * b + n), "eq", "es", 128 * b, "win", "wins", lo, n)
             lin(V("dw", 4 * (wn - new) + b, 4 * wn, 4), V("p_d", 512 * b + n - new, 512 * b + n), 0.5)
@@ -446,79 +489,81 @@ def rank_program(g, core, T, topo):
         for h in range(2):
             scan(V("pm", P1 * h + 1, P1 * h + P1), vv[h], V("neg", 0, NI), -BIG, A.max, A.max)
         for h in range(2):
-            scan(V("m2", NI * h, NI * h + NI), vv[h], V("pm", P1 * h, P1 * h + NI), -BIG, A.max, A.min)
+            scan(V("m2", W2 * h, W2 * h + NI), vv[h], V("pm", P1 * h, P1 * h + NI), -BIG, A.max, A.min)
         m1 = [c("pm", P1 * h + NI) for h in range(2)]
         for h in range(2):
-            act(V("junk", NI * h, NI * h + NI), V("pm", P1 * h + 1, P1 * h + P1), ACT.Sign, c("goal", h), scale=-1.0, bias=m1[h])
-            lin(c("gid", h), c("goal", h), GID, c("pc", ID + h))
             if t > 0:
-                act(c("pen", h), m1[h], ACT.Relu, scale=4.0, bias=c("pc", THR))
-                lin(h32("mr", h), V("minus", 0, 32), c("pen", h), m1[h])
-            else:
-                lin(h32("mr", h), V("zero", 0, 32), None, m1[h])
-        for h in range(2):
-            ts(h32("bb", h), h32("mr", h), c("m2", NI * h + NI - 1), A.subtract, NIL, A.add)
-        turn(V("tr", 0, 64), V("bb", 0, 64))
-        for h in range(2):
-            lin(V("th", 64 * h, 64 * h + 64), V("tb1", 64 * h, 64 * h + 64), c("bb", 32 * h))
-            tt(V("a1", 64 * h, 64 * h + 64), V("tr", 0, 64), V("th", 64 * h, 64 * h + 64), A.is_gt)
-            red(c("qr", h), V("a1", 64 * h, 64 * h + 64), A.add)
-            ts(h32("w1", h), V("k1", 0, 32), c("qr", h), A.is_equal, c("bb", 32 * h), A.mult)
-            ts(h32("w1", 2 + h), V("k1", 0, 32), c("qr", h), A.is_equal, c("gid", h), A.mult)
+                act(c("m2", W2 * h + NI), m1[h], ACT.Relu, scale=4.0, bias=c("pc", THR))
+            act(V("junk", NI * h, NI * h + NI), V("pm", P1 * h + 1, P1 * h + P1), ACT.Sign, c("goal", h), scale=-1.0, bias=m1[h])
+            lin(c("gid", h), c("goal", h), GID * U, c("pc", IDU + h))
+        scan(V("bb0", 32, 99, -1), V("m2", NI - 1, NI + 66), V("cf", 29, 96), m1[0], A.subtract, A.mult)
+        scan(V("bb1", 0, 67, -1), V("m2", W2 + NI - 1, W2 + NI + 66), V("cf", 61, 128), m1[1], A.subtract, A.mult)
+        turn(V("tr", 32, 96), V("bb0", 32, 96))
         for j in range(2):
-            turn(V("w1t", 64 * j, 64 * j + 64), V("w1", 64 * j, 64 * j + 64))
-            red(c("xx", j), V("w1t", 64 * j, 64 * j + 64), A.add)
+            turn(h32("tr", 3 * j), h32("bb1", j))
+        for h in range(2):
+            lin(V("eb", 120 * h + 96, 120 * h + 120), V("cg", 0, I), c("bb%d" % h, 63))
+            ts(V("a1", 120 * h, 120 * h + 64), V("tr", 64 * h, 64 * h + 64), c("bb%d" % h, 63), A.is_ge, H, A.mult)
+        for h in range(2):
+            scan(V("w1", 120 * h, 120 * h + 120, -1), V("a1", 120 * h, 120 * h + 120), V("eb", 120 * h, 120 * h + 120), c("gid", h), A.add, A.min)
+        turn(V("w1t", 32, 96), V("w1", 0, 64))
+        for j in range(2):
+            turn(h32("w1t", 3 * j), V("w1", 120 + 32 * j, 152 + 32 * j))
+        red(c("xx", 0), V("w1t", 0, 64), A.max)
+        red(c("xx", 1), V("w1t", 64, 128), A.min, apply_absolute_value=True)
         for d in range(2):
             cp(V("xx", 2, 4, 1, 64 * d, 64 * d + 64), V("xx", 0, 2, 1, 64 - 64 * d, 128 - 64 * d))
         for d in range(4):
             cp(V("xx", 4, 8, 1, 32 * d, 32 * d + 32), V("xx", 0, 4, 1, 32 * (d ^ 1), 32 * (d ^ 1) + 32))
-        scan(V("sb", 0, 36), V("xx", 0, 72, 2), V("neg", 0, 36), 0.0, A.add, A.max)
-        scan(V("sg", 0, 36), V("xx", 1, 72, 2), V("neg", 0, 36), 0.0, A.add, A.max)
-        turn(V("br", 0, 32), V("sb", 4, 36))
-        lin(V("d2", 0, 32), tb3, c("sb", 4))
-        turn(V("gf", 0, 32), V("sg", 4, 36))
-        lin(c("sm", 0), c("sg", 4), -1.0 / TAG, -(base + B * rank / TAG))
-        nl = 2 if mid else 1
-        a0 = 98 * t
-        ts(V("g16", 0, nl), V("pc", TWO, TWO + nl), c("sg", 4), A.add, 1.0 / GID, A.mult)
-        tt(V("a2", a0, a0 + 32), V("br", 0, 32), V("d2", 0, 32), A.is_gt)
-        lin(V("gr", 0, 32), V("gf", 0, 32), 1.0 / GID, WHOLE)
-        ts(c("a2", a0 + 33), c("g16", 0), GID / TAG, A.mult, c("sm", 0), A.add)
-        if not last:
-            act(c("sm", 7), c("sb", 4), ACT.Relu, bias=c("pc", LESS))
-        for h in range(2):
-            act(h32("mm", h), V("gr", 0, 32), ACT.Abs, scale=FAR, bias=c("pc", KEY + h))
-            tt(h32("cap", h), V("br", 0, 32), h32("mm", h), A.subtract)
+        scan(V("sb", 0, 77, -1), V("xx", 0, 154, 2), V("cg", 19, 96), 0.0, A.max, A.mult)
+        scan(V("sg", 0, 6), V("xx", 1, 13, 2), V("rnd", 0, 6), (NI * GID - B - 1) * U, A.min, A.add)
+        bid, gid, goal = c("sb", 24), c("sg", 3), c("sg", 5)
+        a2, a0 = ("a2b", 64) if t else ("a2a", 96)
+        turn(V("br", 0, 32), V("sb", 0, 32))
+        lin(c("sm", 2), goal, FALL / (GID * U))
+        lin(c(a2, a0 + 24), goal, -RISE / (GID * U), c("pc", TMP + 5))
+        lin(c("sm", 0), goal, -1.0, gid)
         if t > 0:
+            nl = 2 if mid else 1
+            ts(V("g16", 0, nl), V("pc", TWO, TWO + nl), goal, A.add, 1.0 / (GID * U), A.mult)
             tt(V("lk", 0, 16 * nl), ind(V("srow", 0, NI * nl), V("g16", 0, nl)), V("dm", 0, 16 * nl), A.mult)
             red(c("sm", 4), V("lk", 0, 16), A.add)
         else:
-            ts(c("sm", 4), c("g16", 0), 4.0, A.mult)
+            lin(c("sm", 4), goal, 4.0 / (GID * U))
+            lin(V("nb", 0, 56), V("sb", 0, 56), -1.0)
         if mid:
-            red(c("sm", 5), V("lk", 16, 32), A.add)
-            lin(c("sm", 6), c("sm", 5), None, c("sm", 7))
-        lin(c("sm", 3), c("a2", a0 + 33), -4 * TAG, -4 * (base * TAG + B * rank))
-        scan(V("r2", 0, 97), V("a2", a0, a0 + 97), V("rk", 0, 97), 0.0, A.add, A.mult)
-        r2 = c("r2", 32)
-        turn(V("kt", 0, 64), V("r2", 33, 97))
+            cp(c("lk", 32), bid)
+            red(c("sm", 6), V("lk", 16, 33), A.add)
+        ts(V(a2, a0, a0 + 24), V("br", 0, 24), bid, A.is_ge, -H, A.mult)
+        ts(V(a2, a0 + 25, a0 + 73), V("irow", 0, NC), c("sm", 2), A.add, RISE, A.min)
+        lin(c("sm", 1), c("sm", 0), H / (TAG * U), (LIFT + wn + K * rank + K - OUT + B * rank / TAG) * H)
+        scan(V("rb", 0, 73), V(a2, a0, a0 + 73), V("sb", 0, 73), (K + 0.5 - OUT) * H, A.add, A.min)
+        scan(V("rt", 0, 73), V(a2, a0, a0 + 73), V("neg", 0, 73), c("sm", 1), A.add, A.max)
+        r2 = c("rb", 23)
         ld, l0 = "land%d" % t, 8 * (N - 1 - rank)
-        if not last:
-            ts(h32("pk", 0), V("kp", 0, 32), r2, A.is_equal, c("sm", 6 if t else 7), A.mult)
-            turn(h32("pk", 1), h32("pk", 0))
-            red(c(ld, l0 + 4), h32("pk", 1), A.add)
-        for h in range(2):
-            tt(h32("tm", h), V("kt", 0, 32), h32("mm", h), A.add)
-            tt(h32("bm", h), h32("cap", h), h32("kt", 1), A.min)
-            red(c(ld, l0 + 2 + h), h32("tm", h), A.min)
-            red(c(ld, l0 + h), h32("bm", h), A.max)
-        bids = send("a%d" % t)
-        for j in range(2):
-            ts(V("w2", 64 * j, 64 * j + 64), V("kx", 0, 64), r2, A.is_equal, c("sm", 3 + j), A.mult)
-            turn(V("w2t", 64 * j, 64 * j + 64), V("w2", 64 * j, 64 * j + 64))
+        if t == 0:
+            scan(V("pk", 0, 56), V(a2, 64, 120, -1), V("nb", 0, 56), 32 * H, A.add, A.max)
+            turn(V("pkt", 0, 32), V("pk", 24, 56))
+            red(c(ld, l0 + 4), V("pkt", 0, 32), A.min, negate=True)
+        if mid:
+            ts(V("pk", 24, 56), V("kp", 0, 32), r2, A.is_equal, c("sm", 6), A.mult)
+            turn(V("pkt", 0, 32), V("pk", 24, 56))
+            red(c(ld, l0 + 4), V("pkt", 0, 32), A.add)
+        turn(V("kt", 0, 64), V("rb", 17, 81))
+        turn(V("kt", 64, 128), V("rt", 17, 81))
         for j in range(4):
-            red(c("u2", j), h32("w2t", j), A.add)
+            red(c(ld, l0 + j), V("kt", 32 * j, 32 * j + I), A.max)
+        bids = send("a%d" % t)
+        scan(V("rx", 0, a0 + 24), V(a2, 0, a0 + 24, -1), V("neg", 0, a0 + 24), c("sm", 0), A.add, A.max)
+        ts(V("w2", 0, 64), V("kw", 0, 64), r2, A.is_equal, c("sm", 4), A.mult)
+        turn(V("w2t", 0, 64), V("rx", a0 - 40, a0 + 24))
+        turn(V("w2t", 64, 128), V("w2", 0, 64))
         for j in range(2):
-            ts(V("l2", 2 * j, 2 * j + 2), V("u2", 2 * j, 2 * j + 2), c("pc", L4), A.add)
+            red(c("u2", j), V("w2t", 32 * j, 32 * j + I), A.min, apply_absolute_value=True)
+        for j in range(2, 4):
+            red(c("u2", j), V("w2t", 32 * j, 32 * j + I), A.add)
+        ts(V("l2", 0, 2), V("u2", 0, 2), 4.0 / U, A.mult, c("pc", L4), A.add)
+        ts(V("l2", 2, 4), V("u2", 2, 4), c("pc", L4), A.add)
         cp(V("xg", 0, 32), ind(V("dx", 0, 1024), V("l2", 0, 2)))
         tt(V("ct", 0, 32), ind(V("dw", 0, 4 * wn), V("l2", 2, 4)), V("xg", 0, 32), A.add)
         quant(V("cq%d" % t, 0, 128), V("cs%d" % t, 0, 128), V("ct", 0, 512))
@@ -530,8 +575,6 @@ def rank_program(g, core, T, topo):
             cp(V("yw", 0, NI), V("p_y", 0, NI))
             for h in range(2):
                 cp(V("vw%d" % h, 0, NI), vv[h])
-        for h in range(2):
-            lin(V("od", 66 * h + 33, 66 * h + 65), V("mk", 1, 33), None, c("tag", 2 * t + h))
         if not last:
             cp(V("idg", 0, 32), ind(V("jr", 0, 1024), V("l2", 0, 2)))
             for h in range(2):
@@ -541,7 +584,7 @@ def rank_program(g, core, T, topo):
             for h in range(2):
                 mm(V("p_s", 512 * h, 512 * h + 128), "pq", "ps", 128 * h, "win", "wins", w2 - 128, 128)
             for h in range(2):
-                act(V("cpc", 2 + 4 * h, 6 + 4 * h), V(ld, 36 - 32 * h, 68 - 32 * h, 8), ACT.Identity, c("cpc", h))
+                act(V("cpc", 2 + 4 * h, 6 + 4 * h), V(ld, 36 - 32 * h, 68 - 32 * h, 8), ACT.Relu, c("cpc", h), bias=c("pc", LESS))
                 lin(h32("cpb", h), V("zero", 0, 32), None, c("cpc", h))
             turn(V("cpt", 0, 64), V("cpb", 0, 64))
             for h in range(2):
@@ -551,35 +594,36 @@ def rank_program(g, core, T, topo):
                 cp(V("cpw", wn, w2), V("cpt", 8, 8 + NC))
         mm(V("p_y", 0, 128), "wq", "ws", 0, "win", "wins", w2 - 128, 128)
         cp(V("yw", wn, w2), V("p_y", 128 - NC, 128))
-        bs = [c("best", 40 * h + 8) for h in range(2)]
+        bs = [c("best", 63 - 40 * h) for h in range(2)]
+        c0 = 118 * t
         for h in range(2):
-            scan(V("best", 40 * h, 40 * h + 40), V(ld, h, 320, 8), V("neg", 0, 40), -1.0, A.max, A.max)
-            turn(h32("t3", h), V("best", 40 * h + 8, 40 * h + 40))
-            lin(h32("d3", h), tb3, bs[h])
+            scan(V("best", 40 - 40 * h, 72 - 40 * h, -1), V(ld, h, 256, 8), V("cg", 56 + 8 * h, 88 + 8 * h), -1.0, A.max, A.mult)
+        turn(V("t3", 0, 64), V("best", 0, 64))
+        for h in range(2):
             act(V("mw", 8 * h, 8 * h + 8), V(ld, h, 64, 8), ACT.Sign, scale=-1.0, bias=bs[h])
-        act(V("a3", 32, 132, 66), V("best", 8, 80, 40), ACT.Relu, scale=-OFF)
         for h in range(2):
-            tt(V("a3", 66 * h, 66 * h + 32), h32("t3", h), h32("d3", h), A.is_gt)
-            scan(V("wn", 8 * h, 8 * h + 8), V("mw", 8 * h, 8 * h + 8), V(ld, 2 + h, 64, 8), c("tag", 2 * t + h), A.mult, A.min)
-            scan(V("cn", 66 * h, 66 * h + 65), V("a3", 66 * h, 66 * h + 65), V("od", 66 * h, 66 * h + 65), 0.5 - M, A.add, A.min)
-            ts(h32("mb", h), V("cn", 66 * h + 33, 66 * h + 65), c("wn", 8 * h + 7), A.max, 0.0, A.min)
-        for h in (own_h, 1 - own_h)[:1 if last else 2]:
-            ts(c("tag", 2 * t + 2 + h), c("cn", 66 * h + 32), c("tag", 2 * t + h), A.min, c("wn", 8 * h + 7), A.max)
-        turn(V("mbt", 0, 64), V("mb", 0, 64))
+            ts(V("a3", 59 * h, 59 * h + I), V("t3", 40 - 40 * h, 64 - 40 * h), bs[h], A.is_lt, 0.5, A.max)
+            scan(V("a3", 59 * h + 26, 59 * h + 27 + 7 * GAP, -GAP), V("mw", 8 * h, 8 * h + 8), V(ld, 2 + h, 64, 8), 0.0, A.mult, A.max)
+        for h in range(2):
+            scan(V("cn", c0 + 59 * h, c0 + 59 * h + 59, 1 - 2 * h), V("a3", 59 * h, 59 * h + 59), V("od", 59 * h, 59 * h + 59), 1.0, A.mult, A.max)
+        if not last:
+            cp(V("od", 26, 86, 59), V("cn", c0 + 26, c0 + 92, 65))
+        turn(V("mbt", 0, 64), V("cn", c0 + 27, c0 + 91))
         for a in range(4):
             scan(V("x3", 48 * a, 48 * a + 48, 1, 0, 32), V("keep", 0, 48, 1, 32 * a, 32 * a + 32),
-                 V("mbt", 8, 56, 1, 32 * a, 32 * a + 32), 0.0, A.mult, A.min)
+                 V("mbt", 8, 56, 1, 32 * a, 32 * a + 32), 0.0, A.mult, A.max)
         for d in range(4):
-            ts(V("lst", 12 * t, 12 * t + 12, 1, 32 * d, 32 * d + 32), V("x3", 15, 192, 16, 0, 32), -UNIT, A.mult)
+            ts(V("lst", 12 * t, 12 * t + 12, 1, 32 * d, 32 * d + 32), V("x3", 15, 192, 16, 0, 32), 1.0 / H, A.mult, -LIFT, A.add)
         h, k = own_h, 8 * t
+        tag, sold = c("cn", c0 + 26 + 65 * h), c("cn", c0 + 25 + 67 * h)
         act(c("bk", k), bs[h], ACT.Relu, bias=c("pc", LESS))
-        ts(c("bk", k + 1), c("cn", 66 * h + 32), 0.0, A.is_lt, c("bk", k), A.mult)
+        ts(c("bk", k + 1), sold, 0.75, A.is_gt, c("bk", k), A.mult)
         lin(c("price", t + 1), c("bk", k + 1), None, c("price", t))
-        dma("y", T.pr[t, :], V("price", t + 1, t + 2, 1, own_p, own_p + I))
-        lin(c("bk", k + 2), c("tag", 2 * t + 2 + h), -UNIT, WHOLE)
+        stored.append(dma("y", T.pr[t, :], V("price", t + 1, t + 2, 1, own_p, own_p + I)))
+        lin(c("bk", k + 2), tag, 1.0 / H, WHOLE)
         lin(c("bk", k + 3), c("bk", k + 2), -TAG, TAG * WHOLE)
-        lin(c("bk", k + 4), c("tag", 2 * t + 2 + h), -TAG * UNIT, c("bk", k + 3))
-        dma("y", T.ho[t, :], V("bk", k + 4, k + 5, 1, own_p, own_p + I))
+        lin(c("bk", k + 4), tag, TAG / H, c("bk", k + 3))
+        stored.append(dma("y", T.ho[t, :], V("bk", k + 4, k + 5, 1, own_p, own_p + I)))
 
     l0 = 12 * (R - 1)
     c0 = I * rank // 32 * 2

from concourse.bass import DstId, RemoteDMATransfer
from concourse.mybir import dt, AluOpType, AxisListType, ActivationFunctionType

N, I, B, K, M, R = 8, 24, 256, 6, 6, 3
NI = N * I
NC = N * K
NW = NI + R * NC
BIG = 1.0e29
HELD = 1.0e28
NIL = 2.0 ** -100
H = 2.0 ** 80
OUT = 1024.0
TAG = 4096.0
LIFT = 512.0
GID = 512.0
U = H / 2.0 ** 18
WHOLE = 2.0 ** 23
STEP = 0.5 / WHOLE
DIM = 2.0 ** -20
RISE, FALL = 8 * H, 8192 * H
W2 = NI + 99
GAP = 140
CUTS = (((0, 12),), ((0, 12),))
C4, U8, F, BF, I32, U16 = "float8_e4m3fn_x4", "uint8", "float32", "bfloat16", "int32", "uint16"


def _sb(n, d=F):
    return ("sbuf", [128, n], d)


SCRATCH = {
    "itt": _sb(512, BF), "iq": _sb(128, C4), "isc": _sb(128, U8),
    "xt": _sb(1024, BF), "xp": _sb(1024, BF), "wt": _sb(512, BF), "et": _sb(2048, BF), "ident": _sb(128, BF),
    "xq": _sb(256, C4), "xs": _sb(256, U8), "pq": _sb(256, C4), "ps": _sb(256, U8),
    "wq": _sb(128, C4), "ws": _sb(128, U8), "eq": _sb(512, C4), "es": _sb(512, U8),
    "win": _sb(NW, C4), "wins": _sb(NW, U8), "oq": _sb(64, C4), "osc2": _sb(64, U8),
    "ej": _sb(129), "jr": _sb(1024), "pi": _sb(8, I32), "pc": _sb(28), "neg": _sb(NI), "zero": _sb(32),
    "cf": _sb(128), "cg": _sb(128), "kp": _sb(32), "kx": _sb(96), "kl": _sb(65), "kw": _sb(64), "mk": _sb(34), "mi": _sb(34),
    "dm": _sb(32), "keep": _sb(48), "rnd": _sb(6), "irow": _sb(48), "tmp": _sb(120),
    "dx": _sb(1024), "dw": _sb(4 * (NI + 2 * NC)), "xg": _sb(32), "ct": _sb(512, BF),
    "vw0": _sb(NI + 2 * NC), "vw1": _sb(NI + 2 * NC), "cpw": _sb(NI + NC),
    "yw": _sb(NW), "yf": _sb(NI), "v0": _sb(NI), "v1": _sb(NI),
    "pm": _sb(2 * NI + 2), "m2": _sb(2 * W2),
    "junk": _sb(2 * NI), "goal": _sb(2), "gid": _sb(2),
    "srow": _sb(2 * NI), "bb0": _sb(99), "bb1": _sb(91), "tr": _sb(128), "a1": _sb(240),
    "eb": _sb(240), "w1": _sb(240), "w1t": _sb(128), "xx": _sb(154), "sb": _sb(77), "sg": _sb(6), "br": _sb(32),
    "a2a": _sb(169), "a2b": _sb(137), "nb": _sb(56), "rb": _sb(81), "rt": _sb(81), "rx": _sb(120), "kt": _sb(128),
    "pk": _sb(56), "pkt": _sb(32),
    "g16": _sb(2, U16), "sm": _sb(8), "lk": _sb(33), "w2": _sb(64), "w2t": _sb(128), "u2": _sb(4),
    "l2": _sb(4, U16), "idg": _sb(32), "eh": _sb(2 * NC), "cpx": _sb(2 * NC), "cpc": _sb(10), "cpb": _sb(64), "cpt": _sb(64),
    "best": _sb(80), "t3": _sb(64), "a3": _sb(8 * GAP), "od": _sb(134), "cn": _sb(134 * R), "mw": _sb(16),
    "price": _sb(R + 1), "bk": _sb(8 * R), "mbt": _sb(64),
    "x3": _sb(192), "lst": _sb(12 * R, U16),
    "hb": _sb(8 * R), "hc": _sb(I, C4), "hs": _sb(4 * I, U8),
    "p_s": ("psum", [128, 1024], F), "p_d": ("psum", [128, 2048], F), "p_y": ("psum", [128, 512], F),
}
for _t in range(R):
    SCRATCH["land%d" % _t] = _sb(64 + 256)
    SCRATCH["cq%d" % _t] = _sb(128, C4)
    SCRATCH["cs%d" % _t] = _sb(128, U8)
    SCRATCH["hc%d" % _t] = _sb(K, C4)
    SCRATCH["hs%d" % _t] = _sb(4 * K, U8)

STAGES = ["i"] + ["%s%d" % (k, t) for t in range(R) for k in "ab"]
SEMAPHORES = (["sv", "ss", "st", "sg", "loc"] + ["arr_" + s for s in STAGES] + ["hop_" + s for s in STAGES]
              + ["dm%d" % k for k in range(16)])
A = AluOpType
ACT = ActivationFunctionType
CYCLE, COPY, SEND, SLOW, WAY = 0.00095, 1.8, 0.5, 0.015, {"i": 6.0, "a": 4.7, "b": 4.9}
ORDER = """
47 3 7 5 0 6 65 44 92 97 4 45 98 73 41 2 87 40 101 42 43 10 1 24 46 50 15 9 67 29 69 21 99 68 74 18 17 70 83 11 12 13 71 16 72
19 93 22 76 20 37 27 31 77 106 49 95 23 66 61 82 78 96 53 25 28 91 100 54 26 62 102 51 55 75 84 30 86 94 79 88 63 81 33 89 85
133 143 64 134 144 145 146 151 38 32 152 153 154 35 155 157 90 147 159 57 149 148 156 160 150 80 158 161 162 163 164 165 166
168' 171' 36 103 34 167 172 169' 170 173 174 178 177 183 180 179 175 176' 181 182 196 184 185 186 189 190 187 191 192 188 193
194 198 197 139 141 142 201 140 137 135 138 136 199 203 202 200 204 205 206 207 208 218 8 113 117 217' 107 128 60 52 112 111
104 130 48 59 110 118 123 116 56 132 119 120 131 122 109 14 129 219 114' 58 220 121 115' 125 124 108 221 39 195 209 210 212 213
105 211 222 223 226 237 236 238 240 244 239 224 241 243 242 246 245 227 225 228 233 248 231 250 252 251 249 229 255 256 254 253
230 261 262 263 232 265' 257 258 266 277 271 269 278 259 282 281 284 279 280 287 288 283 285 273 292 294 289 290 291 286 293
295 296 297 298 276 299 300 301 275 267 302 304' 303 308 306 307' 305' 309 310 312 311 315 313 314 320 321 316 318 323 335 322
324 328 319 325 329 330 326 331 332 333 270 272 317 336 337 338 327 339 340 342' 343 341 274 268 344 345' 346 347 260 264 334
348 349 350 353 351 247' 354 126 352 358 356 355 369 372 370 360 373 371 375 374 376 377 378 357 359 361 404 379 362 381 365
383 384 382 394 390 385 363 387 405 386 389 388 364 366 399 400 406 402 403 395 401 398' 391 409 413 414 410 416 411 412 417
415 419 392 424 420 426 418 396 407 421 422 423 425 427 428 429 430 431 432 433 434 436' 435 437' 438' 440 439 441 408 442 443
446 444' 447 450 451 448 445 453 452 454 462 455 456 464 457 459 460 458 449 463 467 466 465 469 470 472 468' 471 473 474 393
397 461 475 478 479 127 214 215 216' 234 235 367 368' 476 477 480 380 482 483 484 485 488 487 486 490 489 491 502 492 493 497
494 495 506 507 496 503 499 501 504 481 508 509 500 505 498 510' 511 512 513' 516' 517' 519 514 515 518'
"""


def V(name, c0, c1, step=1, p0=0, p1=128):
    return (name, c0, c1, step, p0, p1)


def _deal(engines, parts):
    n = len(engines) // parts
    return [sum(1 << e for e in engines[n * k:n * k + n]) for k in range(parts)]


def _bits(m):
    return bin(m).count("1")


def _routes(T, topo, r, stage):
    me = T.cores[r]
    others = [T.cores[(r + d) % N] for d in range(1, N)]
    near = [c for c in others if topo.may_write(me, c)]
    far = [c for c in others if not topo.may_write(me, c)]
    mates = sorted([c for c in topo.cores_of(me) if c != me], key=lambda c: topo.die(c) != topo.die(me))
    port = [c for c in mates if all(topo.may_write(c, d) for d in far)]
    spare = [c for c in mates if c not in port][0]
    on = topo.engines(me, port[0])
    off = topo.mask(me, near[0])
    only = [e for e in on if e not in topo.engines(me, near[0])]
    half = len(far) // 2
    if stage[0] == "a":
        hand = [("b", [(spare, near), (port[0], far[:half]), (port[1], far[half:])])]
        out = []
    else:
        hand = [("c", [(port[2], far[:half] + near[:1]), (port[0], far[half:])]),
                ("s", [(port[3], far[:half] + near[:1]), (port[1], far[half:])])]
        out = [(me, near[1:], "c", off, False, 1), (me, [spare], "s", _deal(only, 1)[0], True, 1),
               (spare, near[1:2], "s", off, False, 0), (me, near[2:], "s", off, False, 2)]
    for (k, hs), m in zip(hand, _deal(on, len(hand))):
        out.append((me, [h for h, ds in hs], k, m, True, 0))
        for h, ds in hs:
            out.append((h, ds, k, topo.mask(h, ds[0]), False, 0))
        if k != "b":
            out.append((hs[0][0], [me], k, _deal(only, 2)[0], False, int(stage == "i")))
    return out


def _places(r, stage, kind):
    if stage == "i":
        if kind == "c":
            return V("iq", 0, I), V("iq", 0, I), V("hc", 0, I), V("hc", 0, I), V("win", I * r, I * r + I)
        return V("isc", 0, I), V("isc", 0, 4 * I), V("hs", 0, 4 * I), V("hs", 0, I), V("wins", I * r, I * r + I)
    t = int(stage[1])
    c = NI + NC * t + K * r
    if kind == "b":
        n = 5 if t < R - 1 else 4
        v = V("land%d" % t, 8 * (N - 1 - r), 8 * (N - 1 - r) + n)
        return v, v, V("hb", 8 * t, 8 * t + n), V("hb", 8 * t, 8 * t + n), v
    if kind == "c":
        return V("cq%d" % t, 0, K), V("cq%d" % t, 0, K), V("hc%d" % t, 0, K), V("hc%d" % t, 0, K), V("win", c, c + K)
    return V("cs%d" % t, 0, K), V("cs%d" % t, 0, 4 * K), V("hs%d" % t, 0, 4 * K), V("hs%d" % t, 0, K), V("wins", c, c + K)


def _ap(T, v):
    if v[0] == "ind":
        return _ap(T, v[1]).indirect(_ap(T, v[2]))
    n, c0, c1, s, p0, p1 = v
    if s < 0:
        return T[n][p0:p1, c1 - 1:c0 - 1:s] if c0 else T[n][p0:p1, c1 - 1::s]
    return T[n][p0:p1, c0:c1] if s == 1 else T[n][p0:p1, c0:c1:s]


def _bytes(T, v):
    a = _ap(T, v)
    return a.bitcast(dt.uint8) if SCRATCH[v[0]][2] == C4 else a


def _calls(g, T, topo, r, stage, writes):
    for k in sorted(set(w[5] for w in writes)):
        trs = []
        for src, dsts, kind, m, hop, call in [w for w in writes if w[5] == k]:
            home, hand, held, leave, land = _places(r, stage, kind)
            a, b = (hand, held) if hop else ((home if src == T.cores[r] else leave), land)
            ids = [DstId(rid=topo.addr(d, src)[0], pnc=topo.addr(d, src)[1]) for d in dsts]
            trs.append(RemoteDMATransfer(dst_ids=ids, dma_engine_mask=m, remote_sem=T.sem[("hop_" if hop else "arr_") + stage],
                                         srcs=[_bytes(T, a)], dsts=[_bytes(T, b) for d in dsts]))
        g.remote_dma_fused(trs, local_sem=T.sem.loc)
    return sum(_bits(w[3]) for w in writes)


def _helper(g, core, T, topo):
    owners = [r for r in range(N) if core in topo.cores_of(T.cores[r])]
    if not owners:
        return
    r, sent = owners[0], 0
    for stage in STAGES:
        rt = _routes(T, topo, r, stage)
        mine = [w for w in rt if w[0] == core]
        if mine:
            g.wait_ge(T.sem["hop_" + stage], sum(_bits(w[3]) for w in rt if core in w[1]))
            sent += _calls(g, T, topo, r, stage, mine)
    if sent:
        g.wait_ge(T.sem.loc, sent)


def _place(calls):
    plan = [None] * len(calls)
    for at, word in enumerate(ORDER.split()):
        k = int(word.strip("'"))
        plan[k] = (at, calls[k]["ways"][int(word[-1] == "'")])
    assert all(plan[d][0] < plan[k][0] for k in range(len(calls)) for d in calls[k]["deps"])
    return plan


def rank_program(g, core, T, topo):
    rank = T.rank_of(core)
    if rank is None:
        return _helper(g, core, T, topo)
    Q = {"v": g.vector, "s": g.scalar, "t": g.tensor, "g": g, "y": g.sync}
    calls, log = [], {}

    def flat(vs):
        out = []
        for v in vs:
            if isinstance(v, tuple):
                out += [v[1], v[2]] if v[0] == "ind" else [v]
        return [((v[0], v[1] // 512 * 512, v[1] // 512 * 512 + 512, 1, 0, 128) if SCRATCH[v[0]][0] == "psum" else v) for v in out]

    def meet(a, b):
        if a[5] <= b[4] or b[5] <= a[4] or a[2] <= b[1] or b[2] <= a[1]:
            return False
        return (abs(a[3]) == 1 and abs(b[3]) == 1) or bool(set(range(a[1], a[2], abs(a[3]))) & set(range(b[1], b[2], abs(b[3]))))

    def put(ways, reads, writes, late=0.0, after=(), sem=None):
        deps, k = set(after), len(calls)
        mine = ways[0][0] if len(ways) == 1 else None
        for vs, w in ((flat(reads), False), (flat(writes), True)):
            for v in vs:
                for u, uw, j, uq in log.get(v[0], []):
                    if (w or uw or (SCRATCH[v[0]][0] == "psum" and (uq != mine or mine is None))) and meet(u, v):
                        deps.add(j)
        for vs, w in ((flat(reads), False), (flat(writes), True)):
            for v in vs:
                log.setdefault(v[0], []).append((v, w, k, mine))
        calls.append({"ways": ways, "deps": sorted(deps), "late": late, "sem": sem, "name": (flat(writes) + flat(reads) + [("-", 0)])[0][:2]})
        return k

    def width(v):
        return 16 * (v[2][2] - v[2][1]) if v[0] == "ind" else len(range(v[1], v[2], abs(v[3])))

    def time(a, per=1.0):
        return 0.07 + 1.56 * width(a) * CYCLE if a[0] == "ind" else max(64, per * width(a)) * CYCLE

    def op(q, call, out, ins, held, more=()):
        return put([(q, held, call)], ins, [out] + list(more))

    def x(v):
        return _ap(T, v) if isinstance(v, tuple) else v

    def ts_(out, a, s1, o0, s2=None, o1=None):
        if o1 is None:
            return ("v", time(a), lambda: g.vector.tensor_scalar(x(out), x(a), x(s1), None, o0))
        return ("v", time(a), lambda: g.vector.tensor_scalar(x(out), x(a), x(s1), x(s2), o0, o1))

    def act_(out, a, f, acc=None, **kw):
        def call():
            kx = {k: x(kw[k]) for k in kw}
            if acc is not None:
                kx["accum_out"] = x(acc)
            return g.scalar.activation(x(out), x(a), f, **kx)
        return ("s", time(a) + SLOW + (0.02 if acc else 0.0), call)

    def ts(out, a, s1, o0, s2=None, o1=None):
        put([ts_(out, a, s1, o0, s2, o1)], [a, s1, s2], [out])

    def tt(out, a, b, o):
        per = 1.0 if a[0] != "ind" and SCRATCH[a[0]][0] == "psum" else 2.0
        op("v", lambda: g.vector.tensor_tensor(x(out), x(a), x(b), o), out, [a, b], time(a, per))

    def fill(out, c):
        op("v", lambda: g.vector.memset(x(out), c), out, [], time(out, 0.5 if SCRATCH[out[0]][2] == BF else 1.0))

    def scan(out, a, b, init, o0, o1):
        op("v", lambda: g.vector.tensor_tensor_scan(x(out), x(a), x(b), x(init), o0, o1), out, [a, b, init], time(a))

    def turn(out, a):
        op("v", lambda: g.vector.transpose(x(out), x(a)), out, [a], time(a))

    def quant(q, s, a):
        op("v", lambda: g.vector.quantize_mx(x(q), x(s), x(a)), q, [a], 0.015 + 0.000275 * width(a), [s])

    def act(out, a, f, acc=None, **kw):
        put([act_(out, a, f, acc, **kw)], [a] + list(kw.values()), [out] + ([acc] if acc else []))

    def cp(out, a, side=None):
        ways = [act_(out, a, ACT.Copy), ("v", time(a), lambda: g.vector.tensor_copy(x(out), x(a)))]
        put(ways if side is None else [ways[1 - side]], [a], [out])

    def lin(out, a, scale=None, bias=None):
        f = ACT.Identity if isinstance(bias, tuple) or isinstance(scale, tuple) else ACT.Copy
        if bias is None:
            ways = [act_(out, a, f, scale=scale), ts_(out, a, scale, A.mult)]
        elif scale is None:
            ways = [act_(out, a, f, bias=bias), ts_(out, a, bias, A.add)]
        else:
            ways = [act_(out, a, f, scale=scale, bias=bias), ts_(out, a, scale, A.mult, bias, A.add)]
        put(ways, [a, scale, bias], [out])

    def red(out, a, o, **kw):
        way = ("v", time(a), lambda: g.vector.tensor_reduce(x(out), x(a), AxisListType.X, o, **kw))
        if o == A.add:
            put([act_(a, a, ACT.Identity, out), way], [a], [out, a])
        else:
            put([way], [a], [out])

    def mm(out, lq, ls, l0, rq, rs, r0, n):
        a, b, c, d = V(lq, l0, l0 + 128), V(ls, l0, l0 + 128), V(rq, r0, r0 + n), V(rs, r0, r0 + n)
        op("t", lambda: g.tensor.matmul_mx(x(out), x(a), x(b), x(c), x(d), True, True), out, [a, b, c, d], (n + 16) * 0.6 * CYCLE)

    def iota(out, pat, base, cm, small=True):
        held = 0.13 + 2 * width(out) * CYCLE
        if small:
            op("g", lambda: g.iota(x(out), pat, base, cm, allow_small_or_imprecise_dtypes=True), out, [], held)
        else:
            op("g", lambda: g.iota(x(out), pat, base, cm), out, [], held)

    ndma, sent, went, stored = [0], [0], [], []

    def dma(q, out, a, after=()):
        ins = [a] if isinstance(a, tuple) else []
        outs = [out] if isinstance(out, tuple) else []
        s = "dm%d" % ndma[0]
        ndma[0] += 1
        ways = [(z, 0.06, lambda z=z: Q[z].dma_start(_bytes(T, out) if outs else out, _bytes(T, a) if ins else a)) for z in q]
        return put(ways, ins, outs, COPY, after, (s, 16))

    def send(stage):
        mine = [w for w in _routes(T, topo, rank, stage) if w[0] == core]
        sent[0] += sum(_bits(w[3]) for w in mine)
        went.append(put([("g", SEND, lambda: _calls(g, T, topo, rank, stage, mine))], [_places(rank, stage, w[2])[1] for w in mine], [],
                        after=went + stored, sem=("loc", None)))
        return went[-1]

    def arrive(stage, k):
        come = [(r, w) for r in range(N) for w in _routes(T, topo, r, stage) if core in w[1]]
        way = put([("r" + stage, 0.001, None)], [], [], WAY[stage[0]] - SEND, [k], ("loc", 0))
        return put([("r" + stage, 0.001, None)], [], [_places(r, stage, w[2])[4] for r, w in come], 0.0, [way, went[-1]],
                   ("arr_" + stage, sum(_bits(w[3]) for r, w in come)))

    def ind(w, o):
        return ("ind", w, o)

    def c(name, j):
        return V(name, j, j + 1)

    def h32(name, h):
        return V(name, 32 * h, 32 * h + 32)

    dma("y", V("itt", 0, 4 * I), T.it[:, :])
    dma("y", V("xt", 0, 1024), T.x[:, :])
    fill(V("itt", 4 * I, 512), 0.0)
    iota(c("pi", 0), [[0, 1]], 0, 1, False)
    iota(V("ej", 0, 128), [[1, 128]], 0, 0)
    iota(c("ej", 128), [[0, 1]], 0, 1)
    iota(V("kx", 0, 32), [[0, 2], [-1, 4], [0, 4]], K - 1, 0)
    iota(V("kx", 32, 64), [[0, 2], [-1, 4], [0, 4]], K - 5, 0)
    iota(V("kx", 64, 96), [[0, 2], [1, 16]], 0, 0)
    fill(V("et", 0, 2048), 0.0)
    quant(V("iq", 0, 128), V("isc", 0, 128), V("itt", 0, 512))
    items = arrive("i", send("i"))

    iota(V("jr", 0, 1024), [[1, 1024]], 0, 0)
    ts(V("ident", 0, 128), V("ej", 0, 128), c("ej", 128), A.is_equal)
    for b in range(4):
        cp(V("et", 512 * b + b, 512 * b + 512, 4), V("ident", 0, 128), 0)
    quant(V("eq", 0, 512), V("es", 0, 512), V("et", 0, 2048))
    for h in range(2):
        for a in range(4):
            cp(V("xp", 512 * h + 128 * a, 512 * h + 128 * a + 128), V("xt", 256 * a + 128 * h, 256 * a + 128 * h + 128), h)
    quant(V("xq", 0, 256), V("xs", 0, 256), V("xt", 0, 1024))
    quant(V("pq", 0, 256), V("ps", 0, 256), V("xp", 0, 1024))
    for b in range(4):
        mm(V("p_d", 512 * b, 512 * b + 256), "eq", "es", 128 * b, "xq", "xs", 0, 256)
        act(V("dx", b, 1024, 4), V("p_d", 512 * b, 512 * b + 256), ACT.Identity, scale=0.5)
    stored.append(dma("y", V("wt", 0, 512), T.w[:, :], [items]))
    LANE, QUAD, L16, L4, L8, ID, ID4, IDU, TMP, THR, TWO, LESS = 0, 1, 2, 3, 4, 6, 8, 10, 12, 20, 22, 24
    ts(c("pi", 1), c("pi", 0), 31, A.bitwise_and)
    ts(c("pi", 2), c("pi", 0), 5, A.logical_shift_right)
    ts(c("pi", 3), c("pi", 0), 15, A.bitwise_and)
    ts(c("pi", 4), c("pi", 0), 3, A.bitwise_and)
    ts(c("pi", 6), c("pi", 0), 8.0, A.add)
    ts(c("pi", 5), c("pi", 6), 15, A.bitwise_and)
    cp(V("pc", 0, 5), V("pi", 1, 6), 0)
    fill(V("neg", 0, NI), -BIG)
    fill(V("zero", 0, 32), 0.0)
    fill(V("pm", 0, 2 * NI + 2, NI + 1), -BIG)
    slot0 = K * (rank % 4) + (8 if rank < 4 else 0)
    lin(c("pc", TMP), c("pc", QUAD), 6.0)
    lin(c("pc", ID), c("pc", QUAD), 64.0, c("pc", LANE))
    lin(c("pc", TMP + 1), c("pc", QUAD), 48.0, c("pc", LANE))
    lin(c("pc", TMP + 2), c("pc", QUAD), 48.0)
    lin(c("pc", TMP + 3), c("pc", LANE), -1.0, 32.0)
    lin(c("pc", ID + 1), c("pc", ID), None, 32.0)
    lin(V("pc", ID4, ID4 + 2), V("pc", ID, ID + 2), 4.0)
    lin(V("pc", IDU, IDU + 2), V("pc", ID, ID + 2), U)
    lin(V("pc", TWO, TWO + 2), V("ej", 0, 2), NI * GID * U)
    fill(c("pc", LESS), -NIL)
    fill(c("pc", THR), -HELD / 10)
    fill(V("cg", 0, 128), 1.0)
    ts(V("tmp", 0, 33), V("ej", 0, 33), c("pc", TMP + 3), A.is_equal, -STEP, A.mult)
    lin(V("cg", 64, 97), V("tmp", 0, 33), None, 1.0)
    lin(V("cf", 0, 128), V("cg", 0, 128), -1.0)
    fill(V("m2", 0, 2 * W2), 0.0)
    fill(V("m2", NI + 1, 2 * W2, W2), -NIL)
    ts(V("tmp", 33, 57), V("ej", 0, 24), c("pc", TMP), A.subtract)
    ts(V("tmp", 57, 81), V("tmp", 33, 57), -1.5, A.is_gt, H, A.mult)
    ts(V("tmp", 81, 105), V("tmp", 33, 57), 4.5, A.is_gt, -H, A.mult)
    tt(V("tmp", 57, 81), V("tmp", 57, 81), V("tmp", 81, 105), A.add)
    ts(V("tmp", 81, 105), V("tmp", 33, 57), 5.0, A.is_equal, -6 * H, A.mult)
    tt(V("a1", 64, 88, -1), V("tmp", 57, 81), V("tmp", 81, 105), A.add)
    fill(V("a1", 89, 96), 0.0)
    ts(c("tmp", 105), c("pc", QUAD), 0.5, A.is_lt, H, A.mult)
    lin(c("a1", 88), c("tmp", 105), None, -OUT * H)
    ts(V("tmp", 81, 105), V("tmp", 33, 57), 5.0, A.is_equal, (OUT - 5.5) * H, A.mult)
    tt(V("tmp", 57, 81), V("tmp", 57, 81), V("tmp", 81, 105), A.add)
    ts(V("tmp", 81, 105), V("tmp", 33, 57), -1.0, A.is_equal, -(OUT + 1) * H, A.mult)
    tt(V("a1", 96, 120, -1), V("tmp", 57, 81), V("tmp", 81, 105), A.add)
    cp(V("a1", 184, 240), V("a1", 64, 120))
    for h in range(2):
        fill(V("eb", 120 * h, 120 * h + 96), BIG)
    fill(V("xx", 8, 154), 0.0)
    fill(V("xx", 9, 13, 2), BIG)
    fill(V("rnd", 0, 4), 0.0)
    fill(c("rnd", 4), WHOLE * GID * U)
    fill(c("rnd", 5), -WHOLE * GID * U)
    lin(c("pc", TMP + 4), c("pc", TMP + 2), None, -0.5)
    ts(V("irow", 0, NC), V("ej", 0, NC), c("pc", TMP + 4), A.add, -FALL, A.mult)
    lin(c("pc", TMP + 5), c("pc", TMP + 2), RISE, OUT * H - RISE)
    fill(V("rb", 73, 81), -BIG)
    fill(V("rt", 73, 81), -BIG)
    fill(V("a2a", 64, 96), 0.0)
    fill(V("a2a", 96 - K - slot0, 95 - slot0), -H)
    fill(c("a2a", 95 - slot0), -26.5 * H)
    back = slot0 + K < 32
    fill(c("a2a", 95 - K - slot0) if back else c("tmp", 119), 32 * H)
    fill(c("kl", 0), 0.0)
    ts(V("kl", 1, 65), V("kx", 0, 64), 0.0, A.max, 1.0, A.add)
    tt(V("kw", 0, 64), V("kl", 1, 65), V("kl", 0, 64), A.subtract)
    lin(V("a2a", 0, 63, -1), V("kw", 1, 64), H)
    fill(c("a2a", 63), (K + 31.5 - (32 if back else 0)) * H)
    lin(V("a2b", 0, 64, -1), V("kw", 0, 64), H)
    lin(V("kw", 0, 64), V("kx", 0, 64), -H, (5.5 - OUT) * H)
    fill(V("kp", 0, 32), BIG)
    lin(V("kp", slot0, slot0 + K), V("ej", 0, K), H, (0.5 - OUT) * H)
    fill(V("ct", 32, 512), 0.0)
    fill(V("od", 0, 118), 0.0)
    for h in range(2):
        fill(V("od", 59 * h, 59 * h + I), 0.5 ** (M + 1))
    fill(V("od", 24, 118, 59), -0.5 ** M)
    fill(V("od", 25, 118, 59), -BIG)
    fill(V("a3", 24, 118, 59), -1.0)
    fill(V("a3", 25, 118, 59), -2.0 ** M)
    lin(c("od", 26), c("pc", TMP + 1), H, (LIFT - 8 - 1 / TAG) * H)
    lin(c("od", 85), c("pc", TMP + 1), H, (LIFT + 24 - 1 / TAG) * H)
    fill(V("best", 32, 40), -1.0)
    fill(V("mi", 0, 34, 33), 1.0)
    ts(V("mk", 1, 33), V("kx", 64, 96), c("pc", L8), A.is_equal, DIM, A.max)
    ts(V("tmp", 0, 32), V("kx", 64, 96), c("pc", L8), A.not_equal, 1 / DIM, A.mult)
    ts(V("mi", 1, 33), V("tmp", 0, 32), 1.0, A.max)
    tt(V("a3", 27, 59), V("mk", 1, 33), V("mi", 0, 32), A.mult)
    tt(V("a3", 86, 118), V("mk", 1, 33, -1), V("mi", 2, 34, -1), A.mult)
    fill(V("keep", 0, 48), 1.0)
    fill(V("keep", 0, 48, 16), 0.0)
    for t in range(R):
        fill(V("land%d" % t, 64, 256), -BIG)
    ts(V("dm", 0, 16), V("ej", 0, 16), c("pc", L16), A.is_equal, 4.0, A.mult)
    ts(V("dm", 16, 32), V("ej", 0, 16), c("pc", L16), A.is_equal)
    fill(c("price", 0), 0.0)
    fill(V("cpw", 0, NI), 0.0)
    fill(V("eh", 0, 2 * NC), 0.0)
    own_h, own_p = rank % 2, 32 * (rank // 2) + (0 if rank % 2 else 8)

    P1 = NI + 1
    for t in range(R):
        last = t == R - 1
        mid = 0 < t < R - 1
        wn = NI + NC * t
        n, lo = (NI, 0) if t == 0 else (128, wn - 128)
        new = NI if t == 0 else NC
        lst = V("lst", 12 * (t - 1), 12 * t)
        vv = [V("p_s", 512 * h, 512 * h + NI) if t == 0 else V("v%d" % h, 0, NI) for h in range(2)]
        for h in range(2):
            if t == 0:
                mm(vv[h], "pq", "ps", 128 * h, "win", "wins", lo, n)
            else:
                for j0, j1 in CUTS[h]:
                    cp(V("v%d" % h, 16 * j0, 16 * j1), ind(V("vw%d" % h, 0, wn), V("lst", 12 * (t - 1) + j0, 12 * (t - 1) + j1)))
        for b in range(4):
            mm(V("p_d", 512 * b, 512 * b + n), "eq", "es", 128 * b, "win", "wins", lo, n)
            lin(V("dw", 4 * (wn - new) + b, 4 * wn, 4), V("p_d", 512 * b + n - new, 512 * b + n), 0.5)
        if t > 0:
            cp(V("srow", 0, NI), ind(V("jr", 0, wn), lst))
        if mid:
            cp(V("srow", NI, 2 * NI), ind(V("cpw", 0, wn), lst))
        for h in range(2):
            scan(V("pm", P1 * h + 1, P1 * h + P1), vv[h], V("neg", 0, NI), -BIG, A.max, A.max)
        for h in range(2):
            scan(V("m2", W2 * h, W2 * h + NI), vv[h], V("pm", P1 * h, P1 * h + NI), -BIG, A.max, A.min)
        m1 = [c("pm", P1 * h + NI) for h in range(2)]
        for h in range(2):
            if t > 0:
                act(c("m2", W2 * h + NI), m1[h], ACT.Relu, scale=4.0, bias=c("pc", THR))
            act(V("junk", NI * h, NI * h + NI), V("pm", P1 * h + 1, P1 * h + P1), ACT.Sign, c("goal", h), scale=-1.0, bias=m1[h])
            lin(c("gid", h), c("goal", h), GID * U, c("pc", IDU + h))
        scan(V("bb0", 32, 99, -1), V("m2", NI - 1, NI + 66), V("cf", 29, 96), m1[0], A.subtract, A.mult)
        scan(V("bb1", 0, 67, -1), V("m2", W2 + NI - 1, W2 + NI + 66), V("cf", 61, 128), m1[1], A.subtract, A.mult)
        turn(V("tr", 32, 96), V("bb0", 32, 96))
        for j in range(2):
            turn(h32("tr", 3 * j), h32("bb1", j))
        for h in range(2):
            lin(V("eb", 120 * h + 96, 120 * h + 120), V("cg", 0, I), c("bb%d" % h, 63))
            ts(V("a1", 120 * h, 120 * h + 64), V("tr", 64 * h, 64 * h + 64), c("bb%d" % h, 63), A.is_ge, H, A.mult)
        for h in range(2):
            scan(V("w1", 120 * h, 120 * h + 120, -1), V("a1", 120 * h, 120 * h + 120), V("eb", 120 * h, 120 * h + 120), c("gid", h), A.add, A.min)
        turn(V("w1t", 32, 96), V("w1", 0, 64))
        for j in range(2):
            turn(h32("w1t", 3 * j), V("w1", 120 + 32 * j, 152 + 32 * j))
        red(c("xx", 0), V("w1t", 0, 64), A.max)
        red(c("xx", 1), V("w1t", 64, 128), A.min, apply_absolute_value=True)
        for d in range(2):
            cp(V("xx", 2, 4, 1, 64 * d, 64 * d + 64), V("xx", 0, 2, 1, 64 - 64 * d, 128 - 64 * d))
        for d in range(4):
            cp(V("xx", 4, 8, 1, 32 * d, 32 * d + 32), V("xx", 0, 4, 1, 32 * (d ^ 1), 32 * (d ^ 1) + 32))
        scan(V("sb", 0, 77, -1), V("xx", 0, 154, 2), V("cg", 19, 96), 0.0, A.max, A.mult)
        scan(V("sg", 0, 6), V("xx", 1, 13, 2), V("rnd", 0, 6), (NI * GID - B - 1) * U, A.min, A.add)
        bid, gid, goal = c("sb", 24), c("sg", 3), c("sg", 5)
        a2, a0 = ("a2b", 64) if t else ("a2a", 96)
        turn(V("br", 0, 32), V("sb", 0, 32))
        lin(c("sm", 2), goal, FALL / (GID * U))
        lin(c(a2, a0 + 24), goal, -RISE / (GID * U), c("pc", TMP + 5))
        lin(c("sm", 0), goal, -1.0, gid)
        if t > 0:
            nl = 2 if mid else 1
            ts(V("g16", 0, nl), V("pc", TWO, TWO + nl), goal, A.add, 1.0 / (GID * U), A.mult)
            tt(V("lk", 0, 16 * nl), ind(V("srow", 0, NI * nl), V("g16", 0, nl)), V("dm", 0, 16 * nl), A.mult)
            red(c("sm", 4), V("lk", 0, 16), A.add)
        else:
            lin(c("sm", 4), goal, 4.0 / (GID * U))
            lin(V("nb", 0, 56), V("sb", 0, 56), -1.0)
        if mid:
            cp(c("lk", 32), bid)
            red(c("sm", 6), V("lk", 16, 33), A.add)
        ts(V(a2, a0, a0 + 24), V("br", 0, 24), bid, A.is_ge, -H, A.mult)
        ts(V(a2, a0 + 25, a0 + 73), V("irow", 0, NC), c("sm", 2), A.add, RISE, A.min)
        lin(c("sm", 1), c("sm", 0), H / (TAG * U), (LIFT + wn + K * rank + K - OUT + B * rank / TAG) * H)
        scan(V("rb", 0, 73), V(a2, a0, a0 + 73), V("sb", 0, 73), (K + 0.5 - OUT) * H, A.add, A.min)
        scan(V("rt", 0, 73), V(a2, a0, a0 + 73), V("neg", 0, 73), c("sm", 1), A.add, A.max)
        r2 = c("rb", 23)
        ld, l0 = "land%d" % t, 8 * (N - 1 - rank)
        if t == 0:
            scan(V("pk", 0, 56), V(a2, 64, 120, -1), V("nb", 0, 56), 32 * H, A.add, A.max)
            turn(V("pkt", 0, 32), V("pk", 24, 56))
            red(c(ld, l0 + 4), V("pkt", 0, 32), A.min, negate=True)
        if mid:
            ts(V("pk", 24, 56), V("kp", 0, 32), r2, A.is_equal, c("sm", 6), A.mult)
            turn(V("pkt", 0, 32), V("pk", 24, 56))
            red(c(ld, l0 + 4), V("pkt", 0, 32), A.add)
        turn(V("kt", 0, 64), V("rb", 17, 81))
        turn(V("kt", 64, 128), V("rt", 17, 81))
        for j in range(4):
            red(c(ld, l0 + j), V("kt", 32 * j, 32 * j + I), A.max)
        bids = send("a%d" % t)
        scan(V("rx", 0, a0 + 24), V(a2, 0, a0 + 24, -1), V("neg", 0, a0 + 24), c("sm", 0), A.add, A.max)
        ts(V("w2", 0, 64), V("kw", 0, 64), r2, A.is_equal, c("sm", 4), A.mult)
        turn(V("w2t", 0, 64), V("rx", a0 - 40, a0 + 24))
        turn(V("w2t", 64, 128), V("w2", 0, 64))
        for j in range(2):
            red(c("u2", j), V("w2t", 32 * j, 32 * j + I), A.min, apply_absolute_value=True)
        for j in range(2, 4):
            red(c("u2", j), V("w2t", 32 * j, 32 * j + I), A.add)
        ts(V("l2", 0, 2), V("u2", 0, 2), 4.0 / U, A.mult, c("pc", L4), A.add)
        ts(V("l2", 2, 4), V("u2", 2, 4), c("pc", L4), A.add)
        cp(V("xg", 0, 32), ind(V("dx", 0, 1024), V("l2", 0, 2)))
        tt(V("ct", 0, 32), ind(V("dw", 0, 4 * wn), V("l2", 2, 4)), V("xg", 0, 32), A.add)
        quant(V("cq%d" % t, 0, 128), V("cs%d" % t, 0, 128), V("ct", 0, 512))
        arrive("b%d" % t, send("b%d" % t))
        arrive("a%d" % t, bids)
        if t == 0:
            quant(V("wq", 0, 128), V("ws", 0, 128), V("wt", 0, 512))
            mm(V("p_y", 0, n), "wq", "ws", 0, "win", "wins", lo, n)
            cp(V("yw", 0, NI), V("p_y", 0, NI))
            for h in range(2):
                cp(V("vw%d" % h, 0, NI), vv[h])
        if not last:
            cp(V("idg", 0, 32), ind(V("jr", 0, 1024), V("l2", 0, 2)))
            for h in range(2):
                ts(V("eh", NC * h + K * rank, NC * h + K * rank + K), V("idg", 0, 4 * K, 4), c("pc", ID4 + h), A.is_equal, HELD, A.mult)
        w2 = wn + NC
        if not last:
            for h in range(2):
                mm(V("p_s", 512 * h, 512 * h + 128), "pq", "ps", 128 * h, "win", "wins", w2 - 128, 128)
            for h in range(2):
                act(V("cpc", 2 + 4 * h, 6 + 4 * h), V(ld, 36 - 32 * h, 68 - 32 * h, 8), ACT.Relu, c("cpc", h), bias=c("pc", LESS))
                lin(h32("cpb", h), V("zero", 0, 32), None, c("cpc", h))
            turn(V("cpt", 0, 64), V("cpb", 0, 64))
            for h in range(2):
                tt(V("cpx", NC * h, NC * h + NC), V("cpt", 8, 8 + NC), V("eh", NC * h, NC * h + NC), A.subtract)
                tt(V("vw%d" % h, wn, w2), V("p_s", 512 * h + 128 - NC, 512 * h + 128), V("cpx", NC * h, NC * h + NC), A.subtract)
            if t == 0:
                cp(V("cpw", wn, w2), V("cpt", 8, 8 + NC))
        mm(V("p_y", 0, 128), "wq", "ws", 0, "win", "wins", w2 - 128, 128)
        cp(V("yw", wn, w2), V("p_y", 128 - NC, 128))
        bs = [c("best", 63 - 40 * h) for h in range(2)]
        c0 = 118 * t
        for h in range(2):
            scan(V("best", 40 - 40 * h, 72 - 40 * h, -1), V(ld, h, 256, 8), V("cg", 56 + 8 * h, 88 + 8 * h), -1.0, A.max, A.mult)
        turn(V("t3", 0, 64), V("best", 0, 64))
        for h in range(2):
            act(V("mw", 8 * h, 8 * h + 8), V(ld, h, 64, 8), ACT.Sign, scale=-1.0, bias=bs[h])
        for h in range(2):
            ts(V("a3", 59 * h, 59 * h + I), V("t3", 40 - 40 * h, 64 - 40 * h), bs[h], A.is_lt, 0.5, A.max)
            scan(V("a3", 59 * h + 26, 59 * h + 27 + 7 * GAP, -GAP), V("mw", 8 * h, 8 * h + 8), V(ld, 2 + h, 64, 8), 0.0, A.mult, A.max)
        for h in range(2):
            scan(V("cn", c0 + 59 * h, c0 + 59 * h + 59, 1 - 2 * h), V("a3", 59 * h, 59 * h + 59), V("od", 59 * h, 59 * h + 59), 1.0, A.mult, A.max)
        if not last:
            cp(V("od", 26, 86, 59), V("cn", c0 + 26, c0 + 92, 65))
        turn(V("mbt", 0, 64), V("cn", c0 + 27, c0 + 91))
        for a in range(4):
            scan(V("x3", 48 * a, 48 * a + 48, 1, 0, 32), V("keep", 0, 48, 1, 32 * a, 32 * a + 32),
                 V("mbt", 8, 56, 1, 32 * a, 32 * a + 32), 0.0, A.mult, A.max)
        for d in range(4):
            ts(V("lst", 12 * t, 12 * t + 12, 1, 32 * d, 32 * d + 32), V("x3", 15, 192, 16, 0, 32), 1.0 / H, A.mult, -LIFT, A.add)
        h, k = own_h, 8 * t
        tag, sold = c("cn", c0 + 26 + 65 * h), c("cn", c0 + 25 + 67 * h)
        act(c("bk", k), bs[h], ACT.Relu, bias=c("pc", LESS))
        ts(c("bk", k + 1), sold, 0.75, A.is_gt, c("bk", k), A.mult)
        lin(c("price", t + 1), c("bk", k + 1), None, c("price", t))
        stored.append(dma("y", T.pr[t, :], V("price", t + 1, t + 2, 1, own_p, own_p + I)))
        lin(c("bk", k + 2), tag, 1.0 / H, WHOLE)
        lin(c("bk", k + 3), c("bk", k + 2), -TAG, TAG * WHOLE)
        lin(c("bk", k + 4), tag, TAG / H, c("bk", k + 3))
        stored.append(dma("y", T.ho[t, :], V("bk", k + 4, k + 5, 1, own_p, own_p + I)))

    l0 = 12 * (R - 1)
    c0 = I * rank // 32 * 2
    c1 = -(-(I * rank + I) // 16)
    at, n = I * rank - 16 * c0, 16 * (c1 - c0)
    sub = V("lst", l0 + c0, l0 + c1)
    for h in range(2):
        cp(V("yf", 96 * h, 96 * h + 96), ind(V("yw", 0, NW), V("lst", l0 + 6 * h, l0 + 6 * h + 6)))
    k = dma("y", T.y[:, :], V("yf", 0, NI))
    calls[k]["late"] += 0.3
    cp(V("osc2", 0, n), ind(V("wins", 0, NW), sub))
    op("v", lambda: g.vector.tensor_copy(T.oq[:, 0:n].bitcast(dt.uint32), T.win[:, 0:NW].bitcast(dt.uint32).indirect(x(sub))),
       V("oq", 0, n), [V("win", 0, NW), sub], time(ind(None, sub)))
    dma("ys", T.oc[:, :], V("oq", at, at + I))
    for k in range(4):
        dma("ys", T.osc[4 * k:4 * k + 4, :], V("osc2", at, at + I, 1, 32 * k, 32 * k + 4))

    plan = _place(calls)
    count = {"sv": 0, "ss": 0, "st": 0, "sg": 0, "loc": sent[0]}
    waited = {q: {} for q in Q}
    token = {}

    def need(q, s, n):
        if waited[q].get(s, 0) < n:
            Q[q].wait_ge(T.sem[s], n)
            waited[q][s] = n

    for k in sorted(range(len(calls)), key=lambda j: (plan[j][0], j)):
        q, held, call = plan[k][1]
        sem = calls[k]["sem"]
        if call is None:
            token[k] = sem
            count[sem[0]] = max(count.get(sem[0], 0), sem[1])
            continue
        want = {}
        for d in calls[k]["deps"]:
            if d in token:
                want[token[d][0]] = max(want.get(token[d][0], 0), token[d][1])
        for s in want:
            need(q, s, want[s])
        if sem is None:
            count["s" + q] += 1
            call().then_inc(T.sem["s" + q], 1)
            token[k] = ("s" + q, count["s" + q])
        elif sem[1] is None:
            call()
        else:
            call().then_inc(T.sem[sem[0]], sem[1])
            token[k] = sem
            count[sem[0]] = sem[1]
    for s in count:
        if max(waited[q].get(s, 0) for q in Q) < count[s]:
            need("g", s, count[s])
